import numpy as np
import ml_dtypes


def mxq(x, axis, fmt="e4m3"):
    dtype, down = {"e4m3": (ml_dtypes.float8_e4m3fn, 7), "e5m2": (ml_dtypes.float8_e5m2, 14)}[fmt]
    v = np.moveaxis(np.asarray(x, np.float32).astype(ml_dtypes.bfloat16).astype(np.float64), axis, -1)
    blocks = v.reshape(v.shape[:-1] + (-1, 32))
    amax = np.abs(blocks).max(-1, keepdims=True)
    byte = np.maximum(np.where(amax > 0, np.frexp(amax)[1] - 1 + 127, 0) - down, 1)
    scale = np.exp2(byte - 127.0)
    codes = (blocks / scale).astype(np.float32).astype(dtype).astype(np.float64)
    return np.moveaxis((codes * scale).reshape(v.shape), -1, axis)


WIDE = False


def mx_kscale(k):
    if not WIDE:
        return np.ones(k)
    levels = np.array([10, -10, 5, -5, 0])
    if k % 512:
        return np.exp2(np.random.permutation(np.resize(levels, k // 32))).repeat(32)
    a = np.empty((k // 512, 16))
    for p in range(k // 512):
        a[p, :8] = np.random.permutation(np.resize(levels, 8))
        for g in range(8):
            far = levels[np.abs(levels - a[p, g]) >= 10]
            a[p, g + 8] = far[np.random.randint(len(far))]
    return np.exp2(a.ravel()).repeat(32)


def f64(x):
    return np.asarray(x).astype(np.float64)


def striped(idx):
    return np.tile(np.asarray(idx).reshape(-1, 16).T, (8, 1)).astype(np.uint16)


def unstriped(offs):
    return offs[:16].T.reshape(-1).astype(np.int64)


E2M1 = np.array([0.0, 0.5, 1.0, 1.5, 2.0, 3.0, 4.0, 6.0, -0.0, -0.5, -1.0, -1.5, -2.0, -3.0, -4.0, -6.0])


def pack_weight(w, fmt):
    k, n = w.shape
    w = f64(np.asarray(w, np.float32).astype(ml_dtypes.bfloat16)).reshape(k // 32, 32, n)
    amax = np.abs(w).max(1)
    if fmt == "e4m3":
        byte = np.frexp(amax)[1] - 1 + 127 - 7
    else:
        mant, ex = np.frexp(amax / 6.0)
        byte = np.where(mant > 0.5, ex, ex - 1) + 127
    byte = np.clip(np.where(amax > 0, byte, 1), 1, 254)
    scaled = (w * np.exp2(127.0 - byte)[:, None, :]).reshape(k, n).astype(np.float32)
    by_word = np.ascontiguousarray(scaled.reshape(k // 512, 128, 4, n).transpose(0, 1, 3, 2))
    if fmt == "e4m3":
        words = by_word.astype(ml_dtypes.float8_e4m3fn).view(np.uint8)
    else:
        c = by_word.astype(ml_dtypes.float4_e2m1fn).view(np.uint8) & 0xF
        words = (c[..., 0::2] | (c[..., 1::2] << 4)).reshape(k // 512, 128, 2 * n)
    return np.ascontiguousarray(words), np.ascontiguousarray(byte.astype(np.uint8).reshape(k // 512, 16, n))


def unpack_weight(words, scales, fmt):
    g, _, n = scales.shape
    words = np.ascontiguousarray(words).reshape(g, 128, n, -1)
    if fmt == "e4m3":
        vals = words.view(ml_dtypes.float8_e4m3fn).astype(np.float64)
    else:
        nib = np.empty((g, 128, n, 4), np.uint8)
        nib[..., 0::2] = words & 0xF
        nib[..., 1::2] = words >> 4
        vals = E2M1[nib]
    vals = vals * np.repeat(np.exp2(scales.astype(np.float64) - 127.0), 8, axis=1)[..., None]
    return vals.transpose(0, 1, 3, 2).reshape(g * 512, n)


B, N, T, D, DV, NQ = 2, 512, 2048, 512, 128, 256
PAGE = 128
DRAFT = 128


def setup_inputs():
    n = np.random.standard_normal
    pages = np.random.permutation(T // PAGE)[:B * N // PAGE]
    idx = (pages[:, None] * PAGE + np.arange(PAGE)[None, :]).reshape(-1)
    s = mx_kscale(D)[:, None]
    u = np.ones(T)
    u[idx] = mx_kscale(B * N)
    r = np.random.uniform(0.5, 2.0, T)
    qp = [pack_weight(x, "e4m3") for x in n((B, D, NQ)) * s * (0.80 / np.sqrt(D))]
    k = n((D, T)) / s
    v = n((DV, T)) / (u * r)
    kp = pack_weight(k, "e4m3")
    when = np.zeros(T)
    when[idx] = np.concatenate([np.concatenate([np.arange(N - DRAFT), N - DRAFT + np.random.randint(0, 16, DRAFT)]) for b in range(B)])
    return {
        "q_words": np.stack([x[0] for x in qp]),
        "q_scales": np.stack([x[1] for x in qp]),
        "k_words": kp[0],
        "k_scales": kp[1],
        "vT": v.astype(np.float32),
        "vs": np.tile(u * r, (128, 1)).astype(np.float32),
        "pos": np.tile(when, (128, 1)).astype(np.float32),
        "qpos": np.random.randint(N - DRAFT, N - DRAFT + 16, (B, NQ, 1)).astype(np.float32),
        "sink": (2.0 + 3.0 * n((B, NQ, 1))).astype(np.float32),
        "offs": striped(idx),
    }


def reference(q_words, q_scales, k_words, k_scales, vT, vs, pos, qpos, sink, offs):
    idx = unstriped(offs)
    k = unpack_weight(k_words, k_scales, "e4m3")
    v = f64(vT)
    pick = lambda x: x[:, idx].reshape(x.shape[0], B, N).transpose(1, 0, 2)
    q = np.stack([unpack_weight(q_words[b], q_scales[b], "e4m3") for b in range(B)])
    score = q.transpose(0, 2, 1) @ pick(k)
    score = np.where(pick(f64(pos))[:, :1, :] <= f64(qpos), score, -30000.0)
    m = np.maximum(score.max(-1, keepdims=True), f64(sink))
    p = np.exp(score - m)
    total = p.sum(-1, keepdims=True) + np.exp(f64(sink) - m)
    w = p * pick(f64(vs))[:, :1, :]
    y = mxq(w, 2, "e4m3") @ mxq(pick(v).transpose(0, 2, 1), 1, "e4m3")
    y = y / total
    return y

@@ -1,0 +1,177 @@
+from contextlib import ExitStack
+
+import concourse.mybir as mybir
+
+B, N, T, D, DV, NQ = 2, 512, 2048, 512, 128, 256
+P = 128
+QT = NQ // P
+FLOPS = 2 * B * NQ * N * (D + DV)
+
+F32 = mybir.dt.float32
+BF16 = mybir.dt.bfloat16
+I32 = mybir.dt.int32
+U32 = mybir.dt.uint32
+U16 = mybir.dt.uint16
+U8 = mybir.dt.uint8
+FP8X4 = mybir.dt.float8_e4m3fn_x4
+ALU = mybir.AluOpType
+ACT = mybir.ActivationFunctionType
+
+BIG = 2.0 ** 64
+MASKED = 30000.0
+
+
+def turn_and_quantise(nc, psum, work, ident, rows, codes, scales):
+    words = rows[:].bitcast(F32)
+    turned = psum.tile([P, 2, P], F32, name="turned", tag="turned", bufs=3)
+    for u in range(2):
+        nc.tensor.transpose(turned[:, u, :], words[:, u : N // 2 : 2], ident[:])
+    woven = work.tile([P, P, 2], F32, name="woven", tag="woven", bufs=6, align_bytes=64)
+    nc.scalar.copy(woven[:], turned[:].rearrange("p u c -> p c u"))
+    nc.vector.quantize_mx(
+        out=codes[:].bitcast(FP8X4),
+        scales=scales[:],
+        in_=woven[:].rearrange("p c u -> p (c u)").bitcast(BF16),
+    )
+
+
+def tile_attend_soft_draft_sink_pgb2q256n512t2048_kernel(
+    tc, q_words, q_scales, k_words, k_scales, vT, vs, pos, qpos, sink, offs, out
+):
+    nc = tc.nc
+    with ExitStack() as ctx:
+        held = ctx.enter_context(tc.tile_pool(name="held", bufs=1))
+        work = ctx.enter_context(tc.tile_pool(name="work", bufs=1))
+        psum = ctx.enter_context(tc.psum_pool(name="psum", bufs=1))
+
+        offsets = held.tile([P, B * N // 16], U16, name="offsets")
+        ks_pool = held.tile([P, T], U8, name="ks_pool", align_bytes=64)
+        v_pool = held.tile([P, T], BF16, name="v_pool")
+        rows = held.tile([P, P], F32, name="rows")
+        ident = held.tile([P, P], F32, name="ident")
+
+        nc.vector.memset(ks_pool[:].bitcast(I32), 0)
+        nc.vector.memset(rows[:], 0.0)
+
+        large = ctx.enter_context(tc.tile_pool(name="large", bufs=1))
+        zeros = large.tile([P, 4 * T + B * NQ + B * NQ // 4], F32, name="zeros", offset=0)
+        nc.gpsimd.memset(zeros[:, :P], 0.0)
+        nc.gpsimd.affine_select(
+            out=ident[:], in_=zeros[:, :P], compare_op=ALU.not_equal, fill=1.0, base=0, pattern=[[-1, P]], channel_multiplier=1
+        )
+        pos_pool = large.tile([P, T], F32, name="pos_pool", offset=0)
+        kw_pool = large.tile([P, T], I32, name="kw_pool", offset=4 * T)
+        v_raw = large.tile([P, T], F32, name="v_raw", offset=8 * T)
+        vs_pool = large.tile([P, T], F32, name="vs_pool", offset=12 * T)
+        qw = large.tile([P, B, NQ], I32, name="qw", offset=16 * T, align_bytes=64)
+        qs = large.tile([P, B * NQ], U8, name="qs", offset=16 * T + 4 * B * NQ, align_bytes=64)
+        nc.vector.memset(qs[:].bitcast(I32), 0)
+
+        nc.sync.dma_start(offsets[:], offs)
+        for g in range(4):
+            nc.sync.dma_start(ks_pool[32 * g : 32 * g + 4, :].bitcast(I32), k_scales[0, 4 * g : 4 * g + 4, :].bitcast(I32))
+        nc.sync.dma_start(pos_pool[:], pos)
+        nc.sync.dma_start(rows[0:4, :], qpos.rearrange("b (h p) o -> (b h) (p o)", p=P))
+        nc.sync.dma_start(rows[4:8, :], sink.rearrange("b (h p) o -> (b h) (p o)", p=P))
+        nc.sync.dma_start(kw_pool[:], k_words[0].rearrange("p t r -> p (t r)").bitcast(I32))
+        nc.sync.dma_start(qw[:], q_words.rearrange("b o p q r -> p (b o) (q r)").bitcast(I32))
+        for g in range(4):
+            nc.sync.dma_start(
+                qs[32 * g : 32 * g + 4, :].bitcast(I32).rearrange("f (b q) -> f b q", b=B),
+                q_scales[:, 0, 4 * g : 4 * g + 4, :].rearrange("b f q -> f b q").bitcast(I32),
+            )
+        nc.sync.dma_start(v_raw[:], vT)
+        nc.sync.dma_start(vs_pool[:], vs)
+
+        lists = [offsets[:, b * N // 16 : (b + 1) * N // 16] for b in range(B)]
+
+        nq = held.tile([P, B * QT], F32, name="nq")
+        cols = psum.tile([P, P], F32, name="y", tag="y", bufs=1)
+        nc.tensor.transpose(cols[:], rows[:], ident[:])
+        nc.scalar.activation(nq[:], cols[:, 0:4], ACT.Copy, scale=-BIG)
+        xs = [held.tile([P, N + 1], F32, name=f"x{j}") for j in range(B * QT)]
+        for j in range(B * QT):
+            nc.scalar.activation(xs[j][:, N : N + 1], cols[:, 4 + j : 5 + j], ACT.Copy, scale=-1.0)
+
+        ks = [held.tile([P, N], U8, name=f"ks{b}", align_bytes=64) for b in range(B)]
+        kw = [held.tile([P, N], U32, name=f"kw{b}", align_bytes=64) for b in range(B)]
+        pg = [held.tile([P, N], F32, name=f"pg{b}") for b in range(B)]
+        sg = [held.tile([P, N], F32, name=f"sg{b}") for b in range(B)]
+        vg = [held.tile([P, N], BF16, name=f"vg{b}") for b in range(B)]
+        for b in range(B):
+            nc.vector.tensor_copy(ks[b][:], ks_pool[:].indirect(lists[b]))
+        for b in range(B):
+            nc.vector.tensor_copy(pg[b][:], pos_pool[:].indirect(lists[b]))
+        for b in range(B):
+            nc.vector.tensor_copy(kw[b][:], kw_pool[:].bitcast(U32).indirect(lists[b]))
+
+        scores = []
+        for j in range(B * QT):
+            b = j // QT
+            s = psum.tile([P, N], F32, name=f"s{j}")
+            nc.tensor.matmul_mx(
+                out=s[:],
+                lhsT=qw[:, b, (j % QT) * P : (j % QT + 1) * P].bitcast(FP8X4),
+                lhsT_scale=qs[:, j * P : (j + 1) * P],
+                rhs=kw[b][:].bitcast(FP8X4),
+                rhs_scale=ks[b][:],
+                start=True,
+                stop=True,
+            )
+            scores.append(s)
+
+        pens = []
+        for j in range(B * QT):
+            pen = work.tile([P, N], F32, name=f"pen{j}")
+            nc.scalar.activation(pen[:], pg[j // QT][:], ACT.Relu, bias=nq[:, j : j + 1], scale=BIG)
+            pens.append(pen)
+        for h in range(2):
+            nc.scalar.activation(v_pool[:, h * T // 2 : (h + 1) * T // 2], v_raw[:, h * T // 2 : (h + 1) * T // 2], ACT.Copy)
+        for b in range(B):
+            nc.scalar.activation(vg[b][:], v_pool[:].indirect(lists[b]), ACT.Copy)
+
+        nm = held.tile([P, B * QT], F32, name="nm")
+        total = held.tile([P, B * QT], F32, name="total")
+        inv = held.tile([P, B * QT], F32, name="inv")
+        ps = []
+        for b in range(B):
+            tiles = range(b * QT, (b + 1) * QT)
+            raws = {}
+            for j in tiles:
+                raws[j] = work.tile([P, N], F32, name=f"raw{j}")
+                nc.vector.tensor_tensor(raws[j][:], pens[j][:], scores[j][:], ALU.subtract)
+            for j in tiles:
+                nc.vector.tensor_scalar(
+                    xs[j][:, :N], raws[j][:], MASKED, xs[j][:, N : N + 1], ALU.min, ALU.min, accum_out=nm[:, j : j + 1]
+                )
+                p = work.tile([P, N + 1], F32, name=f"p{j}")
+                nc.scalar.activation(p[:], xs[j][:], ACT.Exp, bias=nm[:, j : j + 1], scale=-1.0, accum_out=total[:, j : j + 1])
+                ps.append(p)
+        for b in range(B):
+            nc.vector.tensor_copy(sg[b][:], vs_pool[:].indirect(lists[b]))
+
+        vq = [held.tile([P, DV], U32, name=f"vq{b}", align_bytes=64) for b in range(B)]
+        vsc = [held.tile([P, DV], U8, name=f"vsc{b}", align_bytes=64) for b in range(B)]
+        for j in range(B * QT):
+            b = j // QT
+            if j % QT == 0:
+                turn_and_quantise(nc, psum, work, ident, vg[b], vq[b], vsc[b])
+                nc.vector.reciprocal(inv[:, j : j + QT], total[:, j : j + QT])
+            w = work.tile([P, N], BF16, name=f"w{j}")
+            nc.vector.tensor_tensor(w[:], ps[j][:, :N], sg[b][:], ALU.mult)
+            wq = work.tile([P, P], U32, name=f"wq{j}", align_bytes=64)
+            wsc = work.tile([P, P], U8, name=f"wsc{j}", align_bytes=64)
+            turn_and_quantise(nc, psum, work, ident, w, wq, wsc)
+            y = psum.tile([P, DV], F32, name="y", tag="y", bufs=1)
+            nc.tensor.matmul_mx(
+                out=y[:],
+                lhsT=wq[:].bitcast(FP8X4),
+                lhsT_scale=wsc[:],
+                rhs=vq[b][:].bitcast(FP8X4),
+                rhs_scale=vsc[b][:],
+                start=True,
+                stop=True,
+            )
+            res = work.tile([P, DV], F32, name=f"res{j}")
+            nc.scalar.activation(res[:], y[:], ACT.Copy, scale=inv[:, j : j + 1])
+            nc.sync.dma_start(out[b, (j % QT) * P : (j % QT + 1) * P, :], res[:])

@@ -21,18 +21,16 @@ BIG = 2.0 ** 64
 MASKED = 30000.0
 
 
-def turn_and_quantise(nc, psum, work, ident, rows, codes, scales):
-    words = rows[:].bitcast(F32)
-    turned = psum.tile([P, 2, P], F32, name="turned", tag="turned", bufs=3)
+def turn(nc, psum, ident, rows, woven):
+    words = rows.bitcast(F32)
+    turned = psum.tile([P, 2, P], F32, name="turned", tag="turned", bufs=4)
     for u in range(2):
         nc.tensor.transpose(turned[:, u, :], words[:, u : N // 2 : 2], ident[:])
-    woven = work.tile([P, P, 2], F32, name="woven", tag="woven", bufs=6, align_bytes=64)
-    nc.scalar.copy(woven[:], turned[:].rearrange("p u c -> p c u"))
-    nc.vector.quantize_mx(
-        out=codes[:].bitcast(FP8X4),
-        scales=scales[:],
-        in_=woven[:].rearrange("p c u -> p (c u)").bitcast(BF16),
-    )
+    nc.scalar.copy(woven.rearrange("p (c u) -> p c u", u=2), turned[:].rearrange("p u c -> p c u"))
+
+
+def quantise(nc, woven, codes, scales):
+    nc.vector.quantize_mx(out=codes.bitcast(FP8X4), scales=scales, in_=woven.bitcast(BF16))
 
 
 def tile_attend_soft_draft_sink_pgb2q256n512t2048_kernel(
@@ -84,12 +82,14 @@ def tile_attend_soft_draft_sink_pgb2q256n512t2048_kernel(
         nc.sync.dma_start(vs_pool[:], vs)
 
         lists = [offsets[:, b * N // 16 : (b + 1) * N // 16] for b in range(B)]
+        late = ctx.enter_context(tc.tile_pool(name="late", bufs=1))
+        XB = 4 * N + 64
 
         nq = held.tile([P, B * QT], F32, name="nq")
-        cols = psum.tile([P, P], F32, name="y", tag="y", bufs=1)
+        cols = psum.tile([P, P], F32, name="cols", tag="turned", bufs=4)
         nc.tensor.transpose(cols[:], rows[:], ident[:])
         nc.scalar.activation(nq[:], cols[:, 0:4], ACT.Copy, scale=-BIG)
-        xs = [held.tile([P, N + 1], F32, name=f"x{j}") for j in range(B * QT)]
+        xs = [late.tile([P, N + 1], F32, name=f"x{j}", offset=j * XB) for j in range(B * QT)]
         for j in range(B * QT):
             nc.scalar.activation(xs[j][:, N : N + 1], cols[:, 4 + j : 5 + j], ACT.Copy, scale=-1.0)
 
@@ -97,7 +97,6 @@ def tile_attend_soft_draft_sink_pgb2q256n512t2048_kernel(
         kw = [held.tile([P, N], U32, name=f"kw{b}", align_bytes=64) for b in range(B)]
         pg = [held.tile([P, N], F32, name=f"pg{b}") for b in range(B)]
         sg = [held.tile([P, N], F32, name=f"sg{b}") for b in range(B)]
-        vg = [held.tile([P, N], BF16, name=f"vg{b}") for b in range(B)]
         for b in range(B):
             nc.vector.tensor_copy(ks[b][:], ks_pool[:].indirect(lists[b]))
         for b in range(B):
@@ -108,7 +107,7 @@ def tile_attend_soft_draft_sink_pgb2q256n512t2048_kernel(
         scores = []
         for j in range(B * QT):
             b = j // QT
-            s = psum.tile([P, N], F32, name=f"s{j}")
+            s = psum.tile([P, N], F32, name="s", tag="sums", bufs=4)
             nc.tensor.matmul_mx(
                 out=s[:],
                 lhsT=qw[:, b, (j % QT) * P : (j % QT + 1) * P].bitcast(FP8X4),
@@ -127,48 +126,71 @@ def tile_attend_soft_draft_sink_pgb2q256n512t2048_kernel(
             pens.append(pen)
         for h in range(2):
             nc.scalar.activation(v_pool[:, h * T // 2 : (h + 1) * T // 2], v_raw[:, h * T // 2 : (h + 1) * T // 2], ACT.Copy)
-        for b in range(B):
-            nc.scalar.activation(vg[b][:], v_pool[:].indirect(lists[b]), ACT.Copy)
 
         nm = held.tile([P, B * QT], F32, name="nm")
         total = held.tile([P, B * QT], F32, name="total")
         inv = held.tile([P, B * QT], F32, name="inv")
         ps = []
+        vg = []
         for b in range(B):
             tiles = range(b * QT, (b + 1) * QT)
             raws = {}
             for j in tiles:
-                raws[j] = work.tile([P, N], F32, name=f"raw{j}")
+                if b == 0:
+                    raws[j] = work.tile([P, N], F32, name=f"raw{j}")
+                else:
+                    raws[j] = large.tile([P, N], F32, name=f"raw{j}", offset=12 * T + 4 * N * (j % QT))
                 nc.vector.tensor_tensor(raws[j][:], pens[j][:], scores[j][:], ALU.subtract)
             for j in tiles:
                 nc.vector.tensor_scalar(
                     xs[j][:, :N], raws[j][:], MASKED, xs[j][:, N : N + 1], ALU.min, ALU.min, accum_out=nm[:, j : j + 1]
                 )
-                p = work.tile([P, N + 1], F32, name=f"p{j}")
+                if b == 0:
+                    p = large.tile([P, N + 1], F32, name=f"p{j}", offset=8 * T + XB * j)
+                else:
+                    p = work.tile([P, N + 1], F32, name=f"p{j}")
                 nc.scalar.activation(p[:], xs[j][:], ACT.Exp, bias=nm[:, j : j + 1], scale=-1.0, accum_out=total[:, j : j + 1])
                 ps.append(p)
-        for b in range(B):
-            nc.vector.tensor_copy(sg[b][:], vs_pool[:].indirect(lists[b]))
+            if b == 0:
+                for c in range(B):
+                    nc.vector.tensor_copy(sg[c][:], vs_pool[:].indirect(lists[c]))
+                for c in range(B):
+                    vg.append(late.tile([P, N], BF16, name=f"vg{c}", offset=XB + 2 * N * c))
+                    nc.scalar.activation(vg[c][:], v_pool[:].indirect(lists[c]), ACT.Copy)
 
-        vq = [held.tile([P, DV], U32, name=f"vq{b}", align_bytes=64) for b in range(B)]
-        vsc = [held.tile([P, DV], U8, name=f"vsc{b}", align_bytes=64) for b in range(B)]
+        H = N // 2
+        ws = [work.tile([P, N], BF16, name=f"w{j}") for j in range(B * QT)]
+        v_woven = work.tile([P, B * H], F32, name="v_woven", align_bytes=64)
+        w_woven = [work.tile([P, QT * H], F32, name=f"w_woven{b}", align_bytes=64) for b in range(B)]
+        for j in range(QT):
+            nc.gpsimd.tensor_tensor(ws[j][:], ps[j][:, :N], sg[0][:], ALU.mult)
+        for j in range(QT):
+            turn(nc, psum, ident, vg[j][:], v_woven[:, j * H : (j + 1) * H])
+            turn(nc, psum, ident, ws[j][:], w_woven[0][:, j * H : (j + 1) * H])
+        base = 12 * T + 4 * N
+        vq = large.tile([P, B * DV], U32, name="vq", offset=base, align_bytes=64)
+        vsc = large.tile([P, B * DV], U8, name="vsc", offset=base + 1024, align_bytes=64)
+        wq = [large.tile([P, NQ], U32, name="wq0", offset=base - 4 * N, align_bytes=64), work.tile([P, NQ], U32, name="wq1", align_bytes=64)]
+        wsc = [large.tile([P, NQ], U8, name="wsc0", offset=base + 1024 + 256, align_bytes=64), work.tile([P, NQ], U8, name="wsc1", align_bytes=64)]
+        nc.vector.reciprocal(inv[:, 0:QT], total[:, 0:QT])
+        quantise(nc, v_woven[:], vq[:], vsc[:])
+        quantise(nc, w_woven[0][:], wq[0][:], wsc[0][:])
+        for j in range(QT, B * QT):
+            nc.vector.tensor_tensor(ws[j][:], ps[j][:, :N], sg[1][:], ALU.mult)
+        nc.vector.reciprocal(inv[:, QT:], total[:, QT:])
+        for h in range(QT):
+            turn(nc, psum, ident, ws[QT + h][:], w_woven[1][:, h * H : (h + 1) * H])
         for j in range(B * QT):
-            b = j // QT
-            if j % QT == 0:
-                turn_and_quantise(nc, psum, work, ident, vg[b], vq[b], vsc[b])
-                nc.vector.reciprocal(inv[:, j : j + QT], total[:, j : j + QT])
-            w = work.tile([P, N], BF16, name=f"w{j}")
-            nc.vector.tensor_tensor(w[:], ps[j][:, :N], sg[b][:], ALU.mult)
-            wq = work.tile([P, P], U32, name=f"wq{j}", align_bytes=64)
-            wsc = work.tile([P, P], U8, name=f"wsc{j}", align_bytes=64)
-            turn_and_quantise(nc, psum, work, ident, w, wq, wsc)
-            y = psum.tile([P, DV], F32, name="y", tag="y", bufs=1)
+            b, h = divmod(j, QT)
+            if b == 1:
+                quantise(nc, w_woven[1][:, h * H : (h + 1) * H], wq[1][:, h * P : (h + 1) * P], wsc[1][:, h * P : (h + 1) * P])
+            y = psum.tile([P, DV], F32, name="y", tag="sums", bufs=4)
             nc.tensor.matmul_mx(
                 out=y[:],
-                lhsT=wq[:].bitcast(FP8X4),
-                lhsT_scale=wsc[:],
-                rhs=vq[b][:].bitcast(FP8X4),
-                rhs_scale=vsc[b][:],
+                lhsT=wq[b][:, h * P : (h + 1) * P].bitcast(FP8X4),
+                lhsT_scale=wsc[b][:, h * P : (h + 1) * P],
+                rhs=vq[:, b * DV : (b + 1) * DV].bitcast(FP8X4),
+                rhs_scale=vsc[:, b * DV : (b + 1) * DV],
                 start=True,
                 stop=True,
             )

@@ -40,37 +40,46 @@ def tile_attend_soft_draft_sink_pgb2q256n512t2048_kernel(
     with ExitStack() as ctx:
         held = ctx.enter_context(tc.tile_pool(name="held", bufs=1))
         work = ctx.enter_context(tc.tile_pool(name="work", bufs=1))
+        shared = ctx.enter_context(tc.tile_pool(name="shared", bufs=1))
         psum = ctx.enter_context(tc.psum_pool(name="psum", bufs=1))
+        sums = ctx.enter_context(tc.psum_pool(name="sums", bufs=1))
+
+        KB = 1024
+        BANK = 2 * KB
+        AT_KEYS, AT_POS, AT_VS, AT_SG, AT_X1, AT_P3 = 0, 11 * KB, 19 * KB, 27 * KB, 32 * KB, 35 * KB
+        AT_P0, AT_P1 = 38 * KB, 41 * KB
+        H = N // 2
 
         offsets = held.tile([P, B * N // 16], U16, name="offsets")
         ks_pool = held.tile([P, T], U8, name="ks_pool", align_bytes=64)
+        v_raw = [held.tile([P, T // 2], F32, name=f"v_raw{h}") for h in range(2)]
         v_pool = held.tile([P, T], BF16, name="v_pool")
-        rows = held.tile([P, P], F32, name="rows")
         ident = held.tile([P, P], F32, name="ident")
+        rows = shared.tile([P, P], F32, name="rows", offset=AT_VS)
+        pos_pool = shared.tile([P, T], F32, name="pos_pool", offset=AT_POS)
 
         nc.vector.memset(ks_pool[:].bitcast(I32), 0)
-        nc.vector.memset(rows[:], 0.0)
+        nc.vector.memset(rows[: P - 8, :], 0.0)
+        nc.vector.memset(pos_pool[: P - 1, :], 0.0)
 
-        large = ctx.enter_context(tc.tile_pool(name="large", bufs=1))
-        zeros = large.tile([P, 4 * T + B * NQ + B * NQ // 4], F32, name="zeros", offset=0)
+        zeros = shared.tile([P, T + B * NQ + B * NQ // 4], F32, name="zeros", offset=AT_KEYS)
         nc.gpsimd.memset(zeros[:, :P], 0.0)
         nc.gpsimd.affine_select(
             out=ident[:], in_=zeros[:, :P], compare_op=ALU.not_equal, fill=1.0, base=0, pattern=[[-1, P]], channel_multiplier=1
         )
-        pos_pool = large.tile([P, T], F32, name="pos_pool", offset=0)
-        kw_pool = large.tile([P, T], I32, name="kw_pool", offset=4 * T)
-        v_raw = large.tile([P, T], F32, name="v_raw", offset=8 * T)
-        vs_pool = large.tile([P, T], F32, name="vs_pool", offset=12 * T)
-        qw = large.tile([P, B, NQ], I32, name="qw", offset=16 * T, align_bytes=64)
-        qs = large.tile([P, B * NQ], U8, name="qs", offset=16 * T + 4 * B * NQ, align_bytes=64)
-        nc.vector.memset(qs[:].bitcast(I32), 0)
+        kw_pool = shared.tile([P, T], I32, name="kw_pool", offset=AT_KEYS)
+        qw = shared.tile([P, B, NQ], I32, name="qw", offset=AT_KEYS + 4 * T, align_bytes=64)
+        qs = shared.tile([P, B * NQ], U8, name="qs", offset=AT_KEYS + 4 * T + 4 * B * NQ, align_bytes=64)
+        nc.gpsimd.memset(qs[:].bitcast(I32), 0)
 
         nc.sync.dma_start(offsets[:], offs)
+        nc.sync.dma_start(pos_pool[P - 1 :, :], pos[P - 1 :, :])
+        nc.sync.dma_start(rows[P - 8 : P - 4, :], qpos.rearrange("b (h p) o -> (b h) (p o)", p=P))
+        nc.sync.dma_start(rows[P - 4 :, :], sink.rearrange("b (h p) o -> (b h) (p o)", p=P))
+        for h in range(2):
+            nc.sync.dma_start(v_raw[h][:], vT[:, h * T // 2 : (h + 1) * T // 2])
         for g in range(4):
             nc.sync.dma_start(ks_pool[32 * g : 32 * g + 4, :].bitcast(I32), k_scales[0, 4 * g : 4 * g + 4, :].bitcast(I32))
-        nc.sync.dma_start(pos_pool[:], pos)
-        nc.sync.dma_start(rows[0:4, :], qpos.rearrange("b (h p) o -> (b h) (p o)", p=P))
-        nc.sync.dma_start(rows[4:8, :], sink.rearrange("b (h p) o -> (b h) (p o)", p=P))
         nc.sync.dma_start(kw_pool[:], k_words[0].rearrange("p t r -> p (t r)").bitcast(I32))
         nc.sync.dma_start(qw[:], q_words.rearrange("b o p q r -> p (b o) (q r)").bitcast(I32))
         for g in range(4):
@@ -78,113 +87,144 @@ def tile_attend_soft_draft_sink_pgb2q256n512t2048_kernel(
                 qs[32 * g : 32 * g + 4, :].bitcast(I32).rearrange("f (b q) -> f b q", b=B),
                 q_scales[:, 0, 4 * g : 4 * g + 4, :].rearrange("b f q -> f b q").bitcast(I32),
             )
-        nc.sync.dma_start(v_raw[:], vT)
-        nc.sync.dma_start(vs_pool[:], vs)
 
         lists = [offsets[:, b * N // 16 : (b + 1) * N // 16] for b in range(B)]
-        late = ctx.enter_context(tc.tile_pool(name="late", bufs=1))
-        XB = 4 * N + 64
 
-        nq = held.tile([P, B * QT], F32, name="nq")
         cols = psum.tile([P, P], F32, name="cols", tag="turned", bufs=4)
         nc.tensor.transpose(cols[:], rows[:], ident[:])
-        nc.scalar.activation(nq[:], cols[:, 0:4], ACT.Copy, scale=-BIG)
-        xs = [late.tile([P, N + 1], F32, name=f"x{j}", offset=j * XB) for j in range(B * QT)]
+        vs_pool = shared.tile([P, T], F32, name="vs_pool", offset=AT_VS)
+        nc.sync.dma_start(vs_pool[:], vs)
+        nq = work.tile([P, B * QT], F32, name="nq")
+        nc.scalar.activation(nq[:], cols[:, P - 8 : P - 4], ACT.Copy, scale=-BIG)
+        xs = []
         for j in range(B * QT):
-            nc.scalar.activation(xs[j][:, N : N + 1], cols[:, 4 + j : 5 + j], ACT.Copy, scale=-1.0)
+            if j == 1:
+                xs.append(shared.tile([P, N + 1], F32, name="x1", offset=AT_X1))
+            else:
+                xs.append(work.tile([P, N + 1], F32, name=f"x{j}"))
+            nc.scalar.activation(xs[j][:, N : N + 1], cols[:, P - 4 + j : P - 3 + j], ACT.Copy, scale=-1.0)
+        q_row = psum.tile([P, NQ], F32, name="q_row", tag="turned", bufs=4)
+        for h in range(QT):
+            nc.tensor.transpose(q_row[:, h * P : (h + 1) * P], nq[:, QT + h : QT + h + 1].to_broadcast([P, P]), ident[:])
 
-        ks = [held.tile([P, N], U8, name=f"ks{b}", align_bytes=64) for b in range(B)]
-        kw = [held.tile([P, N], U32, name=f"kw{b}", align_bytes=64) for b in range(B)]
-        pg = [held.tile([P, N], F32, name=f"pg{b}") for b in range(B)]
-        sg = [held.tile([P, N], F32, name=f"sg{b}") for b in range(B)]
+        for h in range(2):
+            nc.scalar.activation(v_pool[:, h * T // 2 : (h + 1) * T // 2], v_raw[h][:], ACT.Copy)
+
+        upright = sums.tile([P, 16, P], F32, name="upright", offset=0)
+        columns = []
         for b in range(B):
-            nc.vector.tensor_copy(ks[b][:], ks_pool[:].indirect(lists[b]))
-        for b in range(B):
-            nc.vector.tensor_copy(pg[b][:], pos_pool[:].indirect(lists[b]))
+            pg = work.tile([P, N], F32, name=f"pg{b}")
+            nc.vector.tensor_copy(pg[:], pos_pool[:].indirect(lists[b]))
+            for c in range(4):
+                nc.tensor.transpose(upright[:, 4 * b + c, :], pg[:, c * P : (c + 1) * P], ident[:])
+            columns.append(work.tile([P, 4], F32, name=f"columns{b}"))
+            nc.scalar.activation(columns[b][:], upright[:, 4 * b : 4 * b + 4, P - 1], ACT.Copy, scale=BIG)
+        places = psum.tile([P, N], F32, name="places", tag="turned", bufs=4)
+        for c in range(4):
+            nc.tensor.transpose(places[:, c * P : (c + 1) * P], columns[0][:, c : c + 1].to_broadcast([P, P]), ident[:])
+        pens = [work.tile([P, N], F32, name=f"pen{h}") for h in range(QT)]
+        for h in range(QT):
+            nc.scalar.activation(pens[h][:], places[:], ACT.Relu, bias=nq[:, h : h + 1], scale=1.0)
+        pen_t = work.tile([P, 4, NQ], F32, name="pen_t")
+        for c in range(4):
+            nc.scalar.activation(pen_t[:, c, :], q_row[:], ACT.Relu, bias=columns[1][:, c : c + 1], scale=1.0)
+
+        ks = shared.tile([P, B * N], U8, name="ks", align_bytes=64, offset=AT_POS)
+        kw = [shared.tile([P, N], U32, name=f"kw{b}", align_bytes=64, offset=AT_POS + 2 * KB * (b + 1)) for b in range(B)]
+        nc.vector.tensor_copy(ks[:], ks_pool[:].indirect(offsets[:]))
         for b in range(B):
             nc.vector.tensor_copy(kw[b][:], kw_pool[:].bitcast(U32).indirect(lists[b]))
-
-        scores = []
-        for j in range(B * QT):
-            b = j // QT
-            s = psum.tile([P, N], F32, name="s", tag="sums", bufs=4)
+        scores = [sums.tile([P, N], F32, name=f"s{h}", offset=BANK * h) for h in range(QT)]
+        for h in range(QT):
             nc.tensor.matmul_mx(
-                out=s[:],
-                lhsT=qw[:, b, (j % QT) * P : (j % QT + 1) * P].bitcast(FP8X4),
-                lhsT_scale=qs[:, j * P : (j + 1) * P],
-                rhs=kw[b][:].bitcast(FP8X4),
-                rhs_scale=ks[b][:],
+                out=scores[h][:],
+                lhsT=qw[:, 0, h * P : (h + 1) * P].bitcast(FP8X4),
+                lhsT_scale=qs[:, h * P : (h + 1) * P],
+                rhs=kw[0][:].bitcast(FP8X4),
+                rhs_scale=ks[:, :N],
                 start=True,
                 stop=True,
             )
-            scores.append(s)
+        neg_t = work.tile([P, 4, NQ], F32, name="neg_t")
+        for g in range(2):
+            scores_t = sums.tile([P, 2, NQ], F32, name=f"st{g}", offset=BANK * (QT + g))
+            for e in range(2):
+                c = 2 * g + e
+                nc.tensor.matmul_mx(
+                    out=scores_t[:, e, :],
+                    lhsT=kw[1][:, c * P : (c + 1) * P].bitcast(FP8X4),
+                    lhsT_scale=ks[:, N + c * P : N + (c + 1) * P],
+                    rhs=qw[:, 1, :].bitcast(FP8X4),
+                    rhs_scale=qs[:, NQ:],
+                    start=True,
+                    stop=True,
+                )
+            nc.scalar.activation(neg_t[:, 2 * g : 2 * g + 2, :], scores_t[:], ACT.Copy, scale=-1.0)
 
-        pens = []
-        for j in range(B * QT):
-            pen = work.tile([P, N], F32, name=f"pen{j}")
-            nc.scalar.activation(pen[:], pg[j // QT][:], ACT.Relu, bias=nq[:, j : j + 1], scale=BIG)
-            pens.append(pen)
-        for h in range(2):
-            nc.scalar.activation(v_pool[:, h * T // 2 : (h + 1) * T // 2], v_raw[:, h * T // 2 : (h + 1) * T // 2], ACT.Copy)
+        vg = [work.tile([P, N], BF16, name="vg0")]
+        nc.scalar.activation(vg[0][:], v_pool[:].indirect(lists[0]), ACT.Copy)
 
-        nm = held.tile([P, B * QT], F32, name="nm")
         total = held.tile([P, B * QT], F32, name="total")
         inv = held.tile([P, B * QT], F32, name="inv")
         ps = []
-        vg = []
-        for b in range(B):
-            tiles = range(b * QT, (b + 1) * QT)
-            raws = {}
-            for j in tiles:
-                if b == 0:
-                    raws[j] = work.tile([P, N], F32, name=f"raw{j}")
-                else:
-                    raws[j] = large.tile([P, N], F32, name=f"raw{j}", offset=12 * T + 4 * N * (j % QT))
-                nc.vector.tensor_tensor(raws[j][:], pens[j][:], scores[j][:], ALU.subtract)
-            for j in tiles:
-                nc.vector.tensor_scalar(
-                    xs[j][:, :N], raws[j][:], MASKED, xs[j][:, N : N + 1], ALU.min, ALU.min, accum_out=nm[:, j : j + 1]
-                )
-                if b == 0:
-                    p = large.tile([P, N + 1], F32, name=f"p{j}", offset=8 * T + XB * j)
-                else:
-                    p = work.tile([P, N + 1], F32, name=f"p{j}")
-                nc.scalar.activation(p[:], xs[j][:], ACT.Exp, bias=nm[:, j : j + 1], scale=-1.0, accum_out=total[:, j : j + 1])
-                ps.append(p)
-            if b == 0:
-                for c in range(B):
-                    nc.vector.tensor_copy(sg[c][:], vs_pool[:].indirect(lists[c]))
-                for c in range(B):
-                    vg.append(late.tile([P, N], BF16, name=f"vg{c}", offset=XB + 2 * N * c))
-                    nc.scalar.activation(vg[c][:], v_pool[:].indirect(lists[c]), ACT.Copy)
 
-        H = N // 2
+        def softmax(b, raws, nm, places_of_p):
+            for h in range(QT):
+                j = b * QT + h
+                nc.vector.tensor_scalar(
+                    xs[j][:, :N], raws[h][:], MASKED, xs[j][:, N : N + 1], ALU.min, ALU.min, accum_out=nm[:, h : h + 1]
+                )
+                ps.append(shared.tile([P, N + 1], F32, name=f"p{j}", offset=places_of_p[h]))
+                nc.scalar.activation(ps[j][:], xs[j][:], ACT.Exp, bias=nm[:, h : h + 1], scale=-1.0, accum_out=total[:, j : j + 1])
+
+        raws = [shared.tile([P, N], F32, name=f"raw{h}", offset=AT_SG + 2 * KB * (1 - h)) for h in range(QT)]
+        for h in range(QT):
+            nc.vector.tensor_tensor(raws[h][:], pens[h][:], scores[h][:], ALU.subtract)
+        softmax(0, raws, work.tile([P, QT], F32, name="nm0"), [AT_P0, AT_P1])
+        raws = [sums.tile([P, N], F32, name=f"raw{QT + h}", offset=BANK * h) for h in range(QT)]
+        for h in range(QT):
+            for c in range(4):
+                for k, part in enumerate((neg_t, pen_t)):
+                    nc.tensor.matmul(
+                        raws[h][:, c * P : (c + 1) * P],
+                        lhsT=part[:, c, h * P : (h + 1) * P],
+                        rhs=ident[:],
+                        start=(k == 0),
+                        stop=(k == 1),
+                        is_transpose=True,
+                    )
+        sg = [shared.tile([P, N], F32, name=f"sg{b}", offset=AT_SG + 2 * KB * b) for b in range(B)]
+        for b in range(B):
+            nc.vector.tensor_copy(sg[b][:], vs_pool[:].indirect(lists[b]))
+        vg.append(shared.tile([P, N], BF16, name="vg1", offset=AT_X1))
+        nc.scalar.activation(vg[1][:], v_pool[:].indirect(lists[1]), ACT.Copy)
+
         ws = [work.tile([P, N], BF16, name=f"w{j}") for j in range(B * QT)]
         v_woven = work.tile([P, B * H], F32, name="v_woven", align_bytes=64)
         w_woven = [work.tile([P, QT * H], F32, name=f"w_woven{b}", align_bytes=64) for b in range(B)]
-        for j in range(QT):
-            nc.gpsimd.tensor_tensor(ws[j][:], ps[j][:, :N], sg[0][:], ALU.mult)
-        for j in range(QT):
-            turn(nc, psum, ident, vg[j][:], v_woven[:, j * H : (j + 1) * H])
-            turn(nc, psum, ident, ws[j][:], w_woven[0][:, j * H : (j + 1) * H])
-        base = 12 * T + 4 * N
-        vq = large.tile([P, B * DV], U32, name="vq", offset=base, align_bytes=64)
-        vsc = large.tile([P, B * DV], U8, name="vsc", offset=base + 1024, align_bytes=64)
-        wq = [large.tile([P, NQ], U32, name="wq0", offset=base - 4 * N, align_bytes=64), work.tile([P, NQ], U32, name="wq1", align_bytes=64)]
-        wsc = [large.tile([P, NQ], U8, name="wsc0", offset=base + 1024 + 256, align_bytes=64), work.tile([P, NQ], U8, name="wsc1", align_bytes=64)]
-        nc.vector.reciprocal(inv[:, 0:QT], total[:, 0:QT])
-        quantise(nc, v_woven[:], vq[:], vsc[:])
-        quantise(nc, w_woven[0][:], wq[0][:], wsc[0][:])
+        for b in range(B):
+            turn(nc, psum, ident, vg[b][:], v_woven[:, b * H : (b + 1) * H])
+
+        softmax(1, raws, shared.tile([P, QT], F32, name="nm1", offset=AT_VS), [AT_X1, AT_P3])
+        for h in range(QT):
+            nc.gpsimd.tensor_tensor(ws[h][:], ps[h][:, :N], sg[0][:], ALU.mult)
+            turn(nc, psum, ident, ws[h][:], w_woven[0][:, h * H : (h + 1) * H])
         for j in range(QT, B * QT):
             nc.vector.tensor_tensor(ws[j][:], ps[j][:, :N], sg[1][:], ALU.mult)
-        nc.vector.reciprocal(inv[:, QT:], total[:, QT:])
+        vq = shared.tile([P, B * DV], U32, name="vq", offset=AT_P3, align_bytes=64)
+        vsc = work.tile([P, B * DV], U8, name="vsc", align_bytes=64)
+        quantise(nc, v_woven[:], vq[:], vsc[:])
+        wq = [shared.tile([P, NQ], U32, name="wq0", offset=AT_P3 + KB, align_bytes=64), work.tile([P, NQ], U32, name="wq1", align_bytes=64)]
+        wsc = [work.tile([P, NQ], U8, name=f"wsc{b}", align_bytes=64) for b in range(B)]
+        quantise(nc, w_woven[0][:], wq[0][:], wsc[0][:])
+        nc.vector.reciprocal(inv[:], total[:])
         for h in range(QT):
             turn(nc, psum, ident, ws[QT + h][:], w_woven[1][:, h * H : (h + 1) * H])
         for j in range(B * QT):
             b, h = divmod(j, QT)
             if b == 1:
                 quantise(nc, w_woven[1][:, h * H : (h + 1) * H], wq[1][:, h * P : (h + 1) * P], wsc[1][:, h * P : (h + 1) * P])
-            y = psum.tile([P, DV], F32, name="y", tag="sums", bufs=4)
+            y = sums.tile([P, DV], F32, name=f"y{j}", offset=BANK * ((j + QT) % 4))
             nc.tensor.matmul_mx(
                 out=y[:],
                 lhsT=wq[b][:, h * P : (h + 1) * P].bitcast(FP8X4),
@@ -195,5 +235,8 @@ def tile_attend_soft_draft_sink_pgb2q256n512t2048_kernel(
                 stop=True,
             )
             res = work.tile([P, DV], F32, name=f"res{j}")
-            nc.scalar.activation(res[:], y[:], ACT.Copy, scale=inv[:, j : j + 1])
-            nc.sync.dma_start(out[b, (j % QT) * P : (j % QT + 1) * P, :], res[:])
+            if j == B * QT - 1:
+                nc.vector.tensor_scalar(res[:], y[:], inv[:, j : j + 1], None, ALU.mult)
+            else:
+                nc.scalar.activation(res[:], y[:], ACT.Copy, scale=inv[:, j : j + 1])
+            nc.sync.dma_start(out[b, h * P : (h + 1) * P, :], res[:])

@@ -46,13 +46,13 @@ def tile_attend_soft_draft_sink_pgb2q256n512t2048_kernel(
 
         KB = 1024
         BANK = 2 * KB
-        AT_KEYS, AT_POS, AT_VS, AT_SG, AT_X1, AT_P3 = 0, 11 * KB, 19 * KB, 27 * KB, 32 * KB, 35 * KB
-        AT_P0, AT_P1 = 38 * KB, 41 * KB
+        AT_KEYS, AT_POS, AT_VS, AT_SG, AT_X1, AT_X3 = 0, 11 * KB, 19 * KB, 27 * KB, 32 * KB, 35 * KB
+        AT_PG, AT_V = 38 * KB, 44 * KB
         H = N // 2
 
         offsets = held.tile([P, B * N // 16], U16, name="offsets")
         ks_pool = held.tile([P, T], U8, name="ks_pool", align_bytes=64)
-        v_raw = [held.tile([P, T // 2], F32, name=f"v_raw{h}") for h in range(2)]
+        v_raw = [shared.tile([P, T // 2], F32, name=f"v_raw{h}", offset=AT_V + 4 * KB * h) for h in range(2)]
         v_pool = held.tile([P, T], BF16, name="v_pool")
         ident = held.tile([P, P], F32, name="ident")
         rows = shared.tile([P, P], F32, name="rows", offset=AT_VS)
@@ -98,8 +98,8 @@ def tile_attend_soft_draft_sink_pgb2q256n512t2048_kernel(
         nc.scalar.activation(nq[:], cols[:, P - 8 : P - 4], ACT.Copy, scale=-BIG)
         xs = []
         for j in range(B * QT):
-            if j == 1:
-                xs.append(shared.tile([P, N + 1], F32, name="x1", offset=AT_X1))
+            if j % QT == 1:
+                xs.append(shared.tile([P, N + 1], F32, name=f"x{j}", offset=(AT_X1, AT_X3)[j // QT]))
             else:
                 xs.append(work.tile([P, N + 1], F32, name=f"x{j}"))
             nc.scalar.activation(xs[j][:, N : N + 1], cols[:, P - 4 + j : P - 3 + j], ACT.Copy, scale=-1.0)
@@ -113,11 +113,11 @@ def tile_attend_soft_draft_sink_pgb2q256n512t2048_kernel(
         upright = sums.tile([P, 16, P], F32, name="upright", offset=0)
         columns = []
         for b in range(B):
-            pg = work.tile([P, N], F32, name=f"pg{b}")
+            pg = shared.tile([P, N], F32, name=f"pg{b}", offset=AT_PG + 3 * KB * b)
             nc.vector.tensor_copy(pg[:], pos_pool[:].indirect(lists[b]))
             for c in range(4):
                 nc.tensor.transpose(upright[:, 4 * b + c, :], pg[:, c * P : (c + 1) * P], ident[:])
-            columns.append(work.tile([P, 4], F32, name=f"columns{b}"))
+            columns.append(shared.tile([P, 4], F32, name=f"columns{b}", offset=AT_V + 4 * KB + 32 * b))
             nc.scalar.activation(columns[b][:], upright[:, 4 * b : 4 * b + 4, P - 1], ACT.Copy, scale=BIG)
         places = psum.tile([P, N], F32, name="places", tag="turned", bufs=4)
         for c in range(4):
@@ -129,8 +129,11 @@ def tile_attend_soft_draft_sink_pgb2q256n512t2048_kernel(
         for c in range(4):
             nc.scalar.activation(pen_t[:, c, :], q_row[:], ACT.Relu, bias=columns[1][:, c : c + 1], scale=1.0)
 
-        ks = shared.tile([P, B * N], U8, name="ks", align_bytes=64, offset=AT_POS)
-        kw = [shared.tile([P, N], U32, name=f"kw{b}", align_bytes=64, offset=AT_POS + 2 * KB * (b + 1)) for b in range(B)]
+        vg = [work.tile([P, N], BF16, name="vg0")]
+        nc.scalar.activation(vg[0][:], v_pool[:].indirect(lists[0]), ACT.Copy)
+
+        ks = shared.tile([P, B * N], U8, name="ks", align_bytes=64, offset=AT_PG)
+        kw = [shared.tile([P, N], U32, name=f"kw{b}", align_bytes=64, offset=AT_PG + 2 * KB * (b + 1)) for b in range(B)]
         nc.vector.tensor_copy(ks[:], ks_pool[:].indirect(offsets[:]))
         for b in range(B):
             nc.vector.tensor_copy(kw[b][:], kw_pool[:].bitcast(U32).indirect(lists[b]))
@@ -161,26 +164,27 @@ def tile_attend_soft_draft_sink_pgb2q256n512t2048_kernel(
                 )
             nc.scalar.activation(neg_t[:, 2 * g : 2 * g + 2, :], scores_t[:], ACT.Copy, scale=-1.0)
 
-        vg = [work.tile([P, N], BF16, name="vg0")]
-        nc.scalar.activation(vg[0][:], v_pool[:].indirect(lists[0]), ACT.Copy)
-
         total = held.tile([P, B * QT], F32, name="total")
         inv = held.tile([P, B * QT], F32, name="inv")
         ps = []
 
-        def softmax(b, raws, nm, places_of_p):
+        def softmax(b, raws):
+            nm = work.tile([P, QT], F32, name=f"nm{b}")
             for h in range(QT):
                 j = b * QT + h
                 nc.vector.tensor_scalar(
                     xs[j][:, :N], raws[h][:], MASKED, xs[j][:, N : N + 1], ALU.min, ALU.min, accum_out=nm[:, h : h + 1]
                 )
-                ps.append(shared.tile([P, N + 1], F32, name=f"p{j}", offset=places_of_p[h]))
+                if j == QT:
+                    ps.append(shared.tile([P, N + 1], F32, name=f"p{j}", offset=AT_X1))
+                else:
+                    ps.append(work.tile([P, N + 1], F32, name=f"p{j}"))
                 nc.scalar.activation(ps[j][:], xs[j][:], ACT.Exp, bias=nm[:, h : h + 1], scale=-1.0, accum_out=total[:, j : j + 1])
 
-        raws = [shared.tile([P, N], F32, name=f"raw{h}", offset=AT_SG + 2 * KB * (1 - h)) for h in range(QT)]
+        raws = [shared.tile([P, N], F32, name=f"raw{h}", offset=AT_SG + 2 * KB * h) for h in range(QT)]
         for h in range(QT):
             nc.vector.tensor_tensor(raws[h][:], pens[h][:], scores[h][:], ALU.subtract)
-        softmax(0, raws, work.tile([P, QT], F32, name="nm0"), [AT_P0, AT_P1])
+        softmax(0, raws)
         raws = [sums.tile([P, N], F32, name=f"raw{QT + h}", offset=BANK * h) for h in range(QT)]
         for h in range(QT):
             for c in range(4):
@@ -205,16 +209,16 @@ def tile_attend_soft_draft_sink_pgb2q256n512t2048_kernel(
         for b in range(B):
             turn(nc, psum, ident, vg[b][:], v_woven[:, b * H : (b + 1) * H])
 
-        softmax(1, raws, shared.tile([P, QT], F32, name="nm1", offset=AT_VS), [AT_X1, AT_P3])
+        softmax(1, raws)
         for h in range(QT):
             nc.gpsimd.tensor_tensor(ws[h][:], ps[h][:, :N], sg[0][:], ALU.mult)
             turn(nc, psum, ident, ws[h][:], w_woven[0][:, h * H : (h + 1) * H])
         for j in range(QT, B * QT):
             nc.vector.tensor_tensor(ws[j][:], ps[j][:, :N], sg[1][:], ALU.mult)
-        vq = shared.tile([P, B * DV], U32, name="vq", offset=AT_P3, align_bytes=64)
+        vq = shared.tile([P, B * DV], U32, name="vq", offset=AT_X3, align_bytes=64)
         vsc = work.tile([P, B * DV], U8, name="vsc", align_bytes=64)
         quantise(nc, v_woven[:], vq[:], vsc[:])
-        wq = [shared.tile([P, NQ], U32, name="wq0", offset=AT_P3 + KB, align_bytes=64), work.tile([P, NQ], U32, name="wq1", align_bytes=64)]
+        wq = [shared.tile([P, NQ], U32, name="wq0", offset=AT_X3 + KB, align_bytes=64), work.tile([P, NQ], U32, name="wq1", align_bytes=64)]
         wsc = [work.tile([P, NQ], U8, name=f"wsc{b}", align_bytes=64) for b in range(B)]
         quantise(nc, w_woven[0][:], wq[0][:], wsc[0][:])
         nc.vector.reciprocal(inv[:], total[:])

@@ -46,7 +46,7 @@ def tile_attend_soft_draft_sink_pgb2q256n512t2048_kernel(
 
         KB = 1024
         BANK = 2 * KB
-        AT_KEYS, AT_POS, AT_VS, AT_SG, AT_X1, AT_X3 = 0, 11 * KB, 19 * KB, 27 * KB, 32 * KB, 35 * KB
+        AT_KEYS, AT_POS, AT_VS, AT_PEN1, AT_X2, AT_X0, AT_X3 = 0, 11 * KB, 19 * KB, 27 * KB, 29 * KB, 32 * KB, 35 * KB
         AT_PG, AT_V = 38 * KB, 44 * KB
         H = N // 2
 
@@ -98,8 +98,8 @@ def tile_attend_soft_draft_sink_pgb2q256n512t2048_kernel(
         nc.scalar.activation(nq[:], cols[:, P - 8 : P - 4], ACT.Copy, scale=-BIG)
         xs = []
         for j in range(B * QT):
-            if j % QT == 1:
-                xs.append(shared.tile([P, N + 1], F32, name=f"x{j}", offset=(AT_X1, AT_X3)[j // QT]))
+            if j != 1:
+                xs.append(shared.tile([P, N + 1], F32, name=f"x{j}", offset={0: AT_X0, 2: AT_X2, 3: AT_X3}[j]))
             else:
                 xs.append(work.tile([P, N + 1], F32, name=f"x{j}"))
             nc.scalar.activation(xs[j][:, N : N + 1], cols[:, P - 4 + j : P - 3 + j], ACT.Copy, scale=-1.0)
@@ -122,7 +122,7 @@ def tile_attend_soft_draft_sink_pgb2q256n512t2048_kernel(
         places = psum.tile([P, N], F32, name="places", tag="turned", bufs=4)
         for c in range(4):
             nc.tensor.transpose(places[:, c * P : (c + 1) * P], columns[0][:, c : c + 1].to_broadcast([P, P]), ident[:])
-        pens = [work.tile([P, N], F32, name=f"pen{h}") for h in range(QT)]
+        pens = [work.tile([P, N], F32, name="pen0"), shared.tile([P, N], F32, name="pen1", offset=AT_PEN1)]
         for h in range(QT):
             nc.scalar.activation(pens[h][:], places[:], ACT.Relu, bias=nq[:, h : h + 1], scale=1.0)
         pen_t = work.tile([P, 4, NQ], F32, name="pen_t")
@@ -168,48 +168,45 @@ def tile_attend_soft_draft_sink_pgb2q256n512t2048_kernel(
         inv = held.tile([P, B * QT], F32, name="inv")
         ps = []
 
-        def softmax(b, raws):
-            nm = work.tile([P, QT], F32, name=f"nm{b}")
-            for h in range(QT):
-                j = b * QT + h
-                nc.vector.tensor_scalar(
-                    xs[j][:, :N], raws[h][:], MASKED, xs[j][:, N : N + 1], ALU.min, ALU.min, accum_out=nm[:, h : h + 1]
-                )
-                if j == QT:
-                    ps.append(shared.tile([P, N + 1], F32, name=f"p{j}", offset=AT_X1))
-                else:
-                    ps.append(work.tile([P, N + 1], F32, name=f"p{j}"))
-                nc.scalar.activation(ps[j][:], xs[j][:], ACT.Exp, bias=nm[:, h : h + 1], scale=-1.0, accum_out=total[:, j : j + 1])
+        nm = held.tile([P, B * QT], F32, name="nm")
 
-        raws = [shared.tile([P, N], F32, name=f"raw{h}", offset=AT_SG + 2 * KB * h) for h in range(QT)]
+        def softmax(j, raw):
+            nc.vector.tensor_scalar(
+                xs[j][:, :N], raw[:], MASKED, xs[j][:, N : N + 1], ALU.min, ALU.min, accum_out=nm[:, j : j + 1]
+            )
+            ps.append(work.tile([P, N + 1], F32, name=f"p{j}"))
+            nc.scalar.activation(ps[j][:], xs[j][:], ACT.Exp, bias=nm[:, j : j + 1], scale=-1.0, accum_out=total[:, j : j + 1])
+
+        raws = [work.tile([P, N], F32, name=f"raw{h}") for h in range(QT)]
         for h in range(QT):
             nc.vector.tensor_tensor(raws[h][:], pens[h][:], scores[h][:], ALU.subtract)
-        softmax(0, raws)
-        raws = [sums.tile([P, N], F32, name=f"raw{QT + h}", offset=BANK * h) for h in range(QT)]
         for h in range(QT):
+            raws.append(sums.tile([P, N], F32, name=f"raw{QT + h}", offset=BANK * h))
             for c in range(4):
                 for k, part in enumerate((neg_t, pen_t)):
                     nc.tensor.matmul(
-                        raws[h][:, c * P : (c + 1) * P],
+                        raws[QT + h][:, c * P : (c + 1) * P],
                         lhsT=part[:, c, h * P : (h + 1) * P],
                         rhs=ident[:],
                         start=(k == 0),
                         stop=(k == 1),
                         is_transpose=True,
                     )
-        sg = [shared.tile([P, N], F32, name=f"sg{b}", offset=AT_SG + 2 * KB * b) for b in range(B)]
-        for b in range(B):
-            nc.vector.tensor_copy(sg[b][:], vs_pool[:].indirect(lists[b]))
-        vg.append(shared.tile([P, N], BF16, name="vg1", offset=AT_X1))
+        softmax(0, raws[0])
+        sg = [shared.tile([P, N], F32, name="sg0", offset=AT_PEN1)]
+        nc.vector.tensor_copy(sg[0][:], vs_pool[:].indirect(lists[0]))
+        vg.append(shared.tile([P, N], BF16, name="vg1", offset=AT_X0))
         nc.scalar.activation(vg[1][:], v_pool[:].indirect(lists[1]), ACT.Copy)
+        for j in range(1, B * QT):
+            softmax(j, raws[j])
+        sg.append(shared.tile([P, N], F32, name="sg1", offset=AT_X2))
+        nc.vector.tensor_copy(sg[1][:], vs_pool[:].indirect(lists[1]))
 
         ws = [work.tile([P, N], BF16, name=f"w{j}") for j in range(B * QT)]
         v_woven = work.tile([P, B * H], F32, name="v_woven", align_bytes=64)
         w_woven = [work.tile([P, QT * H], F32, name=f"w_woven{b}", align_bytes=64) for b in range(B)]
         for b in range(B):
             turn(nc, psum, ident, vg[b][:], v_woven[:, b * H : (b + 1) * H])
-
-        softmax(1, raws)
         for h in range(QT):
             nc.gpsimd.tensor_tensor(ws[h][:], ps[h][:, :N], sg[0][:], ALU.mult)
             turn(nc, psum, ident, ws[h][:], w_woven[0][:, h * H : (h + 1) * H])

@@ -58,7 +58,7 @@ def tile_attend_soft_draft_sink_pgb2q256n512t2048_kernel(
         rows = shared.tile([P, P], F32, name="rows", offset=AT_VS)
         pos_pool = shared.tile([P, T], F32, name="pos_pool", offset=AT_POS)
 
-        nc.vector.memset(ks_pool[:].bitcast(I32), 0)
+        nc.gpsimd.memset(ks_pool[:].bitcast(I32), 0)
         nc.vector.memset(rows[: P - 8, :], 0.0)
         nc.vector.memset(pos_pool[: P - 1, :], 0.0)
 

@@ -16,8 +16,12 @@ U8 = mybir.dt.uint8
 FP8X4 = mybir.dt.float8_e4m3fn_x4
 ALU = mybir.AluOpType
 ACT = mybir.ActivationFunctionType
+AXIS = mybir.AxisListType
 
-BIG = 2.0 ** 64
+BIG = 2.0 ** 80
+MARGIN = 2.0 ** 50
+ULP = 2.0 ** -23
+HUGE = 2.0 ** 127
 MASKED = 30000.0
 
 
@@ -102,10 +106,21 @@ def tile_attend_soft_draft_sink_pgb2q256n512t2048_kernel(
                 xs.append(shared.tile([P, N + 1], F32, name=f"x{j}", offset={0: AT_X0, 2: AT_X2, 3: AT_X3}[j]))
             else:
                 xs.append(work.tile([P, N + 1], F32, name=f"x{j}"))
-            nc.scalar.activation(xs[j][:, N : N + 1], cols[:, P - 4 + j : P - 3 + j], ACT.Copy, scale=-1.0)
+            nc.scalar.activation(xs[j][:, N : N + 1], cols[:, P - 4 + j : P - 3 + j], ACT.Copy, scale=1.0 if j < QT else -1.0)
+        step = work.tile([P, QT], F32, name="step")
+        above = work.tile([P, QT], F32, name="above")
+        limit = work.tile([P, QT], F32, name="limit")
+        nc.scalar.activation(step[:], cols[:, P - 8 : P - 6], ACT.Abs, scale=BIG * ULP)
+        nc.scalar.activation(above[:], step[:], ACT.Copy, bias=MARGIN)
+        for h in range(QT):
+            nc.scalar.activation(
+                limit[:, h : h + 1], cols[:, P - 8 + h : P - 7 + h], ACT.Identity, bias=above[:, h : h + 1], scale=BIG
+            )
         q_row = psum.tile([P, NQ], F32, name="q_row", tag="turned", bufs=4)
         for h in range(QT):
             nc.tensor.transpose(q_row[:, h * P : (h + 1) * P], nq[:, QT + h : QT + h + 1].to_broadcast([P, P]), ident[:])
+        q_rows = work.tile([P, NQ], F32, name="q_rows")
+        nc.scalar.copy(q_rows[:], q_row[:])
 
         for h in range(2):
             nc.scalar.activation(v_pool[:, h * T // 2 : (h + 1) * T // 2], v_raw[h][:], ACT.Copy)
@@ -118,16 +133,17 @@ def tile_attend_soft_draft_sink_pgb2q256n512t2048_kernel(
             for c in range(4):
                 nc.tensor.transpose(upright[:, 4 * b + c, :], pg[:, c * P : (c + 1) * P], ident[:])
             columns.append(shared.tile([P, 4], F32, name=f"columns{b}", offset=AT_V + 4 * KB + 32 * b))
-            nc.scalar.activation(columns[b][:], upright[:, 4 * b : 4 * b + 4, P - 1], ACT.Copy, scale=BIG)
+            nc.scalar.activation(columns[b][:], upright[:, 4 * b : 4 * b + 4, P - 1], ACT.Copy, scale=BIG if b else -BIG)
         places = psum.tile([P, N], F32, name="places", tag="turned", bufs=4)
         for c in range(4):
             nc.tensor.transpose(places[:, c * P : (c + 1) * P], columns[0][:, c : c + 1].to_broadcast([P, P]), ident[:])
-        pens = [work.tile([P, N], F32, name="pen0"), shared.tile([P, N], F32, name="pen1", offset=AT_PEN1)]
-        for h in range(QT):
-            nc.scalar.activation(pens[h][:], places[:], ACT.Relu, bias=nq[:, h : h + 1], scale=1.0)
+        place_rows = shared.tile([P, N], F32, name="place_rows", offset=AT_PEN1)
+        nc.scalar.copy(place_rows[:], places[:])
         pen_t = work.tile([P, 4, NQ], F32, name="pen_t")
+        apart = work.tile([P, 4, NQ], F32, name="apart")
         for c in range(4):
-            nc.scalar.activation(pen_t[:, c, :], q_row[:], ACT.Relu, bias=columns[1][:, c : c + 1], scale=1.0)
+            nc.gpsimd.tensor_scalar(apart[:, c, :], q_rows[:], 1.0, columns[1][:, c : c + 1], ALU.mult, ALU.add)
+            nc.gpsimd.tensor_scalar(pen_t[:, c, :], apart[:, c, :], HUGE, 0.0, ALU.min, ALU.max)
 
         vg = [work.tile([P, N], BF16, name="vg0")]
         nc.scalar.activation(vg[0][:], v_pool[:].indirect(lists[0]), ACT.Copy)
@@ -171,15 +187,18 @@ def tile_attend_soft_draft_sink_pgb2q256n512t2048_kernel(
         nm = held.tile([P, B * QT], F32, name="nm")
 
         def softmax(j, raw):
-            nc.vector.tensor_scalar(
-                xs[j][:, :N], raw[:], MASKED, xs[j][:, N : N + 1], ALU.min, ALU.min, accum_out=nm[:, j : j + 1]
-            )
+            if j < QT:
+                nc.vector.tensor_reduce(nm[:, j : j + 1], xs[j][:], AXIS.X, ALU.max, negate=True)
+            else:
+                nc.vector.tensor_scalar(
+                    xs[j][:, :N], raw[:], MASKED, xs[j][:, N : N + 1], ALU.min, ALU.min, accum_out=nm[:, j : j + 1]
+                )
             ps.append(work.tile([P, N + 1], F32, name=f"p{j}"))
-            nc.scalar.activation(ps[j][:], xs[j][:], ACT.Exp, bias=nm[:, j : j + 1], scale=-1.0, accum_out=total[:, j : j + 1])
+            nc.scalar.activation(ps[j][:], xs[j][:], ACT.Exp, bias=nm[:, j : j + 1], scale=1.0 if j < QT else -1.0, accum_out=total[:, j : j + 1])
 
-        raws = [work.tile([P, N], F32, name=f"raw{h}") for h in range(QT)]
+        raws = [None] * QT
         for h in range(QT):
-            nc.vector.tensor_tensor(raws[h][:], pens[h][:], scores[h][:], ALU.subtract)
+            nc.vector.scalar_tensor_tensor(xs[h][:, :N], place_rows[:], limit[:, h : h + 1], scores[h][:], ALU.add, ALU.min)
         for h in range(QT):
             raws.append(sums.tile([P, N], F32, name=f"raw{QT + h}", offset=BANK * h))
             for c in range(4):

@@ -25,11 +25,11 @@ HUGE = 2.0 ** 127
 MASKED = 30000.0
 
 
-def turn(nc, psum, ident, rows, woven):
+def turn(nc, psum, ident, rows, woven, parted=False):
     words = rows.bitcast(F32)
     turned = psum.tile([P, 2, P], F32, name="turned", tag="turned", bufs=4)
     for u in range(2):
-        nc.tensor.transpose(turned[:, u, :], words[:, u : N // 2 : 2], ident[:])
+        nc.tensor.transpose(turned[:, u, :], words[:, u * P : (u + 1) * P] if parted else words[:, u : N // 2 : 2], ident[:])
     nc.scalar.copy(woven.rearrange("p (c u) -> p c u", u=2), turned[:].rearrange("p u c -> p c u"))
 
 
@@ -230,7 +230,12 @@ def tile_attend_soft_draft_sink_pgb2q256n512t2048_kernel(
             nc.gpsimd.tensor_tensor(ws[h][:], ps[h][:, :N], sg[0][:], ALU.mult)
             turn(nc, psum, ident, ws[h][:], w_woven[0][:, h * H : (h + 1) * H])
         for j in range(QT, B * QT):
-            nc.vector.tensor_tensor(ws[j][:], ps[j][:, :N], sg[1][:], ALU.mult)
+            nc.vector.tensor_tensor(
+                ws[j][:].rearrange("q (u p e) -> q p u e", u=2, e=2),
+                ps[j][:, :N].rearrange("q (p u e) -> q p u e", u=2, e=2),
+                sg[1][:].rearrange("q (p u e) -> q p u e", u=2, e=2),
+                ALU.mult,
+            )
         vq = shared.tile([P, B * DV], U32, name="vq", offset=AT_X3, align_bytes=64)
         vsc = work.tile([P, B * DV], U8, name="vsc", align_bytes=64)
         quantise(nc, v_woven[:], vq[:], vsc[:])
@@ -239,7 +244,7 @@ def tile_attend_soft_draft_sink_pgb2q256n512t2048_kernel(
         quantise(nc, w_woven[0][:], wq[0][:], wsc[0][:])
         nc.vector.reciprocal(inv[:], total[:])
         for h in range(QT):
-            turn(nc, psum, ident, ws[QT + h][:], w_woven[1][:, h * H : (h + 1) * H])
+            turn(nc, psum, ident, ws[QT + h][:], w_woven[1][:, h * H : (h + 1) * H], parted=True)
         for j in range(B * QT):
             b, h = divmod(j, QT)
             if b == 1:

@@ -5,6 +5,9 @@ import concourse.mybir as mybir
 B, N, T, D, DV, NQ = 2, 512, 2048, 512, 128, 256
 P = 128
 QT = NQ // P
+TILES = B * QT
+CHUNKS = N // P
+WORDS = N // 2
 FLOPS = 2 * B * NQ * N * (D + DV)
 
 F32 = mybir.dt.float32
@@ -19,18 +22,27 @@ ACT = mybir.ActivationFunctionType
 AXIS = mybir.AxisListType
 
 BIG = 2.0 ** 80
+HALF_STEP = 2.0 ** -24 + 2.0 ** -34
 MARGIN = 2.0 ** 50
-ULP = 2.0 ** -23
 HUGE = 2.0 ** 127
 MASKED = 30000.0
 
 
-def turn(nc, psum, ident, rows, woven, parted=False):
-    words = rows.bitcast(F32)
+def turn(nc, psum, ident, even, odd, woven):
     turned = psum.tile([P, 2, P], F32, name="turned", tag="turned", bufs=4)
-    for u in range(2):
-        nc.tensor.transpose(turned[:, u, :], words[:, u * P : (u + 1) * P] if parted else words[:, u : N // 2 : 2], ident[:])
+    for u, words in enumerate((even, odd)):
+        nc.tensor.transpose(turned[:, u, :], words, ident[:])
     nc.scalar.copy(woven.rearrange("p (c u) -> p c u", u=2), turned[:].rearrange("p u c -> p c u"))
+
+
+def in_slot_order(rows):
+    words = rows.bitcast(F32)
+    return words[:, 0:WORDS:2], words[:, 1:WORDS:2]
+
+
+def in_halves(rows):
+    words = rows.bitcast(F32)
+    return words[:, :P], words[:, P:]
 
 
 def quantise(nc, woven, codes, scales):
@@ -50,9 +62,8 @@ def tile_attend_soft_draft_sink_pgb2q256n512t2048_kernel(
 
         KB = 1024
         BANK = 2 * KB
-        AT_KEYS, AT_POS, AT_VS, AT_PEN1, AT_X2, AT_X0, AT_X3 = 0, 11 * KB, 19 * KB, 27 * KB, 29 * KB, 32 * KB, 35 * KB
-        AT_PG, AT_V = 38 * KB, 44 * KB
-        H = N // 2
+        AT_KEYS, AT_POS, AT_VS, AT_PLACES, AT_X2, AT_X0, AT_X3 = 0, 11 * KB, 19 * KB, 27 * KB, 29 * KB, 32 * KB, 35 * KB
+        AT_GATHERED, AT_V = 38 * KB, 44 * KB
 
         offsets = held.tile([P, B * N // 16], U16, name="offsets")
         ks_pool = held.tile([P, T], U8, name="ks_pool", align_bytes=64)
@@ -63,7 +74,7 @@ def tile_attend_soft_draft_sink_pgb2q256n512t2048_kernel(
         pos_pool = shared.tile([P, T], F32, name="pos_pool", offset=AT_POS)
 
         nc.gpsimd.memset(ks_pool[:].bitcast(I32), 0)
-        nc.vector.memset(rows[: P - 8, :], 0.0)
+        nc.vector.memset(rows[: P - 2 * TILES, :], 0.0)
         nc.vector.memset(pos_pool[: P - 1, :], 0.0)
 
         zeros = shared.tile([P, T + B * NQ + B * NQ // 4], F32, name="zeros", offset=AT_KEYS)
@@ -78,8 +89,8 @@ def tile_attend_soft_draft_sink_pgb2q256n512t2048_kernel(
 
         nc.sync.dma_start(offsets[:], offs)
         nc.sync.dma_start(pos_pool[P - 1 :, :], pos[P - 1 :, :])
-        nc.sync.dma_start(rows[P - 8 : P - 4, :], qpos.rearrange("b (h p) o -> (b h) (p o)", p=P))
-        nc.sync.dma_start(rows[P - 4 :, :], sink.rearrange("b (h p) o -> (b h) (p o)", p=P))
+        nc.sync.dma_start(rows[P - 2 * TILES : P - TILES, :], qpos.rearrange("b (h p) o -> (b h) (p o)", p=P))
+        nc.sync.dma_start(rows[P - TILES :, :], sink.rearrange("b (h p) o -> (b h) (p o)", p=P))
         for h in range(2):
             nc.sync.dma_start(v_raw[h][:], vT[:, h * T // 2 : (h + 1) * T // 2])
         for g in range(4):
@@ -96,64 +107,68 @@ def tile_attend_soft_draft_sink_pgb2q256n512t2048_kernel(
 
         cols = psum.tile([P, P], F32, name="cols", tag="turned", bufs=4)
         nc.tensor.transpose(cols[:], rows[:], ident[:])
+        qpos_cols, sink_cols = cols[:, P - 2 * TILES : P - TILES], cols[:, P - TILES :]
         vs_pool = shared.tile([P, T], F32, name="vs_pool", offset=AT_VS)
         nc.sync.dma_start(vs_pool[:], vs)
-        nq = work.tile([P, B * QT], F32, name="nq")
-        nc.scalar.activation(nq[:], cols[:, P - 8 : P - 4], ACT.Copy, scale=-BIG)
+        minus_q = work.tile([P, QT], F32, name="minus_q")
+        nc.scalar.activation(minus_q[:], qpos_cols[:, QT:], ACT.Copy, scale=-BIG)
+
+        signs = [1.0] * QT + [-1.0] * QT
         xs = []
-        for j in range(B * QT):
-            if j != 1:
-                xs.append(shared.tile([P, N + 1], F32, name=f"x{j}", offset={0: AT_X0, 2: AT_X2, 3: AT_X3}[j]))
-            else:
+        for j, at in enumerate((AT_X0, None, AT_X2, AT_X3)):
+            if at is None:
                 xs.append(work.tile([P, N + 1], F32, name=f"x{j}"))
-            nc.scalar.activation(xs[j][:, N : N + 1], cols[:, P - 4 + j : P - 3 + j], ACT.Copy, scale=1.0 if j < QT else -1.0)
+            else:
+                xs.append(shared.tile([P, N + 1], F32, name=f"x{j}", offset=at))
+            nc.scalar.activation(xs[j][:, N : N + 1], sink_cols[:, j : j + 1], ACT.Copy, scale=signs[j])
+
         step = work.tile([P, QT], F32, name="step")
         above = work.tile([P, QT], F32, name="above")
         limit = work.tile([P, QT], F32, name="limit")
-        nc.scalar.activation(step[:], cols[:, P - 8 : P - 6], ACT.Abs, scale=BIG * ULP)
+        nc.scalar.activation(step[:], qpos_cols[:, :QT], ACT.Abs, scale=BIG * HALF_STEP)
         nc.scalar.activation(above[:], step[:], ACT.Copy, bias=MARGIN)
         for h in range(QT):
-            nc.scalar.activation(
-                limit[:, h : h + 1], cols[:, P - 8 + h : P - 7 + h], ACT.Identity, bias=above[:, h : h + 1], scale=BIG
-            )
-        q_row = psum.tile([P, NQ], F32, name="q_row", tag="turned", bufs=4)
+            nc.scalar.activation(limit[:, h : h + 1], qpos_cols[:, h : h + 1], ACT.Identity, bias=above[:, h : h + 1], scale=BIG)
+
+        q_spread = psum.tile([P, NQ], F32, name="q_spread", tag="turned", bufs=4)
         for h in range(QT):
-            nc.tensor.transpose(q_row[:, h * P : (h + 1) * P], nq[:, QT + h : QT + h + 1].to_broadcast([P, P]), ident[:])
+            nc.tensor.transpose(q_spread[:, h * P : (h + 1) * P], minus_q[:, h : h + 1].to_broadcast([P, P]), ident[:])
         q_rows = work.tile([P, NQ], F32, name="q_rows")
-        nc.scalar.copy(q_rows[:], q_row[:])
+        nc.scalar.copy(q_rows[:], q_spread[:])
 
         for h in range(2):
             nc.scalar.activation(v_pool[:, h * T // 2 : (h + 1) * T // 2], v_raw[h][:], ACT.Copy)
 
-        upright = sums.tile([P, 16, P], F32, name="upright", offset=0)
+        upright = sums.tile([P, 4 * CHUNKS, P], F32, name="upright", offset=0)
         columns = []
         for b in range(B):
-            pg = shared.tile([P, N], F32, name=f"pg{b}", offset=AT_PG + 3 * KB * b)
+            pg = shared.tile([P, N], F32, name=f"pg{b}", offset=AT_GATHERED + 3 * KB * b)
             nc.vector.tensor_copy(pg[:], pos_pool[:].indirect(lists[b]))
-            for c in range(4):
-                nc.tensor.transpose(upright[:, 4 * b + c, :], pg[:, c * P : (c + 1) * P], ident[:])
-            columns.append(shared.tile([P, 4], F32, name=f"columns{b}", offset=AT_V + 4 * KB + 32 * b))
-            nc.scalar.activation(columns[b][:], upright[:, 4 * b : 4 * b + 4, P - 1], ACT.Copy, scale=BIG if b else -BIG)
-        places = psum.tile([P, N], F32, name="places", tag="turned", bufs=4)
-        for c in range(4):
-            nc.tensor.transpose(places[:, c * P : (c + 1) * P], columns[0][:, c : c + 1].to_broadcast([P, P]), ident[:])
-        place_rows = shared.tile([P, N], F32, name="place_rows", offset=AT_PEN1)
-        nc.scalar.copy(place_rows[:], places[:])
-        pen_t = work.tile([P, 4, NQ], F32, name="pen_t")
-        apart = work.tile([P, 4, NQ], F32, name="apart")
-        for c in range(4):
+            for c in range(CHUNKS):
+                nc.tensor.transpose(upright[:, CHUNKS * b + c, :], pg[:, c * P : (c + 1) * P], ident[:])
+            columns.append(shared.tile([P, CHUNKS], F32, name=f"columns{b}", offset=AT_V + 4 * KB + 32 * b))
+            nc.scalar.activation(columns[b][:], upright[:, CHUNKS * b : CHUNKS * (b + 1), P - 1], ACT.Copy, scale=-BIG * signs[QT * b])
+        place_spread = psum.tile([P, N], F32, name="place_spread", tag="turned", bufs=4)
+        for c in range(CHUNKS):
+            nc.tensor.transpose(place_spread[:, c * P : (c + 1) * P], columns[0][:, c : c + 1].to_broadcast([P, P]), ident[:])
+        place_rows = shared.tile([P, N], F32, name="place_rows", offset=AT_PLACES)
+        nc.scalar.copy(place_rows[:], place_spread[:])
+
+        penalty = work.tile([P, CHUNKS, NQ], F32, name="penalty")
+        apart = work.tile([P, CHUNKS, NQ], F32, name="apart")
+        for c in range(CHUNKS):
             nc.gpsimd.tensor_scalar(apart[:, c, :], q_rows[:], 1.0, columns[1][:, c : c + 1], ALU.mult, ALU.add)
-            nc.gpsimd.tensor_scalar(pen_t[:, c, :], apart[:, c, :], HUGE, 0.0, ALU.min, ALU.max)
+            nc.gpsimd.tensor_scalar(penalty[:, c, :], apart[:, c, :], HUGE, 0.0, ALU.min, ALU.max)
 
         vg = [work.tile([P, N], BF16, name="vg0")]
         nc.scalar.activation(vg[0][:], v_pool[:].indirect(lists[0]), ACT.Copy)
 
-        ks = shared.tile([P, B * N], U8, name="ks", align_bytes=64, offset=AT_PG)
-        kw = [shared.tile([P, N], U32, name=f"kw{b}", align_bytes=64, offset=AT_PG + 2 * KB * (b + 1)) for b in range(B)]
+        ks = shared.tile([P, B * N], U8, name="ks", align_bytes=64, offset=AT_GATHERED)
+        kw = [shared.tile([P, N], U32, name=f"kw{b}", align_bytes=64, offset=AT_GATHERED + 2 * KB * (b + 1)) for b in range(B)]
         nc.vector.tensor_copy(ks[:], ks_pool[:].indirect(offsets[:]))
         for b in range(B):
             nc.vector.tensor_copy(kw[b][:], kw_pool[:].bitcast(U32).indirect(lists[b]))
-        scores = [sums.tile([P, N], F32, name=f"s{h}", offset=BANK * h) for h in range(QT)]
+        scores = [sums.tile([P, N], F32, name=f"scores{h}", offset=BANK * h) for h in range(QT)]
         for h in range(QT):
             nc.tensor.matmul_mx(
                 out=scores[h][:],
@@ -164,9 +179,9 @@ def tile_attend_soft_draft_sink_pgb2q256n512t2048_kernel(
                 start=True,
                 stop=True,
             )
-        neg_t = work.tile([P, 4, NQ], F32, name="neg_t")
+        negated = work.tile([P, CHUNKS, NQ], F32, name="negated")
         for g in range(2):
-            scores_t = sums.tile([P, 2, NQ], F32, name=f"st{g}", offset=BANK * (QT + g))
+            scores_t = sums.tile([P, 2, NQ], F32, name=f"scores_t{g}", offset=BANK * (QT + g))
             for e in range(2):
                 c = 2 * g + e
                 nc.tensor.matmul_mx(
@@ -178,78 +193,83 @@ def tile_attend_soft_draft_sink_pgb2q256n512t2048_kernel(
                     start=True,
                     stop=True,
                 )
-            nc.scalar.activation(neg_t[:, 2 * g : 2 * g + 2, :], scores_t[:], ACT.Copy, scale=-1.0)
+            nc.scalar.activation(negated[:, 2 * g : 2 * g + 2, :], scores_t[:], ACT.Copy, scale=-1.0)
 
-        total = held.tile([P, B * QT], F32, name="total")
-        inv = held.tile([P, B * QT], F32, name="inv")
+        total = held.tile([P, TILES], F32, name="total")
+        inv = held.tile([P, TILES], F32, name="inv")
+        minus_m = held.tile([P, TILES], F32, name="minus_m")
         ps = []
 
-        nm = held.tile([P, B * QT], F32, name="nm")
-
-        def softmax(j, raw):
-            if j < QT:
-                nc.vector.tensor_reduce(nm[:, j : j + 1], xs[j][:], AXIS.X, ALU.max, negate=True)
-            else:
-                nc.vector.tensor_scalar(
-                    xs[j][:, :N], raw[:], MASKED, xs[j][:, N : N + 1], ALU.min, ALU.min, accum_out=nm[:, j : j + 1]
-                )
-            ps.append(work.tile([P, N + 1], F32, name=f"p{j}"))
-            nc.scalar.activation(ps[j][:], xs[j][:], ACT.Exp, bias=nm[:, j : j + 1], scale=1.0 if j < QT else -1.0, accum_out=total[:, j : j + 1])
-
-        raws = [None] * QT
         for h in range(QT):
             nc.vector.scalar_tensor_tensor(xs[h][:, :N], place_rows[:], limit[:, h : h + 1], scores[h][:], ALU.add, ALU.min)
+        penalised = []
         for h in range(QT):
-            raws.append(sums.tile([P, N], F32, name=f"raw{QT + h}", offset=BANK * h))
-            for c in range(4):
-                for k, part in enumerate((neg_t, pen_t)):
+            penalised.append(sums.tile([P, N], F32, name=f"penalised{h}", offset=BANK * h))
+            for c in range(CHUNKS):
+                for k, part in enumerate((negated, penalty)):
                     nc.tensor.matmul(
-                        raws[QT + h][:, c * P : (c + 1) * P],
+                        penalised[h][:, c * P : (c + 1) * P],
                         lhsT=part[:, c, h * P : (h + 1) * P],
                         rhs=ident[:],
                         start=(k == 0),
                         stop=(k == 1),
                         is_transpose=True,
                     )
-        softmax(0, raws[0])
-        sg = [shared.tile([P, N], F32, name="sg0", offset=AT_PEN1)]
+
+        def softmax(j):
+            if j < QT:
+                nc.vector.tensor_reduce(minus_m[:, j : j + 1], xs[j][:], AXIS.X, ALU.max, negate=True)
+            else:
+                nc.vector.tensor_scalar(
+                    xs[j][:, :N], penalised[j - QT][:], MASKED, xs[j][:, N : N + 1], ALU.min, ALU.min, accum_out=minus_m[:, j : j + 1]
+                )
+            ps.append(work.tile([P, N + 1], F32, name=f"p{j}"))
+            nc.scalar.activation(ps[j][:], xs[j][:], ACT.Exp, bias=minus_m[:, j : j + 1], scale=signs[j], accum_out=total[:, j : j + 1])
+
+        softmax(0)
+        sg = [shared.tile([P, N], F32, name="sg0", offset=AT_PLACES)]
         nc.vector.tensor_copy(sg[0][:], vs_pool[:].indirect(lists[0]))
         vg.append(shared.tile([P, N], BF16, name="vg1", offset=AT_X0))
         nc.scalar.activation(vg[1][:], v_pool[:].indirect(lists[1]), ACT.Copy)
-        for j in range(1, B * QT):
-            softmax(j, raws[j])
+        for j in range(1, TILES):
+            softmax(j)
         sg.append(shared.tile([P, N], F32, name="sg1", offset=AT_X2))
         nc.vector.tensor_copy(sg[1][:], vs_pool[:].indirect(lists[1]))
 
-        ws = [work.tile([P, N], BF16, name=f"w{j}") for j in range(B * QT)]
-        v_woven = work.tile([P, B * H], F32, name="v_woven", align_bytes=64)
-        w_woven = [work.tile([P, QT * H], F32, name=f"w_woven{b}", align_bytes=64) for b in range(B)]
+        ws = [work.tile([P, N], BF16, name=f"w{j}") for j in range(TILES)]
+        v_woven = work.tile([P, B * WORDS], F32, name="v_woven", align_bytes=64)
+        w_woven = [work.tile([P, QT * WORDS], F32, name=f"w_woven{b}", align_bytes=64) for b in range(B)]
         for b in range(B):
-            turn(nc, psum, ident, vg[b][:], v_woven[:, b * H : (b + 1) * H])
+            turn(nc, psum, ident, *in_slot_order(vg[b][:]), v_woven[:, b * WORDS : (b + 1) * WORDS])
         for h in range(QT):
             nc.gpsimd.tensor_tensor(ws[h][:], ps[h][:, :N], sg[0][:], ALU.mult)
-            turn(nc, psum, ident, ws[h][:], w_woven[0][:, h * H : (h + 1) * H])
-        for j in range(QT, B * QT):
+            turn(nc, psum, ident, *in_slot_order(ws[h][:]), w_woven[0][:, h * WORDS : (h + 1) * WORDS])
+        for j in range(QT, TILES):
             nc.vector.tensor_tensor(
                 ws[j][:].rearrange("q (u p e) -> q p u e", u=2, e=2),
                 ps[j][:, :N].rearrange("q (p u e) -> q p u e", u=2, e=2),
                 sg[1][:].rearrange("q (p u e) -> q p u e", u=2, e=2),
                 ALU.mult,
             )
+
         vq = shared.tile([P, B * DV], U32, name="vq", offset=AT_X3, align_bytes=64)
         vsc = work.tile([P, B * DV], U8, name="vsc", align_bytes=64)
         quantise(nc, v_woven[:], vq[:], vsc[:])
-        wq = [shared.tile([P, NQ], U32, name="wq0", offset=AT_X3 + KB, align_bytes=64), work.tile([P, NQ], U32, name="wq1", align_bytes=64)]
+        wq = [
+            shared.tile([P, NQ], U32, name="wq0", offset=AT_X3 + KB, align_bytes=64),
+            work.tile([P, NQ], U32, name="wq1", align_bytes=64),
+        ]
         wsc = [work.tile([P, NQ], U8, name=f"wsc{b}", align_bytes=64) for b in range(B)]
         quantise(nc, w_woven[0][:], wq[0][:], wsc[0][:])
         nc.vector.reciprocal(inv[:], total[:])
         for h in range(QT):
-            turn(nc, psum, ident, ws[QT + h][:], w_woven[1][:, h * H : (h + 1) * H], parted=True)
-        for j in range(B * QT):
+            turn(nc, psum, ident, *in_halves(ws[QT + h][:]), w_woven[1][:, h * WORDS : (h + 1) * WORDS])
+
+        for j in range(TILES):
             b, h = divmod(j, QT)
             if b == 1:
-                quantise(nc, w_woven[1][:, h * H : (h + 1) * H], wq[1][:, h * P : (h + 1) * P], wsc[1][:, h * P : (h + 1) * P])
-            y = sums.tile([P, DV], F32, name=f"y{j}", offset=BANK * ((j + QT) % 4))
+                quantise(nc, w_woven[1][:, h * WORDS : (h + 1) * WORDS], wq[1][:, h * P : (h + 1) * P], wsc[1][:, h * P : (h + 1) * P])
+            y = sums.tile([P, DV], F32, name=f"y{j}", offset=BANK * ((j + QT) % TILES))
             nc.tensor.matmul_mx(
                 out=y[:],
                 lhsT=wq[b][:, h * P : (h + 1) * P].bitcast(FP8X4),
@@ -260,7 +280,7 @@ def tile_attend_soft_draft_sink_pgb2q256n512t2048_kernel(
                 stop=True,
             )
             res = work.tile([P, DV], F32, name=f"res{j}")
-            if j == B * QT - 1:
+            if j == TILES - 1:
                 nc.vector.tensor_scalar(res[:], y[:], inv[:, j : j + 1], None, ALU.mult)
             else:
                 nc.scalar.activation(res[:], y[:], ACT.Copy, scale=inv[:, j : j + 1])

@@ -7,7 +7,10 @@ P = 128
 QT = NQ // P
 TILES = B * QT
 CHUNKS = N // P
+PLACES = 4
 WORDS = N // 2
+XW = N + PLACES
+RUN = P + PLACES
 FLOPS = 2 * B * NQ * N * (D + DV)
 
 F32 = mybir.dt.float32
@@ -24,29 +27,11 @@ AXIS = mybir.AxisListType
 BIG = 2.0 ** 80
 HALF_STEP = 2.0 ** -24 + 2.0 ** -34
 MARGIN = 2.0 ** 50
-HUGE = 2.0 ** 127
-MASKED = 30000.0
-
-
-def turn(nc, psum, ident, even, odd, woven):
-    turned = psum.tile([P, 2, P], F32, name="turned", tag="turned", bufs=4)
-    for u, words in enumerate((even, odd)):
-        nc.tensor.transpose(turned[:, u, :], words, ident[:])
-    nc.scalar.copy(woven.rearrange("p (c u) -> p c u", u=2), turned[:].rearrange("p u c -> p c u"))
-
-
-def in_slot_order(rows):
-    words = rows.bitcast(F32)
-    return words[:, 0:WORDS:2], words[:, 1:WORDS:2]
-
-
-def in_halves(rows):
-    words = rows.bitcast(F32)
-    return words[:, :P], words[:, P:]
+FILLER = -(2.0 ** 100)
 
 
 def quantise(nc, woven, codes, scales):
-    nc.vector.quantize_mx(out=codes.bitcast(FP8X4), scales=scales, in_=woven.bitcast(BF16))
+    nc.vector.quantize_mx(out=codes.bitcast(FP8X4), scales=scales, in_=woven)
 
 
 def tile_attend_soft_draft_sink_pgb2q256n512t2048_kernel(
@@ -57,42 +42,47 @@ def tile_attend_soft_draft_sink_pgb2q256n512t2048_kernel(
         held = ctx.enter_context(tc.tile_pool(name="held", bufs=1))
         work = ctx.enter_context(tc.tile_pool(name="work", bufs=1))
         shared = ctx.enter_context(tc.tile_pool(name="shared", bufs=1))
-        psum = ctx.enter_context(tc.psum_pool(name="psum", bufs=1))
-        sums = ctx.enter_context(tc.psum_pool(name="sums", bufs=1))
+        banks = ctx.enter_context(tc.psum_pool(name="banks", bufs=1))
 
         KB = 1024
         BANK = 2 * KB
-        AT_KEYS, AT_POS, AT_VS, AT_PLACES, AT_X2, AT_X0, AT_X3 = 0, 11 * KB, 19 * KB, 27 * KB, 29 * KB, 32 * KB, 35 * KB
-        AT_GATHERED, AT_V = 38 * KB, 44 * KB
+        AT_KEYS, AT_Q, AT_QS, AT_ROWS, AT_V, AT_END = 0, 8 * KB, 10 * KB, 11 * KB, 12 * KB, 20 * KB
+        AT_SG1 = AT_END
+        AT_P = AT_END + 2 * KB
+        P_BYTES = 4 * PLACES * RUN
 
         offsets = held.tile([P, B * N // 16], U16, name="offsets")
         ks_pool = held.tile([P, T], U8, name="ks_pool", align_bytes=64)
-        v_raw = [shared.tile([P, T // 2], F32, name=f"v_raw{h}", offset=AT_V + 4 * KB * h) for h in range(2)]
-        v_pool = held.tile([P, T], BF16, name="v_pool")
+        pos_pool = held.tile([P, T], F32, name="pos_pool")
         ident = held.tile([P, P], F32, name="ident")
-        rows = shared.tile([P, P], F32, name="rows", offset=AT_VS)
-        pos_pool = shared.tile([P, T], F32, name="pos_pool", offset=AT_POS)
+        xs = held.tile([P, TILES, XW], F32, name="xs")
 
-        nc.gpsimd.memset(ks_pool[:].bitcast(I32), 0)
-        nc.vector.memset(rows[: P - 2 * TILES, :], 0.0)
+        vs_pool = held.tile([P, T], F32, name="vs_pool")
+        filler = work.tile([P, PLACES], F32, name="filler")
+        nc.vector.memset(filler[:], FILLER)
+        nc.scalar.copy(xs[:, :, N:], filler[:].unsqueeze(1).to_broadcast([P, TILES, PLACES]))
         nc.vector.memset(pos_pool[: P - 1, :], 0.0)
-
-        zeros = shared.tile([P, T + B * NQ + B * NQ // 4], F32, name="zeros", offset=AT_KEYS)
+        zeros = shared.tile([P, AT_END // 4], F32, name="zeros", offset=0)
         nc.gpsimd.memset(zeros[:, :P], 0.0)
+        nc.gpsimd.memset(ks_pool[:].bitcast(I32), 0)
         nc.gpsimd.affine_select(
             out=ident[:], in_=zeros[:, :P], compare_op=ALU.not_equal, fill=1.0, base=0, pattern=[[-1, P]], channel_multiplier=1
         )
         kw_pool = shared.tile([P, T], I32, name="kw_pool", offset=AT_KEYS)
-        qw = shared.tile([P, B, NQ], I32, name="qw", offset=AT_KEYS + 4 * T, align_bytes=64)
-        qs = shared.tile([P, B * NQ], U8, name="qs", offset=AT_KEYS + 4 * T + 4 * B * NQ, align_bytes=64)
+        qw = shared.tile([P, B, NQ], I32, name="qw", offset=AT_Q, align_bytes=64)
+        qs = shared.tile([P, B * NQ], U8, name="qs", offset=AT_QS, align_bytes=64)
+        rows = shared.tile([P, P], F32, name="rows", offset=AT_ROWS)
+        v_pool = shared.tile([P, T], F32, name="v_pool", offset=AT_V)
         nc.gpsimd.memset(qs[:].bitcast(I32), 0)
+        nc.gpsimd.memset(rows[: P - 2 * TILES, :], 0.0)
+        nc.gpsimd.dma_start(rows[P - 2 * TILES : P - TILES, :], qpos.rearrange("b (h p) o -> (b h) (p o)", p=P))
+        nc.gpsimd.dma_start(rows[P - TILES :, :], sink.rearrange("b (h p) o -> (b h) (p o)", p=P))
+        nc.vector.memset(vs_pool[: P - 1, : T // 2], 0.0)
+        nc.gpsimd.memset(vs_pool[: P - 1, T // 2 :], 0.0)
 
         nc.sync.dma_start(offsets[:], offs)
         nc.sync.dma_start(pos_pool[P - 1 :, :], pos[P - 1 :, :])
-        nc.sync.dma_start(rows[P - 2 * TILES : P - TILES, :], qpos.rearrange("b (h p) o -> (b h) (p o)", p=P))
-        nc.sync.dma_start(rows[P - TILES :, :], sink.rearrange("b (h p) o -> (b h) (p o)", p=P))
-        for h in range(2):
-            nc.sync.dma_start(v_raw[h][:], vT[:, h * T // 2 : (h + 1) * T // 2])
+        nc.sync.dma_start(vs_pool[P - 1 :, :], vs[P - 1 :, :])
         for g in range(4):
             nc.sync.dma_start(ks_pool[32 * g : 32 * g + 4, :].bitcast(I32), k_scales[0, 4 * g : 4 * g + 4, :].bitcast(I32))
         nc.sync.dma_start(kw_pool[:], k_words[0].rearrange("p t r -> p (t r)").bitcast(I32))
@@ -102,174 +92,131 @@ def tile_attend_soft_draft_sink_pgb2q256n512t2048_kernel(
                 qs[32 * g : 32 * g + 4, :].bitcast(I32).rearrange("f (b q) -> f b q", b=B),
                 q_scales[:, 0, 4 * g : 4 * g + 4, :].rearrange("b f q -> f b q").bitcast(I32),
             )
+        nc.sync.dma_start(v_pool[:], vT)
 
         lists = [offsets[:, b * N // 16 : (b + 1) * N // 16] for b in range(B)]
 
-        cols = psum.tile([P, P], F32, name="cols", tag="turned", bufs=4)
-        nc.tensor.transpose(cols[:], rows[:], ident[:])
-        qpos_cols, sink_cols = cols[:, P - 2 * TILES : P - TILES], cols[:, P - TILES :]
-        vs_pool = shared.tile([P, T], F32, name="vs_pool", offset=AT_VS)
-        nc.sync.dma_start(vs_pool[:], vs)
-        minus_q = work.tile([P, QT], F32, name="minus_q")
-        nc.scalar.activation(minus_q[:], qpos_cols[:, QT:], ACT.Copy, scale=-BIG)
-
-        signs = [1.0] * QT + [-1.0] * QT
-        xs = []
-        for j, at in enumerate((AT_X0, None, AT_X2, AT_X3)):
-            if at is None:
-                xs.append(work.tile([P, N + 1], F32, name=f"x{j}"))
-            else:
-                xs.append(shared.tile([P, N + 1], F32, name=f"x{j}", offset=at))
-            nc.scalar.activation(xs[j][:, N : N + 1], sink_cols[:, j : j + 1], ACT.Copy, scale=signs[j])
-
-        step = work.tile([P, QT], F32, name="step")
-        above = work.tile([P, QT], F32, name="above")
-        limit = work.tile([P, QT], F32, name="limit")
-        nc.scalar.activation(step[:], qpos_cols[:, :QT], ACT.Abs, scale=BIG * HALF_STEP)
-        nc.scalar.activation(above[:], step[:], ACT.Copy, bias=MARGIN)
-        for h in range(QT):
-            nc.scalar.activation(limit[:, h : h + 1], qpos_cols[:, h : h + 1], ACT.Identity, bias=above[:, h : h + 1], scale=BIG)
-
-        q_spread = psum.tile([P, NQ], F32, name="q_spread", tag="turned", bufs=4)
-        for h in range(QT):
-            nc.tensor.transpose(q_spread[:, h * P : (h + 1) * P], minus_q[:, h : h + 1].to_broadcast([P, P]), ident[:])
-        q_rows = work.tile([P, NQ], F32, name="q_rows")
-        nc.scalar.copy(q_rows[:], q_spread[:])
-
-        for h in range(2):
-            nc.scalar.activation(v_pool[:, h * T // 2 : (h + 1) * T // 2], v_raw[h][:], ACT.Copy)
-
-        upright = sums.tile([P, 4 * CHUNKS, P], F32, name="upright", offset=0)
-        columns = []
-        for b in range(B):
-            pg = shared.tile([P, N], F32, name=f"pg{b}", offset=AT_GATHERED + 3 * KB * b)
-            nc.vector.tensor_copy(pg[:], pos_pool[:].indirect(lists[b]))
-            for c in range(CHUNKS):
-                nc.tensor.transpose(upright[:, CHUNKS * b + c, :], pg[:, c * P : (c + 1) * P], ident[:])
-            columns.append(shared.tile([P, CHUNKS], F32, name=f"columns{b}", offset=AT_V + 4 * KB + 32 * b))
-            nc.scalar.activation(columns[b][:], upright[:, CHUNKS * b : CHUNKS * (b + 1), P - 1], ACT.Copy, scale=-BIG * signs[QT * b])
-        place_spread = psum.tile([P, N], F32, name="place_spread", tag="turned", bufs=4)
-        for c in range(CHUNKS):
-            nc.tensor.transpose(place_spread[:, c * P : (c + 1) * P], columns[0][:, c : c + 1].to_broadcast([P, P]), ident[:])
-        place_rows = shared.tile([P, N], F32, name="place_rows", offset=AT_PLACES)
-        nc.scalar.copy(place_rows[:], place_spread[:])
-
-        penalty = work.tile([P, CHUNKS, NQ], F32, name="penalty")
-        apart = work.tile([P, CHUNKS, NQ], F32, name="apart")
-        for c in range(CHUNKS):
-            nc.gpsimd.tensor_scalar(apart[:, c, :], q_rows[:], 1.0, columns[1][:, c : c + 1], ALU.mult, ALU.add)
-            nc.gpsimd.tensor_scalar(penalty[:, c, :], apart[:, c, :], HUGE, 0.0, ALU.min, ALU.max)
-
-        vg = [work.tile([P, N], BF16, name="vg0")]
-        nc.scalar.activation(vg[0][:], v_pool[:].indirect(lists[0]), ACT.Copy)
-
-        ks = shared.tile([P, B * N], U8, name="ks", align_bytes=64, offset=AT_GATHERED)
-        kw = [shared.tile([P, N], U32, name=f"kw{b}", align_bytes=64, offset=AT_GATHERED + 2 * KB * (b + 1)) for b in range(B)]
+        ks = work.tile([P, B * N], U8, name="ks", align_bytes=64)
+        kw = [work.tile([P, N], U32, name=f"kw{b}", align_bytes=64) for b in range(B)]
         nc.vector.tensor_copy(ks[:], ks_pool[:].indirect(offsets[:]))
         for b in range(B):
             nc.vector.tensor_copy(kw[b][:], kw_pool[:].bitcast(U32).indirect(lists[b]))
-        scores = [sums.tile([P, N], F32, name=f"scores{h}", offset=BANK * h) for h in range(QT)]
-        for h in range(QT):
+
+        pg = [work.tile([P, N], F32, name=f"pg{b}") for b in range(B)]
+        upright = [banks.tile([P, (3 - b) * CHUNKS, P], F32, name=f"upright{b}", offset=BANK * (2 - 2 * b)) for b in range(B)]
+        for b in range(B):
+            nc.scalar.activation(pg[b][:], pos_pool[:].indirect(lists[b]), ACT.Copy)
+            for c in range(CHUNKS):
+                nc.tensor.transpose(upright[b][:, c, :], pg[b][:, c * P : (c + 1) * P], ident[:])
+
+        columns = [shared.tile([P, CHUNKS], F32, name="columns0", offset=AT_SG1), work.tile([P, CHUNKS], F32, name="columns1")]
+        place_rows = [work.tile([P, N], F32, name=f"place_rows{b}") for b in range(B)]
+        scale_cols = [work.tile([P, PLACES], F32, name=f"scale_cols{b}") for b in range(B)]
+
+        def spread(b):
+            place_spread = banks.tile([P, N], F32, name=f"place_spread{b}", offset=BANK * (5 - b))
+            for c in range(CHUNKS):
+                nc.tensor.transpose(place_spread[:, c * P : (c + 1) * P], columns[b][:, c : c + 1].to_broadcast([P, P]), ident[:])
+            nc.scalar.copy(place_rows[b][:], place_spread[:])
+
+        def scales_of(b, sg):
+            nc.scalar.activation(sg[:], vs_pool[:].indirect(lists[b]), ACT.Copy)
+            nc.sync.dma_start(scale_cols[b][:], sg[P - 1 :, :])
+
+        nc.scalar.activation(columns[0][:], upright[0][:, :CHUNKS, P - 1], ACT.Copy, scale=-BIG)
+        scales_of(0, work.tile([P, N], F32, name="sg0"))
+        nc.scalar.activation(columns[1][:], upright[1][:, :CHUNKS, P - 1], ACT.Copy, scale=-BIG)
+        spread(0)
+
+        cols = banks.tile([P, 3 * CHUNKS, P], F32, name="cols", offset=BANK * 2)
+        nc.tensor.transpose(cols[:, 0, :], rows[:], ident[:])
+        qpos_cols, sink_cols = cols[:, 0, P - 2 * TILES : P - TILES], cols[:, 0, P - TILES :]
+        step = work.tile([P, TILES], F32, name="step")
+        base = work.tile([P, TILES], F32, name="base")
+        limit = work.tile([P, TILES], F32, name="limit")
+        nc.scalar.activation(step[:], qpos_cols, ACT.Abs, scale=BIG * HALF_STEP)
+        nc.scalar.activation(base[:], qpos_cols, ACT.Copy, bias=MARGIN, scale=BIG)
+        nc.gpsimd.tensor_tensor(limit[:], base[:], step[:], ALU.add)
+        nc.scalar.activation(xs[:, :, N], sink_cols, ACT.Copy)
+
+        scores = []
+
+        def score(j):
+            b, h = divmod(j, QT)
+            scores.append(banks.tile([P, N], F32, name=f"scores{j}", offset=BANK * j))
             nc.tensor.matmul_mx(
-                out=scores[h][:],
-                lhsT=qw[:, 0, h * P : (h + 1) * P].bitcast(FP8X4),
-                lhsT_scale=qs[:, h * P : (h + 1) * P],
-                rhs=kw[0][:].bitcast(FP8X4),
-                rhs_scale=ks[:, :N],
+                out=scores[j][:],
+                lhsT=qw[:, b, h * P : (h + 1) * P].bitcast(FP8X4),
+                lhsT_scale=qs[:, j * P : (j + 1) * P],
+                rhs=kw[b][:].bitcast(FP8X4),
+                rhs_scale=ks[:, b * N : (b + 1) * N],
                 start=True,
                 stop=True,
             )
-        negated = work.tile([P, CHUNKS, NQ], F32, name="negated")
-        for g in range(2):
-            scores_t = sums.tile([P, 2, NQ], F32, name=f"scores_t{g}", offset=BANK * (QT + g))
-            for e in range(2):
-                c = 2 * g + e
-                nc.tensor.matmul_mx(
-                    out=scores_t[:, e, :],
-                    lhsT=kw[1][:, c * P : (c + 1) * P].bitcast(FP8X4),
-                    lhsT_scale=ks[:, N + c * P : N + (c + 1) * P],
-                    rhs=qw[:, 1, :].bitcast(FP8X4),
-                    rhs_scale=qs[:, NQ:],
-                    start=True,
-                    stop=True,
-                )
-            nc.scalar.activation(negated[:, 2 * g : 2 * g + 2, :], scores_t[:], ACT.Copy, scale=-1.0)
 
+        score(0)
+        score(1)
+        scales_of(1, shared.tile([P, N], F32, name="sg1", offset=AT_SG1))
+        spread(1)
+        score(2)
+        score(3)
+
+        minus_m = held.tile([P, TILES], F32, name="minus_m")
         total = held.tile([P, TILES], F32, name="total")
         inv = held.tile([P, TILES], F32, name="inv")
-        minus_m = held.tile([P, TILES], F32, name="minus_m")
-        ps = []
-
-        for h in range(QT):
-            nc.vector.scalar_tensor_tensor(xs[h][:, :N], place_rows[:], limit[:, h : h + 1], scores[h][:], ALU.add, ALU.min)
-        penalised = []
-        for h in range(QT):
-            penalised.append(sums.tile([P, N], F32, name=f"penalised{h}", offset=BANK * h))
-            for c in range(CHUNKS):
-                for k, part in enumerate((negated, penalty)):
-                    nc.tensor.matmul(
-                        penalised[h][:, c * P : (c + 1) * P],
-                        lhsT=part[:, c, h * P : (h + 1) * P],
-                        rhs=ident[:],
-                        start=(k == 0),
-                        stop=(k == 1),
-                        is_transpose=True,
-                    )
-
-        def softmax(j):
-            if j < QT:
-                nc.vector.tensor_reduce(minus_m[:, j : j + 1], xs[j][:], AXIS.X, ALU.max, negate=True)
-            else:
-                nc.vector.tensor_scalar(
-                    xs[j][:, :N], penalised[j - QT][:], MASKED, xs[j][:, N : N + 1], ALU.min, ALU.min, accum_out=minus_m[:, j : j + 1]
-                )
-            ps.append(work.tile([P, N + 1], F32, name=f"p{j}"))
-            nc.scalar.activation(ps[j][:], xs[j][:], ACT.Exp, bias=minus_m[:, j : j + 1], scale=signs[j], accum_out=total[:, j : j + 1])
-
-        softmax(0)
-        sg = [shared.tile([P, N], F32, name="sg0", offset=AT_PLACES)]
-        nc.vector.tensor_copy(sg[0][:], vs_pool[:].indirect(lists[0]))
-        vg.append(shared.tile([P, N], BF16, name="vg1", offset=AT_X0))
-        nc.scalar.activation(vg[1][:], v_pool[:].indirect(lists[1]), ACT.Copy)
-        for j in range(1, TILES):
-            softmax(j)
-        sg.append(shared.tile([P, N], F32, name="sg1", offset=AT_X2))
-        nc.vector.tensor_copy(sg[1][:], vs_pool[:].indirect(lists[1]))
-
-        ws = [work.tile([P, N], BF16, name=f"w{j}") for j in range(TILES)]
-        v_woven = work.tile([P, B * WORDS], F32, name="v_woven", align_bytes=64)
-        w_woven = [work.tile([P, QT * WORDS], F32, name=f"w_woven{b}", align_bytes=64) for b in range(B)]
         for b in range(B):
-            turn(nc, psum, ident, *in_slot_order(vg[b][:]), v_woven[:, b * WORDS : (b + 1) * WORDS])
-        for h in range(QT):
-            nc.gpsimd.tensor_tensor(ws[h][:], ps[h][:, :N], sg[0][:], ALU.mult)
-            turn(nc, psum, ident, *in_slot_order(ws[h][:]), w_woven[0][:, h * WORDS : (h + 1) * WORDS])
-        for j in range(QT, TILES):
+            for j in range(QT * b, QT * (b + 1)):
+                nc.vector.scalar_tensor_tensor(xs[:, j, :N], place_rows[b][:], limit[:, j : j + 1], scores[j][:], ALU.add, ALU.min)
+            for j in range(QT * b, QT * (b + 1)):
+                nc.vector.tensor_reduce(minus_m[:, j : j + 1], xs[:, j, : N + 1], AXIS.X, ALU.max, negate=True)
+
+        v_turned = []
+        for b in range(B):
+            vg = shared.tile([P, N], BF16, name=f"vg{b}", offset=AT_P + (2 * b + 1) * P_BYTES - KB // 2)
+            nc.scalar.activation(vg[:], v_pool[:].indirect(lists[b]), ACT.Copy)
+            v_turned.append(banks.tile([P, 2, P], F32, name=f"v_turned{b}", offset=BANK * b))
+            words = vg[:].bitcast(F32)
+            for u in range(2):
+                nc.tensor.transpose(v_turned[b][:, u, :], words[:, u:WORDS:2], ident[:])
+
+        w_woven = [work.tile([P, QT * N], BF16, name=f"w_woven{b}", align_bytes=64) for b in range(B)]
+        for j in range(TILES):
+            b, h = divmod(j, QT)
+            p = shared.tile([P, PLACES, RUN], F32, name=f"p{j}", offset=AT_P + j * P_BYTES)
+            nc.scalar.activation(
+                p[:, :, : XW // PLACES].rearrange("q t c -> q c t"),
+                xs[:, j, :].rearrange("q (c t) -> q c t", t=PLACES),
+                ACT.Exp,
+                bias=minus_m[:, j : j + 1],
+                accum_out=total[:, j : j + 1],
+            )
+            p_turned = banks.tile([P, PLACES, P], F32, name=f"p_turned{j}", offset=BANK * (4 + j))
+            for t in range(PLACES):
+                nc.tensor.transpose(p_turned[:, t, :], p[:, t, :P], ident[:])
             nc.vector.tensor_tensor(
-                ws[j][:].rearrange("q (u p e) -> q p u e", u=2, e=2),
-                ps[j][:, :N].rearrange("q (p u e) -> q p u e", u=2, e=2),
-                sg[1][:].rearrange("q (p u e) -> q p u e", u=2, e=2),
+                w_woven[b][:, h * N : (h + 1) * N].rearrange("p (q t) -> p q t", t=PLACES),
+                p_turned[:].rearrange("p t q -> p q t"),
+                scale_cols[b][:].unsqueeze(1).to_broadcast([P, P, PLACES]),
                 ALU.mult,
             )
 
-        vq = shared.tile([P, B * DV], U32, name="vq", offset=AT_X3, align_bytes=64)
-        vsc = work.tile([P, B * DV], U8, name="vsc", align_bytes=64)
-        quantise(nc, v_woven[:], vq[:], vsc[:])
-        wq = [
-            shared.tile([P, NQ], U32, name="wq0", offset=AT_X3 + KB, align_bytes=64),
-            work.tile([P, NQ], U32, name="wq1", align_bytes=64),
-        ]
+        v_woven = work.tile([P, B * WORDS], F32, name="v_woven", align_bytes=64)
+        for b in range(B):
+            nc.scalar.copy(
+                v_woven[:, b * WORDS : (b + 1) * WORDS].rearrange("p (c u) -> p c u", u=2), v_turned[b][:].rearrange("p u c -> p c u")
+            )
+        wq = [work.tile([P, NQ], U32, name=f"wq{b}", align_bytes=64) for b in range(B)]
         wsc = [work.tile([P, NQ], U8, name=f"wsc{b}", align_bytes=64) for b in range(B)]
+        vq = work.tile([P, B * DV], U32, name="vq", align_bytes=64)
+        vsc = work.tile([P, B * DV], U8, name="vsc", align_bytes=64)
         quantise(nc, w_woven[0][:], wq[0][:], wsc[0][:])
         nc.vector.reciprocal(inv[:], total[:])
-        for h in range(QT):
-            turn(nc, psum, ident, *in_halves(ws[QT + h][:]), w_woven[1][:, h * WORDS : (h + 1) * WORDS])
+        quantise(nc, v_woven[:].bitcast(BF16), vq[:], vsc[:])
+        quantise(nc, w_woven[1][:], wq[1][:], wsc[1][:])
 
         for j in range(TILES):
             b, h = divmod(j, QT)
-            if b == 1:
-                quantise(nc, w_woven[1][:, h * WORDS : (h + 1) * WORDS], wq[1][:, h * P : (h + 1) * P], wsc[1][:, h * P : (h + 1) * P])
-            y = sums.tile([P, DV], F32, name=f"y{j}", offset=BANK * ((j + QT) % TILES))
+            y = banks.tile([P, DV], F32, name=f"y{j}", offset=BANK * (4 + (j + QT) % TILES))
             nc.tensor.matmul_mx(
                 out=y[:],
                 lhsT=wq[b][:, h * P : (h + 1) * P].bitcast(FP8X4),

@@ -46,9 +46,7 @@ def tile_attend_soft_draft_sink_pgb2q256n512t2048_kernel(
 
         KB = 1024
         BANK = 2 * KB
-        AT_KEYS, AT_Q, AT_QS, AT_ROWS, AT_V, AT_END = 0, 8 * KB, 10 * KB, 11 * KB, 12 * KB, 20 * KB
-        AT_SG1 = AT_END
-        AT_P = AT_END + 2 * KB
+        AT_KEYS, AT_SG1, AT_P = 0, 8 * KB, 10 * KB
         P_BYTES = 4 * PLACES * RUN
 
         offsets = held.tile([P, B * N // 16], U16, name="offsets")
@@ -62,23 +60,20 @@ def tile_attend_soft_draft_sink_pgb2q256n512t2048_kernel(
         nc.vector.memset(filler[:], FILLER)
         nc.scalar.copy(xs[:, :, N:], filler[:].unsqueeze(1).to_broadcast([P, TILES, PLACES]))
         nc.vector.memset(pos_pool[: P - 1, :], 0.0)
-        zeros = shared.tile([P, AT_END // 4], F32, name="zeros", offset=0)
-        nc.gpsimd.memset(zeros[:, :P], 0.0)
+        nc.vector.memset(vs_pool[: P - 1, :], 0.0)
+        zeros = work.tile([P, P], F32, name="zeros")
         nc.gpsimd.memset(ks_pool[:].bitcast(I32), 0)
+        nc.gpsimd.memset(zeros[:], 0.0)
         nc.gpsimd.affine_select(
-            out=ident[:], in_=zeros[:, :P], compare_op=ALU.not_equal, fill=1.0, base=0, pattern=[[-1, P]], channel_multiplier=1
+            out=ident[:], in_=zeros[:], compare_op=ALU.not_equal, fill=1.0, base=0, pattern=[[-1, P]], channel_multiplier=1
         )
         kw_pool = shared.tile([P, T], I32, name="kw_pool", offset=AT_KEYS)
-        qw = shared.tile([P, B, NQ], I32, name="qw", offset=AT_Q, align_bytes=64)
-        qs = shared.tile([P, B * NQ], U8, name="qs", offset=AT_QS, align_bytes=64)
-        rows = shared.tile([P, P], F32, name="rows", offset=AT_ROWS)
-        v_pool = shared.tile([P, T], F32, name="v_pool", offset=AT_V)
+        qw = work.tile([P, B, NQ], I32, name="qw", align_bytes=64)
+        qs = work.tile([P, B * NQ], U8, name="qs", align_bytes=64)
+        rows = shared.tile([P, P], F32, name="rows", offset=AT_SG1)
+        v_pool = held.tile([P, T], F32, name="v_pool")
         nc.gpsimd.memset(qs[:].bitcast(I32), 0)
         nc.gpsimd.memset(rows[: P - 2 * TILES, :], 0.0)
-        nc.gpsimd.dma_start(rows[P - 2 * TILES : P - TILES, :], qpos.rearrange("b (h p) o -> (b h) (p o)", p=P))
-        nc.gpsimd.dma_start(rows[P - TILES :, :], sink.rearrange("b (h p) o -> (b h) (p o)", p=P))
-        nc.vector.memset(vs_pool[: P - 1, : T // 2], 0.0)
-        nc.gpsimd.memset(vs_pool[: P - 1, T // 2 :], 0.0)
 
         nc.sync.dma_start(offsets[:], offs)
         nc.sync.dma_start(pos_pool[P - 1 :, :], pos[P - 1 :, :])
@@ -86,6 +81,8 @@ def tile_attend_soft_draft_sink_pgb2q256n512t2048_kernel(
         for g in range(4):
             nc.sync.dma_start(ks_pool[32 * g : 32 * g + 4, :].bitcast(I32), k_scales[0, 4 * g : 4 * g + 4, :].bitcast(I32))
         nc.sync.dma_start(kw_pool[:], k_words[0].rearrange("p t r -> p (t r)").bitcast(I32))
+        nc.sync.dma_start(rows[P - 2 * TILES : P - TILES, :], qpos.rearrange("b (h p) o -> (b h) (p o)", p=P))
+        nc.sync.dma_start(rows[P - TILES :, :], sink.rearrange("b (h p) o -> (b h) (p o)", p=P))
         nc.sync.dma_start(qw[:], q_words.rearrange("b o p q r -> p (b o) (q r)").bitcast(I32))
         for g in range(4):
             nc.sync.dma_start(
@@ -103,18 +100,18 @@ def tile_attend_soft_draft_sink_pgb2q256n512t2048_kernel(
             nc.vector.tensor_copy(kw[b][:], kw_pool[:].bitcast(U32).indirect(lists[b]))
 
         pg = [work.tile([P, N], F32, name=f"pg{b}") for b in range(B)]
-        upright = [banks.tile([P, (3 - b) * CHUNKS, P], F32, name=f"upright{b}", offset=BANK * (2 - 2 * b)) for b in range(B)]
+        upright = [banks.tile([P, CHUNKS, P], F32, name=f"upright{b}", offset=BANK * (2 + b)) for b in range(B)]
         for b in range(B):
             nc.scalar.activation(pg[b][:], pos_pool[:].indirect(lists[b]), ACT.Copy)
             for c in range(CHUNKS):
                 nc.tensor.transpose(upright[b][:, c, :], pg[b][:, c * P : (c + 1) * P], ident[:])
 
-        columns = [shared.tile([P, CHUNKS], F32, name="columns0", offset=AT_SG1), work.tile([P, CHUNKS], F32, name="columns1")]
+        columns = [work.tile([P, CHUNKS], F32, name=f"columns{b}") for b in range(B)]
         place_rows = [work.tile([P, N], F32, name=f"place_rows{b}") for b in range(B)]
         scale_cols = [work.tile([P, PLACES], F32, name=f"scale_cols{b}") for b in range(B)]
 
         def spread(b):
-            place_spread = banks.tile([P, N], F32, name=f"place_spread{b}", offset=BANK * (5 - b))
+            place_spread = banks.tile([P, N], F32, name=f"place_spread{b}", offset=BANK * (4 + b))
             for c in range(CHUNKS):
                 nc.tensor.transpose(place_spread[:, c * P : (c + 1) * P], columns[b][:, c : c + 1].to_broadcast([P, P]), ident[:])
             nc.scalar.copy(place_rows[b][:], place_spread[:])
@@ -123,21 +120,19 @@ def tile_attend_soft_draft_sink_pgb2q256n512t2048_kernel(
             nc.scalar.activation(sg[:], vs_pool[:].indirect(lists[b]), ACT.Copy)
             nc.sync.dma_start(scale_cols[b][:], sg[P - 1 :, :])
 
-        nc.scalar.activation(columns[0][:], upright[0][:, :CHUNKS, P - 1], ACT.Copy, scale=-BIG)
+        nc.scalar.activation(columns[0][:], upright[0][:, :, P - 1], ACT.Copy, bias=MARGIN, scale=-BIG)
         scales_of(0, work.tile([P, N], F32, name="sg0"))
-        nc.scalar.activation(columns[1][:], upright[1][:, :CHUNKS, P - 1], ACT.Copy, scale=-BIG)
+        nc.scalar.activation(columns[1][:], upright[1][:, :, P - 1], ACT.Copy, bias=MARGIN, scale=-BIG)
         spread(0)
 
-        cols = banks.tile([P, 3 * CHUNKS, P], F32, name="cols", offset=BANK * 2)
-        nc.tensor.transpose(cols[:, 0, :], rows[:], ident[:])
-        qpos_cols, sink_cols = cols[:, 0, P - 2 * TILES : P - TILES], cols[:, 0, P - TILES :]
+        cols = banks.tile([P, P], F32, name="cols", offset=BANK * 2)
+        nc.tensor.transpose(cols[:], rows[:], ident[:])
+        qpos_cols, sink_cols = cols[:, P - 2 * TILES : P - TILES], cols[:, P - TILES :]
         step = work.tile([P, TILES], F32, name="step")
-        base = work.tile([P, TILES], F32, name="base")
-        limit = work.tile([P, TILES], F32, name="limit")
+        limit = shared.tile([P, TILES], F32, name="limit", offset=AT_KEYS)
         nc.scalar.activation(step[:], qpos_cols, ACT.Abs, scale=BIG * HALF_STEP)
-        nc.scalar.activation(base[:], qpos_cols, ACT.Copy, bias=MARGIN, scale=BIG)
-        nc.gpsimd.tensor_tensor(limit[:], base[:], step[:], ALU.add)
         nc.scalar.activation(xs[:, :, N], sink_cols, ACT.Copy)
+        nc.vector.scalar_tensor_tensor(limit[:], qpos_cols, BIG, step[:], ALU.mult, ALU.add)
 
         scores = []
 
@@ -156,8 +151,8 @@ def tile_attend_soft_draft_sink_pgb2q256n512t2048_kernel(
 
         score(0)
         score(1)
-        scales_of(1, shared.tile([P, N], F32, name="sg1", offset=AT_SG1))
         spread(1)
+        scales_of(1, shared.tile([P, N], F32, name="sg1", offset=AT_SG1))
         score(2)
         score(3)
 

@@ -93,21 +93,24 @@ def tile_attend_soft_draft_sink_pgb2q256n512t2048_kernel(
 
         lists = [offsets[:, b * N // 16 : (b + 1) * N // 16] for b in range(B)]
 
+        pg = [work.tile([P, N], F32, name=f"pg{b}") for b in range(B)]
+        upright = [banks.tile([P, CHUNKS, P], F32, name=f"upright{b}", offset=BANK * (2 + b)) for b in range(B)]
+        for b in range(B):
+            if b == 0:
+                nc.scalar.activation(pg[b][:], pos_pool[:].indirect(lists[b]), ACT.Copy)
+            else:
+                nc.vector.tensor_copy(pg[b][:], pos_pool[:].indirect(lists[b]))
+            for c in range(CHUNKS):
+                nc.tensor.transpose(upright[b][:, c, :], pg[b][:, c * P : (c + 1) * P], ident[:])
+
         ks = work.tile([P, B * N], U8, name="ks", align_bytes=64)
         kw = [work.tile([P, N], U32, name=f"kw{b}", align_bytes=64) for b in range(B)]
         nc.vector.tensor_copy(ks[:], ks_pool[:].indirect(offsets[:]))
         for b in range(B):
             nc.vector.tensor_copy(kw[b][:], kw_pool[:].bitcast(U32).indirect(lists[b]))
 
-        pg = [work.tile([P, N], F32, name=f"pg{b}") for b in range(B)]
-        upright = [banks.tile([P, CHUNKS, P], F32, name=f"upright{b}", offset=BANK * (2 + b)) for b in range(B)]
-        for b in range(B):
-            nc.scalar.activation(pg[b][:], pos_pool[:].indirect(lists[b]), ACT.Copy)
-            for c in range(CHUNKS):
-                nc.tensor.transpose(upright[b][:, c, :], pg[b][:, c * P : (c + 1) * P], ident[:])
-
         columns = [work.tile([P, CHUNKS], F32, name=f"columns{b}") for b in range(B)]
-        place_rows = [work.tile([P, N], F32, name=f"place_rows{b}") for b in range(B)]
+        place_rows = [work.tile([P, N], F32, name="place_rows0"), shared.tile([P, N], F32, name="place_rows1", offset=AT_SG1)]
         scale_cols = [work.tile([P, PLACES], F32, name=f"scale_cols{b}") for b in range(B)]
 
         def spread(b):
@@ -120,9 +123,10 @@ def tile_attend_soft_draft_sink_pgb2q256n512t2048_kernel(
             nc.scalar.activation(sg[:], vs_pool[:].indirect(lists[b]), ACT.Copy)
             nc.sync.dma_start(scale_cols[b][:], sg[P - 1 :, :])
 
-        nc.scalar.activation(columns[0][:], upright[0][:, :, P - 1], ACT.Copy, bias=MARGIN, scale=-BIG)
         scales_of(0, work.tile([P, N], F32, name="sg0"))
-        nc.scalar.activation(columns[1][:], upright[1][:, :, P - 1], ACT.Copy, bias=MARGIN, scale=-BIG)
+        for b in range(B):
+            nc.scalar.activation(columns[b][:], upright[b][:, :, P - 1], ACT.Copy, bias=MARGIN, scale=-BIG)
+        scales_of(1, work.tile([P, N], F32, name="sg1"))
         spread(0)
 
         cols = banks.tile([P, P], F32, name="cols", offset=BANK * 2)
@@ -152,7 +156,6 @@ def tile_attend_soft_draft_sink_pgb2q256n512t2048_kernel(
         score(0)
         score(1)
         spread(1)
-        scales_of(1, shared.tile([P, N], F32, name="sg1", offset=AT_SG1))
         score(2)
         score(3)
 

@@ -46,7 +46,7 @@ def tile_attend_soft_draft_sink_pgb2q256n512t2048_kernel(
 
         KB = 1024
         BANK = 2 * KB
-        AT_KEYS, AT_SG1, AT_P = 0, 8 * KB, 10 * KB
+        AT_KEYS, AT_PLACES, AT_SG0, AT_SG1, AT_P = 0, 8 * KB, 12 * KB, 10 * KB, 14 * KB
         P_BYTES = 4 * PLACES * RUN
 
         offsets = held.tile([P, B * N // 16], U16, name="offsets")
@@ -70,8 +70,8 @@ def tile_attend_soft_draft_sink_pgb2q256n512t2048_kernel(
         kw_pool = shared.tile([P, T], I32, name="kw_pool", offset=AT_KEYS)
         qw = work.tile([P, B, NQ], I32, name="qw", align_bytes=64)
         qs = work.tile([P, B * NQ], U8, name="qs", align_bytes=64)
-        rows = shared.tile([P, P], F32, name="rows", offset=AT_SG1)
-        v_pool = held.tile([P, T], F32, name="v_pool")
+        rows = shared.tile([P, P], F32, name="rows", offset=AT_SG1 - KB // 4)
+        v_raw = [work.tile([P, T // 2], F32, name=f"v_raw{h}") for h in range(2)]
         nc.gpsimd.memset(qs[:].bitcast(I32), 0)
         nc.gpsimd.memset(rows[: P - 2 * TILES, :], 0.0)
 
@@ -89,17 +89,15 @@ def tile_attend_soft_draft_sink_pgb2q256n512t2048_kernel(
                 qs[32 * g : 32 * g + 4, :].bitcast(I32).rearrange("f (b q) -> f b q", b=B),
                 q_scales[:, 0, 4 * g : 4 * g + 4, :].rearrange("b f q -> f b q").bitcast(I32),
             )
-        nc.sync.dma_start(v_pool[:], vT)
+        for h in range(2):
+            nc.sync.dma_start(v_raw[h][:], vT[:, h * T // 2 : (h + 1) * T // 2])
 
         lists = [offsets[:, b * N // 16 : (b + 1) * N // 16] for b in range(B)]
 
-        pg = [work.tile([P, N], F32, name=f"pg{b}") for b in range(B)]
+        pg = [shared.tile([P, N], F32, name="pg0", offset=AT_SG0), work.tile([P, N], F32, name="pg1")]
         upright = [banks.tile([P, CHUNKS, P], F32, name=f"upright{b}", offset=BANK * (2 + b)) for b in range(B)]
         for b in range(B):
-            if b == 0:
-                nc.scalar.activation(pg[b][:], pos_pool[:].indirect(lists[b]), ACT.Copy)
-            else:
-                nc.vector.tensor_copy(pg[b][:], pos_pool[:].indirect(lists[b]))
+            nc.scalar.activation(pg[b][:], pos_pool[:].indirect(lists[b]), ACT.Copy)
             for c in range(CHUNKS):
                 nc.tensor.transpose(upright[b][:, c, :], pg[b][:, c * P : (c + 1) * P], ident[:])
 
@@ -109,8 +107,12 @@ def tile_attend_soft_draft_sink_pgb2q256n512t2048_kernel(
         for b in range(B):
             nc.vector.tensor_copy(kw[b][:], kw_pool[:].bitcast(U32).indirect(lists[b]))
 
+        v_pool = shared.tile([P, T], BF16, name="v_pool", offset=AT_KEYS + 4 * KB)
+        for h in range(2):
+            nc.gpsimd.tensor_copy(v_pool[:, h * T // 2 : (h + 1) * T // 2], v_raw[h][:])
+
         columns = [work.tile([P, CHUNKS], F32, name=f"columns{b}") for b in range(B)]
-        place_rows = [work.tile([P, N], F32, name="place_rows0"), shared.tile([P, N], F32, name="place_rows1", offset=AT_SG1)]
+        place_rows = [work.tile([P, N], F32, name="place_rows0"), shared.tile([P, N], F32, name="place_rows1", offset=AT_PLACES)]
         scale_cols = [work.tile([P, PLACES], F32, name=f"scale_cols{b}") for b in range(B)]
 
         def spread(b):
@@ -123,10 +125,9 @@ def tile_attend_soft_draft_sink_pgb2q256n512t2048_kernel(
             nc.scalar.activation(sg[:], vs_pool[:].indirect(lists[b]), ACT.Copy)
             nc.sync.dma_start(scale_cols[b][:], sg[P - 1 :, :])
 
-        scales_of(0, work.tile([P, N], F32, name="sg0"))
-        for b in range(B):
-            nc.scalar.activation(columns[b][:], upright[b][:, :, P - 1], ACT.Copy, bias=MARGIN, scale=-BIG)
-        scales_of(1, work.tile([P, N], F32, name="sg1"))
+        nc.scalar.activation(columns[0][:], upright[0][:, :, P - 1], ACT.Copy, bias=MARGIN, scale=-BIG)
+        scales_of(0, shared.tile([P, N], F32, name="sg0", offset=AT_SG0))
+        nc.scalar.activation(columns[1][:], upright[1][:, :, P - 1], ACT.Copy, bias=MARGIN, scale=-BIG)
         spread(0)
 
         cols = banks.tile([P, P], F32, name="cols", offset=BANK * 2)
@@ -156,6 +157,7 @@ def tile_attend_soft_draft_sink_pgb2q256n512t2048_kernel(
         score(0)
         score(1)
         spread(1)
+        scales_of(1, shared.tile([P, N], F32, name="sg1", offset=AT_SG1))
         score(2)
         score(3)
 
@@ -169,8 +171,8 @@ def tile_attend_soft_draft_sink_pgb2q256n512t2048_kernel(
                 nc.vector.tensor_reduce(minus_m[:, j : j + 1], xs[:, j, : N + 1], AXIS.X, ALU.max, negate=True)
 
         v_turned = []
-        for b in range(B):
-            vg = shared.tile([P, N], BF16, name=f"vg{b}", offset=AT_P + (2 * b + 1) * P_BYTES - KB // 2)
+        vgs = [shared.tile([P, N], BF16, name="vg0", offset=AT_P + 3 * P_BYTES - KB // 2), work.tile([P, N], BF16, name="vg1")]
+        for b, vg in enumerate(vgs):
             nc.scalar.activation(vg[:], v_pool[:].indirect(lists[b]), ACT.Copy)
             v_turned.append(banks.tile([P, 2, P], F32, name=f"v_turned{b}", offset=BANK * b))
             words = vg[:].bitcast(F32)
@@ -210,7 +212,8 @@ def tile_attend_soft_draft_sink_pgb2q256n512t2048_kernel(
         quantise(nc, w_woven[0][:], wq[0][:], wsc[0][:])
         nc.vector.reciprocal(inv[:], total[:])
         quantise(nc, v_woven[:].bitcast(BF16), vq[:], vsc[:])
-        quantise(nc, w_woven[1][:], wq[1][:], wsc[1][:])
+        for h in range(QT):
+            quantise(nc, w_woven[1][:, h * N : (h + 1) * N], wq[1][:, h * P : (h + 1) * P], wsc[1][:, h * P : (h + 1) * P])
 
         for j in range(TILES):
             b, h = divmod(j, QT)

@@ -60,7 +60,6 @@ def tile_attend_soft_draft_sink_pgb2q256n512t2048_kernel(
         nc.vector.memset(filler[:], FILLER)
         nc.scalar.copy(xs[:, :, N:], filler[:].unsqueeze(1).to_broadcast([P, TILES, PLACES]))
         nc.vector.memset(pos_pool[: P - 1, :], 0.0)
-        nc.vector.memset(vs_pool[: P - 1, :], 0.0)
         zeros = work.tile([P, P], F32, name="zeros")
         nc.gpsimd.memset(ks_pool[:].bitcast(I32), 0)
         nc.gpsimd.memset(zeros[:], 0.0)
@@ -71,9 +70,10 @@ def tile_attend_soft_draft_sink_pgb2q256n512t2048_kernel(
         qw = work.tile([P, B, NQ], I32, name="qw", align_bytes=64)
         qs = work.tile([P, B * NQ], U8, name="qs", align_bytes=64)
         rows = shared.tile([P, P], F32, name="rows", offset=AT_SG1 - KB // 4)
-        v_raw = [work.tile([P, T // 2], F32, name=f"v_raw{h}") for h in range(2)]
+        v_raw = [work.tile([P, T // 2], F32, name="v_raw0"), shared.tile([P, T // 2], F32, name="v_raw1", offset=AT_P + QT * P_BYTES)]
         nc.gpsimd.memset(qs[:].bitcast(I32), 0)
         nc.gpsimd.memset(rows[: P - 2 * TILES, :], 0.0)
+        nc.gpsimd.memset(vs_pool[: P - 1, :], 0.0)
 
         nc.sync.dma_start(offsets[:], offs)
         nc.sync.dma_start(pos_pool[P - 1 :, :], pos[P - 1 :, :])
@@ -170,14 +170,15 @@ def tile_attend_soft_draft_sink_pgb2q256n512t2048_kernel(
             for j in range(QT * b, QT * (b + 1)):
                 nc.vector.tensor_reduce(minus_m[:, j : j + 1], xs[:, j, : N + 1], AXIS.X, ALU.max, negate=True)
 
-        v_turned = []
-        vgs = [shared.tile([P, N], BF16, name="vg0", offset=AT_P + 3 * P_BYTES - KB // 2), work.tile([P, N], BF16, name="vg1")]
-        for b, vg in enumerate(vgs):
+        def values_of(b, vg):
             nc.scalar.activation(vg[:], v_pool[:].indirect(lists[b]), ACT.Copy)
-            v_turned.append(banks.tile([P, 2, P], F32, name=f"v_turned{b}", offset=BANK * b))
+            turned = banks.tile([P, 2, P], F32, name=f"v_turned{b}", offset=BANK * b)
             words = vg[:].bitcast(F32)
             for u in range(2):
-                nc.tensor.transpose(v_turned[b][:, u, :], words[:, u:WORDS:2], ident[:])
+                nc.tensor.transpose(turned[:, u, :], words[:, u:WORDS:2], ident[:])
+            return turned
+
+        v_turned = [values_of(0, work.tile([P, N], BF16, name="vg0"))]
 
         w_woven = [work.tile([P, QT * N], BF16, name=f"w_woven{b}", align_bytes=64) for b in range(B)]
         for j in range(TILES):
@@ -200,6 +201,7 @@ def tile_attend_soft_draft_sink_pgb2q256n512t2048_kernel(
                 ALU.mult,
             )
 
+        v_turned.append(values_of(1, shared.tile([P, N], BF16, name="vg1", offset=AT_P + QT * P_BYTES)))
         v_woven = work.tile([P, B * WORDS], F32, name="v_woven", align_bytes=64)
         for b in range(B):
             nc.scalar.copy(
@@ -211,9 +213,9 @@ def tile_attend_soft_draft_sink_pgb2q256n512t2048_kernel(
         vsc = work.tile([P, B * DV], U8, name="vsc", align_bytes=64)
         quantise(nc, w_woven[0][:], wq[0][:], wsc[0][:])
         nc.vector.reciprocal(inv[:], total[:])
-        quantise(nc, v_woven[:].bitcast(BF16), vq[:], vsc[:])
-        for h in range(QT):
-            quantise(nc, w_woven[1][:, h * N : (h + 1) * N], wq[1][:, h * P : (h + 1) * P], wsc[1][:, h * P : (h + 1) * P])
+        quantise(nc, v_woven[:, :WORDS].bitcast(BF16), vq[:, :DV], vsc[:, :DV])
+        quantise(nc, w_woven[1][:], wq[1][:], wsc[1][:])
+        quantise(nc, v_woven[:, WORDS:].bitcast(BF16), vq[:, DV:], vsc[:, DV:])
 
         for j in range(TILES):
             b, h = divmod(j, QT)

@@ -10,7 +10,6 @@ CHUNKS = N // P
 PLACES = 4
 WORDS = N // 2
 XW = N + PLACES
-RUN = P + PLACES
 FLOPS = 2 * B * NQ * N * (D + DV)
 
 F32 = mybir.dt.float32
@@ -27,7 +26,6 @@ AXIS = mybir.AxisListType
 BIG = 2.0 ** 80
 HALF_STEP = 2.0 ** -24 + 2.0 ** -34
 MARGIN = 2.0 ** 50
-FILLER = -(2.0 ** 100)
 
 
 def quantise(nc, woven, codes, scales):
@@ -47,7 +45,7 @@ def tile_attend_soft_draft_sink_pgb2q256n512t2048_kernel(
         KB = 1024
         BANK = 2 * KB
         AT_KEYS, AT_PLACES, AT_SG0, AT_SG1, AT_P = 0, 8 * KB, 12 * KB, 10 * KB, 14 * KB
-        P_BYTES = 4 * PLACES * RUN
+        P_BYTES = 4 * (N + 8)
 
         offsets = held.tile([P, B * N // 16], U16, name="offsets")
         ks_pool = held.tile([P, T], U8, name="ks_pool", align_bytes=64)
@@ -56,13 +54,10 @@ def tile_attend_soft_draft_sink_pgb2q256n512t2048_kernel(
         xs = held.tile([P, TILES, XW], F32, name="xs")
 
         vs_pool = held.tile([P, T], F32, name="vs_pool")
-        filler = work.tile([P, PLACES], F32, name="filler")
-        nc.vector.memset(filler[:], FILLER)
-        nc.scalar.copy(xs[:, :, N:], filler[:].unsqueeze(1).to_broadcast([P, TILES, PLACES]))
-        nc.vector.memset(pos_pool[: P - 1, :], 0.0)
         zeros = work.tile([P, P], F32, name="zeros")
+        nc.vector.memset(zeros[:], 0.0)
+        nc.vector.memset(pos_pool[: P - 1, :], 0.0)
         nc.gpsimd.memset(ks_pool[:].bitcast(I32), 0)
-        nc.gpsimd.memset(zeros[:], 0.0)
         nc.gpsimd.affine_select(
             out=ident[:], in_=zeros[:], compare_op=ALU.not_equal, fill=1.0, base=0, pattern=[[-1, P]], channel_multiplier=1
         )
@@ -70,27 +65,29 @@ def tile_attend_soft_draft_sink_pgb2q256n512t2048_kernel(
         qw = work.tile([P, B, NQ], I32, name="qw", align_bytes=64)
         qs = work.tile([P, B * NQ], U8, name="qs", align_bytes=64)
         rows = shared.tile([P, P], F32, name="rows", offset=AT_SG1 - KB // 4)
+        sink_cols = shared.tile([P, TILES], F32, name="sink_cols", offset=AT_PLACES)
         v_raw = [work.tile([P, T // 2], F32, name="v_raw0"), shared.tile([P, T // 2], F32, name="v_raw1", offset=AT_P + QT * P_BYTES)]
         nc.gpsimd.memset(qs[:].bitcast(I32), 0)
-        nc.gpsimd.memset(rows[: P - 2 * TILES, :], 0.0)
+        nc.scalar.copy(rows[: P - TILES, :], zeros[: P - TILES, :])
         nc.gpsimd.memset(vs_pool[: P - 1, :], 0.0)
 
         nc.sync.dma_start(offsets[:], offs)
         nc.sync.dma_start(pos_pool[P - 1 :, :], pos[P - 1 :, :])
         nc.sync.dma_start(vs_pool[P - 1 :, :], vs[P - 1 :, :])
-        for g in range(4):
-            nc.sync.dma_start(ks_pool[32 * g : 32 * g + 4, :].bitcast(I32), k_scales[0, 4 * g : 4 * g + 4, :].bitcast(I32))
+        for r in range(4):
+            nc.sync.dma_start(ks_pool[r:P:32, :].bitcast(I32), k_scales[0, r:16:4, :].bitcast(I32))
         nc.sync.dma_start(kw_pool[:], k_words[0].rearrange("p t r -> p (t r)").bitcast(I32))
-        nc.sync.dma_start(rows[P - 2 * TILES : P - TILES, :], qpos.rearrange("b (h p) o -> (b h) (p o)", p=P))
-        nc.sync.dma_start(rows[P - TILES :, :], sink.rearrange("b (h p) o -> (b h) (p o)", p=P))
+        nc.sync.dma_start(rows[P - TILES :, :], qpos.rearrange("b (h p) o -> (b h) (p o)", p=P))
         nc.sync.dma_start(qw[:], q_words.rearrange("b o p q r -> p (b o) (q r)").bitcast(I32))
-        for g in range(4):
+        for r in range(4):
             nc.sync.dma_start(
-                qs[32 * g : 32 * g + 4, :].bitcast(I32).rearrange("f (b q) -> f b q", b=B),
-                q_scales[:, 0, 4 * g : 4 * g + 4, :].rearrange("b f q -> f b q").bitcast(I32),
+                qs[r:P:32, :].bitcast(I32).rearrange("f (b q) -> f b q", b=B),
+                q_scales[:, 0, r:16:4, :].rearrange("b f q -> f b q").bitcast(I32),
             )
-        for h in range(2):
-            nc.sync.dma_start(v_raw[h][:], vT[:, h * T // 2 : (h + 1) * T // 2])
+        nc.sync.dma_start(v_raw[0][:], vT[:, : T // 2])
+        with nc.allow_non_contiguous_dma(reason="one sink a query row, to that row's partition"):
+            nc.sync.dma_start(sink_cols[:], sink.rearrange("b (h p) o -> p (b h o)", p=P))
+        nc.sync.dma_start(v_raw[1][:], vT[:, T // 2 :])
 
         lists = [offsets[:, b * N // 16 : (b + 1) * N // 16] for b in range(B)]
 
@@ -119,7 +116,7 @@ def tile_attend_soft_draft_sink_pgb2q256n512t2048_kernel(
             place_spread = banks.tile([P, N], F32, name=f"place_spread{b}", offset=BANK * (4 + b))
             for c in range(CHUNKS):
                 nc.tensor.transpose(place_spread[:, c * P : (c + 1) * P], columns[b][:, c : c + 1].to_broadcast([P, P]), ident[:])
-            nc.scalar.copy(place_rows[b][:], place_spread[:])
+            nc.scalar.copy(place_rows[b][:].rearrange("q (t c) -> q t c", t=PLACES), place_spread[:].rearrange("q (c t) -> q t c", t=PLACES))
 
         def scales_of(b, sg):
             nc.scalar.activation(sg[:], vs_pool[:].indirect(lists[b]), ACT.Copy)
@@ -132,11 +129,10 @@ def tile_attend_soft_draft_sink_pgb2q256n512t2048_kernel(
 
         cols = banks.tile([P, P], F32, name="cols", offset=BANK * 2)
         nc.tensor.transpose(cols[:], rows[:], ident[:])
-        qpos_cols, sink_cols = cols[:, P - 2 * TILES : P - TILES], cols[:, P - TILES :]
+        qpos_cols = cols[:, P - TILES :]
         step = work.tile([P, TILES], F32, name="step")
         limit = shared.tile([P, TILES], F32, name="limit", offset=AT_KEYS)
         nc.scalar.activation(step[:], qpos_cols, ACT.Abs, scale=BIG * HALF_STEP)
-        nc.scalar.activation(xs[:, :, N], sink_cols, ACT.Copy)
         nc.vector.scalar_tensor_tensor(limit[:], qpos_cols, BIG, step[:], ALU.mult, ALU.add)
 
         scores = []
@@ -156,8 +152,9 @@ def tile_attend_soft_draft_sink_pgb2q256n512t2048_kernel(
 
         score(0)
         score(1)
-        spread(1)
         scales_of(1, shared.tile([P, N], F32, name="sg1", offset=AT_SG1))
+        nc.scalar.copy(xs[:, :, N], sink_cols[:])
+        spread(1)
         score(2)
         score(3)
 
@@ -166,7 +163,14 @@ def tile_attend_soft_draft_sink_pgb2q256n512t2048_kernel(
         inv = held.tile([P, TILES], F32, name="inv")
         for b in range(B):
             for j in range(QT * b, QT * (b + 1)):
-                nc.vector.scalar_tensor_tensor(xs[:, j, :N], place_rows[b][:], limit[:, j : j + 1], scores[j][:], ALU.add, ALU.min)
+                nc.vector.scalar_tensor_tensor(
+                    xs[:, j, :N].rearrange("q (t c) -> q t c", t=PLACES),
+                    place_rows[b][:].rearrange("q (t c) -> q t c", t=PLACES),
+                    limit[:, j : j + 1],
+                    scores[j][:].rearrange("q (c t) -> q t c", t=PLACES),
+                    ALU.add,
+                    ALU.min,
+                )
             for j in range(QT * b, QT * (b + 1)):
                 nc.vector.tensor_reduce(minus_m[:, j : j + 1], xs[:, j, : N + 1], AXIS.X, ALU.max, negate=True)
 
@@ -183,17 +187,11 @@ def tile_attend_soft_draft_sink_pgb2q256n512t2048_kernel(
         w_woven = [work.tile([P, QT * N], BF16, name=f"w_woven{b}", align_bytes=64) for b in range(B)]
         for j in range(TILES):
             b, h = divmod(j, QT)
-            p = shared.tile([P, PLACES, RUN], F32, name=f"p{j}", offset=AT_P + j * P_BYTES)
-            nc.scalar.activation(
-                p[:, :, : XW // PLACES].rearrange("q t c -> q c t"),
-                xs[:, j, :].rearrange("q (c t) -> q c t", t=PLACES),
-                ACT.Exp,
-                bias=minus_m[:, j : j + 1],
-                accum_out=total[:, j : j + 1],
-            )
+            p = shared.tile([P, N + 8], F32, name=f"p{j}", offset=AT_P + j * P_BYTES)
+            nc.scalar.activation(p[:, : N + 1], xs[:, j, : N + 1], ACT.Exp, bias=minus_m[:, j : j + 1], accum_out=total[:, j : j + 1])
             p_turned = banks.tile([P, PLACES, P], F32, name=f"p_turned{j}", offset=BANK * (4 + j))
             for t in range(PLACES):
-                nc.tensor.transpose(p_turned[:, t, :], p[:, t, :P], ident[:])
+                nc.tensor.transpose(p_turned[:, t, :], p[:, t * P : (t + 1) * P], ident[:])
             nc.vector.tensor_tensor(
                 w_woven[b][:, h * N : (h + 1) * N].rearrange("p (q t) -> p q t", t=PLACES),
                 p_turned[:].rearrange("p t q -> p q t"),

@@ -44,7 +44,7 @@ def tile_attend_soft_draft_sink_pgb2q256n512t2048_kernel(
 
         KB = 1024
         BANK = 2 * KB
-        AT_KEYS, AT_PLACES, AT_SG0, AT_SG1, AT_P = 0, 8 * KB, 12 * KB, 10 * KB, 14 * KB
+        AT_KEYS, AT_PLACES, AT_SG1, AT_P = 0, 8 * KB, 10 * KB, 12 * KB
         P_BYTES = 4 * (N + 8)
 
         offsets = held.tile([P, B * N // 16], U16, name="offsets")
@@ -64,11 +64,12 @@ def tile_attend_soft_draft_sink_pgb2q256n512t2048_kernel(
         kw_pool = shared.tile([P, T], I32, name="kw_pool", offset=AT_KEYS)
         qw = work.tile([P, B, NQ], I32, name="qw", align_bytes=64)
         qs = work.tile([P, B * NQ], U8, name="qs", align_bytes=64)
-        rows = shared.tile([P, P], F32, name="rows", offset=AT_SG1 - KB // 4)
+        qpos_cols = shared.tile([P, TILES], F32, name="qpos_cols", offset=AT_SG1)
         sink_cols = shared.tile([P, TILES], F32, name="sink_cols", offset=AT_PLACES)
         v_raw = [work.tile([P, T // 2], F32, name="v_raw0"), shared.tile([P, T // 2], F32, name="v_raw1", offset=AT_P + QT * P_BYTES)]
         nc.gpsimd.memset(qs[:].bitcast(I32), 0)
-        nc.scalar.copy(rows[: P - TILES, :], zeros[: P - TILES, :])
+        margin = work.tile([P, 1], F32, name="margin")
+        nc.scalar.activation(margin[:], zeros[:, :1], ACT.Copy, bias=MARGIN)
         nc.gpsimd.memset(vs_pool[: P - 1, :], 0.0)
 
         nc.sync.dma_start(offsets[:], offs)
@@ -77,13 +78,14 @@ def tile_attend_soft_draft_sink_pgb2q256n512t2048_kernel(
         for r in range(4):
             nc.sync.dma_start(ks_pool[r:P:32, :].bitcast(I32), k_scales[0, r:16:4, :].bitcast(I32))
         nc.sync.dma_start(kw_pool[:], k_words[0].rearrange("p t r -> p (t r)").bitcast(I32))
-        nc.sync.dma_start(rows[P - TILES :, :], qpos.rearrange("b (h p) o -> (b h) (p o)", p=P))
         nc.sync.dma_start(qw[:], q_words.rearrange("b o p q r -> p (b o) (q r)").bitcast(I32))
         for r in range(4):
             nc.sync.dma_start(
                 qs[r:P:32, :].bitcast(I32).rearrange("f (b q) -> f b q", b=B),
                 q_scales[:, 0, r:16:4, :].rearrange("b f q -> f b q").bitcast(I32),
             )
+        with nc.allow_non_contiguous_dma(reason="one place a query row, to that row's partition"):
+            nc.sync.dma_start(qpos_cols[:], qpos.rearrange("b (h p) o -> p (b h o)", p=P))
         nc.sync.dma_start(v_raw[0][:], vT[:, : T // 2])
         with nc.allow_non_contiguous_dma(reason="one sink a query row, to that row's partition"):
             nc.sync.dma_start(sink_cols[:], sink.rearrange("b (h p) o -> p (b h o)", p=P))
@@ -91,10 +93,11 @@ def tile_attend_soft_draft_sink_pgb2q256n512t2048_kernel(
 
         lists = [offsets[:, b * N // 16 : (b + 1) * N // 16] for b in range(B)]
 
-        pg = [shared.tile([P, N], F32, name="pg0", offset=AT_SG0), work.tile([P, N], F32, name="pg1")]
+        pg = [work.tile([P, N], F32, name=f"pg{b}") for b in range(B)]
         upright = [banks.tile([P, CHUNKS, P], F32, name=f"upright{b}", offset=BANK * (2 + b)) for b in range(B)]
+        nc.vector.tensor_copy(pg[0][:], pos_pool[:].indirect(lists[0]))
+        nc.scalar.activation(pg[1][:], pos_pool[:].indirect(lists[1]), ACT.Copy)
         for b in range(B):
-            nc.scalar.activation(pg[b][:], pos_pool[:].indirect(lists[b]), ACT.Copy)
             for c in range(CHUNKS):
                 nc.tensor.transpose(upright[b][:, c, :], pg[b][:, c * P : (c + 1) * P], ident[:])
 
@@ -118,22 +121,23 @@ def tile_attend_soft_draft_sink_pgb2q256n512t2048_kernel(
                 nc.tensor.transpose(place_spread[:, c * P : (c + 1) * P], columns[b][:, c : c + 1].to_broadcast([P, P]), ident[:])
             nc.scalar.copy(place_rows[b][:].rearrange("q (t c) -> q t c", t=PLACES), place_spread[:].rearrange("q (c t) -> q t c", t=PLACES))
 
-        def scales_of(b, sg):
-            nc.scalar.activation(sg[:], vs_pool[:].indirect(lists[b]), ACT.Copy)
-            nc.sync.dma_start(scale_cols[b][:], sg[P - 1 :, :])
+        def scales_of(b, first, sg):
+            count = sg.shape[1]
+            at = b * N + first
+            nc.scalar.activation(sg[:], vs_pool[:].indirect(offsets[:, at // 16 : (at + count) // 16]), ACT.Copy)
+            nc.sync.dma_start(scale_cols[b][first // PLACES : (first + count) // PLACES, :], sg[P - 1 :, :])
 
-        nc.scalar.activation(columns[0][:], upright[0][:, :, P - 1], ACT.Copy, bias=MARGIN, scale=-BIG)
-        scales_of(0, shared.tile([P, N], F32, name="sg0", offset=AT_SG0))
-        nc.scalar.activation(columns[1][:], upright[1][:, :, P - 1], ACT.Copy, bias=MARGIN, scale=-BIG)
+        scales_of(0, 0, work.tile([P, N], F32, name="sg0"))
+        for b in range(B):
+            nc.scalar.activation(columns[b][:], upright[b][:, :, P - 1], ACT.Copy, scale=-BIG)
+        scales_of(1, 0, work.tile([P, N // 2], F32, name="sg1_first"))
         spread(0)
 
-        cols = banks.tile([P, P], F32, name="cols", offset=BANK * 2)
-        nc.tensor.transpose(cols[:], rows[:], ident[:])
-        qpos_cols = cols[:, P - TILES :]
         step = work.tile([P, TILES], F32, name="step")
-        limit = shared.tile([P, TILES], F32, name="limit", offset=AT_KEYS)
-        nc.scalar.activation(step[:], qpos_cols, ACT.Abs, scale=BIG * HALF_STEP)
-        nc.vector.scalar_tensor_tensor(limit[:], qpos_cols, BIG, step[:], ALU.mult, ALU.add)
+        limit = work.tile([P, TILES], F32, name="limit")
+        nc.scalar.activation(step[:], qpos_cols[:], ACT.Abs, scale=BIG * HALF_STEP, bias=margin[:])
+        for j in range(TILES):
+            nc.scalar.activation(limit[:, j : j + 1], qpos_cols[:, j : j + 1], ACT.Identity, scale=BIG, bias=step[:, j : j + 1])
 
         scores = []
 
@@ -152,7 +156,7 @@ def tile_attend_soft_draft_sink_pgb2q256n512t2048_kernel(
 
         score(0)
         score(1)
-        scales_of(1, shared.tile([P, N], F32, name="sg1", offset=AT_SG1))
+        scales_of(1, N // 2, shared.tile([P, N // 2], F32, name="sg1_second", offset=AT_SG1))
         nc.scalar.copy(xs[:, :, N], sink_cols[:])
         spread(1)
         score(2)

@@ -44,7 +44,7 @@ def tile_attend_soft_draft_sink_pgb2q256n512t2048_kernel(
 
         KB = 1024
         BANK = 2 * KB
-        AT_KEYS, AT_PLACES, AT_SG1, AT_P = 0, 8 * KB, 10 * KB, 12 * KB
+        AT_KEYS, AT_PLACES, AT_SG1, AT_STEP, AT_QPOS, AT_P = 0, 8 * KB, 10 * KB, 11 * KB, 12 * KB, 13 * KB
         P_BYTES = 4 * (N + 8)
 
         offsets = held.tile([P, B * N // 16], U16, name="offsets")
@@ -64,8 +64,8 @@ def tile_attend_soft_draft_sink_pgb2q256n512t2048_kernel(
         kw_pool = shared.tile([P, T], I32, name="kw_pool", offset=AT_KEYS)
         qw = work.tile([P, B, NQ], I32, name="qw", align_bytes=64)
         qs = work.tile([P, B * NQ], U8, name="qs", align_bytes=64)
-        qpos_cols = shared.tile([P, TILES], F32, name="qpos_cols", offset=AT_SG1)
-        sink_cols = shared.tile([P, TILES], F32, name="sink_cols", offset=AT_PLACES)
+        qpos_cols = shared.tile([P, TILES], F32, name="qpos_cols", offset=AT_QPOS)
+        sink_cols = shared.tile([P, 16], F32, name="sink_cols", offset=AT_SG1 - 32)
         v_raw = [work.tile([P, T // 2], F32, name="v_raw0"), shared.tile([P, T // 2], F32, name="v_raw1", offset=AT_P + QT * P_BYTES)]
         nc.gpsimd.memset(qs[:].bitcast(I32), 0)
         margin = work.tile([P, 1], F32, name="margin")
@@ -88,18 +88,19 @@ def tile_attend_soft_draft_sink_pgb2q256n512t2048_kernel(
             nc.sync.dma_start(qpos_cols[:], qpos.rearrange("b (h p) o -> p (b h o)", p=P))
         nc.sync.dma_start(v_raw[0][:], vT[:, : T // 2])
         with nc.allow_non_contiguous_dma(reason="one sink a query row, to that row's partition"):
-            nc.sync.dma_start(sink_cols[:], sink.rearrange("b (h p) o -> p (b h o)", p=P))
+            nc.sync.dma_start(sink_cols[:, :TILES], sink.rearrange("b (h p) o -> p (b h o)", p=P))
         nc.sync.dma_start(v_raw[1][:], vT[:, T // 2 :])
 
         lists = [offsets[:, b * N // 16 : (b + 1) * N // 16] for b in range(B)]
 
         pg = [work.tile([P, N], F32, name=f"pg{b}") for b in range(B)]
-        upright = [banks.tile([P, CHUNKS, P], F32, name=f"upright{b}", offset=BANK * (2 + b)) for b in range(B)]
-        nc.vector.tensor_copy(pg[0][:], pos_pool[:].indirect(lists[0]))
+        upright = banks.tile([P, B, CHUNKS, P], F32, name="upright", offset=BANK * 2)
+        nc.vector.tensor_copy(pg[0][:, : N // 2], pos_pool[:].indirect(offsets[:, : N // 32]))
+        nc.scalar.activation(pg[0][:, N // 2 :], pos_pool[:].indirect(offsets[:, N // 32 : N // 16]), ACT.Copy)
         nc.scalar.activation(pg[1][:], pos_pool[:].indirect(lists[1]), ACT.Copy)
         for b in range(B):
             for c in range(CHUNKS):
-                nc.tensor.transpose(upright[b][:, c, :], pg[b][:, c * P : (c + 1) * P], ident[:])
+                nc.tensor.transpose(upright[:, b, c, :], pg[b][:, c * P : (c + 1) * P], ident[:])
 
         ks = work.tile([P, B * N], U8, name="ks", align_bytes=64)
         kw = [work.tile([P, N], U32, name=f"kw{b}", align_bytes=64) for b in range(B)]
@@ -111,7 +112,7 @@ def tile_attend_soft_draft_sink_pgb2q256n512t2048_kernel(
         for h in range(2):
             nc.gpsimd.tensor_copy(v_pool[:, h * T // 2 : (h + 1) * T // 2], v_raw[h][:])
 
-        columns = [work.tile([P, CHUNKS], F32, name=f"columns{b}") for b in range(B)]
+        columns = [work.tile([P, CHUNKS], F32, name="columns0"), shared.tile([P, CHUNKS], F32, name="columns1", offset=AT_QPOS)]
         place_rows = [work.tile([P, N], F32, name="place_rows0"), shared.tile([P, N], F32, name="place_rows1", offset=AT_PLACES)]
         scale_cols = [work.tile([P, PLACES], F32, name=f"scale_cols{b}") for b in range(B)]
 
@@ -127,13 +128,11 @@ def tile_attend_soft_draft_sink_pgb2q256n512t2048_kernel(
             nc.scalar.activation(sg[:], vs_pool[:].indirect(offsets[:, at // 16 : (at + count) // 16]), ACT.Copy)
             nc.sync.dma_start(scale_cols[b][first // PLACES : (first + count) // PLACES, :], sg[P - 1 :, :])
 
+        nc.scalar.activation(columns[0][:], upright[:, 0, :, P - 1], ACT.Copy, scale=-BIG)
         scales_of(0, 0, work.tile([P, N], F32, name="sg0"))
-        for b in range(B):
-            nc.scalar.activation(columns[b][:], upright[b][:, :, P - 1], ACT.Copy, scale=-BIG)
-        scales_of(1, 0, work.tile([P, N // 2], F32, name="sg1_first"))
         spread(0)
 
-        step = work.tile([P, TILES], F32, name="step")
+        step = shared.tile([P, TILES], F32, name="step", offset=AT_STEP)
         limit = work.tile([P, TILES], F32, name="limit")
         nc.scalar.activation(step[:], qpos_cols[:], ACT.Abs, scale=BIG * HALF_STEP, bias=margin[:])
         for j in range(TILES):
@@ -156,8 +155,10 @@ def tile_attend_soft_draft_sink_pgb2q256n512t2048_kernel(
 
         score(0)
         score(1)
+        nc.scalar.activation(columns[1][:], upright[:, 1, :, P - 1], ACT.Copy, scale=-BIG)
+        scales_of(1, 0, shared.tile([P, N // 2], F32, name="sg1_first", offset=AT_STEP))
+        nc.scalar.copy(xs[:, :, N], sink_cols[:, :TILES])
         scales_of(1, N // 2, shared.tile([P, N // 2], F32, name="sg1_second", offset=AT_SG1))
-        nc.scalar.copy(xs[:, :, N], sink_cols[:])
         spread(1)
         score(2)
         score(3)

@@ -44,7 +44,7 @@ def tile_attend_soft_draft_sink_pgb2q256n512t2048_kernel(
 
         KB = 1024
         BANK = 2 * KB
-        AT_KEYS, AT_PLACES, AT_SG1, AT_STEP, AT_QPOS, AT_P = 0, 8 * KB, 10 * KB, 11 * KB, 12 * KB, 13 * KB
+        AT_KEYS, AT_PLACES, AT_SG1, AT_STEP, AT_P = 0, 8 * KB, 10 * KB, 11 * KB, 13 * KB
         P_BYTES = 4 * (N + 8)
 
         offsets = held.tile([P, B * N // 16], U16, name="offsets")
@@ -64,12 +64,10 @@ def tile_attend_soft_draft_sink_pgb2q256n512t2048_kernel(
         kw_pool = shared.tile([P, T], I32, name="kw_pool", offset=AT_KEYS)
         qw = work.tile([P, B, NQ], I32, name="qw", align_bytes=64)
         qs = work.tile([P, B * NQ], U8, name="qs", align_bytes=64)
-        qpos_cols = shared.tile([P, TILES], F32, name="qpos_cols", offset=AT_QPOS)
-        sink_cols = shared.tile([P, 16], F32, name="sink_cols", offset=AT_SG1 - 32)
+        rows = shared.tile([P, 2, P], F32, name="rows", offset=AT_SG1 - KB // 2)
         v_raw = [work.tile([P, T // 2], F32, name="v_raw0"), shared.tile([P, T // 2], F32, name="v_raw1", offset=AT_P + QT * P_BYTES)]
         nc.gpsimd.memset(qs[:].bitcast(I32), 0)
-        margin = work.tile([P, 1], F32, name="margin")
-        nc.scalar.activation(margin[:], zeros[:, :1], ACT.Copy, bias=MARGIN)
+        nc.scalar.copy(rows[: P - TILES], zeros[: P - TILES, :].unsqueeze(1).to_broadcast([P - TILES, 2, P]))
         nc.gpsimd.memset(vs_pool[: P - 1, :], 0.0)
 
         nc.sync.dma_start(offsets[:], offs)
@@ -78,29 +76,27 @@ def tile_attend_soft_draft_sink_pgb2q256n512t2048_kernel(
         for r in range(4):
             nc.sync.dma_start(ks_pool[r:P:32, :].bitcast(I32), k_scales[0, r:16:4, :].bitcast(I32))
         nc.sync.dma_start(kw_pool[:], k_words[0].rearrange("p t r -> p (t r)").bitcast(I32))
+        nc.sync.dma_start(rows[P - TILES :, 0, :], qpos.rearrange("b (h p) o -> (b h) (p o)", p=P))
         nc.sync.dma_start(qw[:], q_words.rearrange("b o p q r -> p (b o) (q r)").bitcast(I32))
         for r in range(4):
             nc.sync.dma_start(
                 qs[r:P:32, :].bitcast(I32).rearrange("f (b q) -> f b q", b=B),
                 q_scales[:, 0, r:16:4, :].rearrange("b f q -> f b q").bitcast(I32),
             )
-        with nc.allow_non_contiguous_dma(reason="one place a query row, to that row's partition"):
-            nc.sync.dma_start(qpos_cols[:], qpos.rearrange("b (h p) o -> p (b h o)", p=P))
         nc.sync.dma_start(v_raw[0][:], vT[:, : T // 2])
-        with nc.allow_non_contiguous_dma(reason="one sink a query row, to that row's partition"):
-            nc.sync.dma_start(sink_cols[:, :TILES], sink.rearrange("b (h p) o -> p (b h o)", p=P))
+        nc.sync.dma_start(rows[P - TILES :, 1, :], sink.rearrange("b (h p) o -> (b h) (p o)", p=P))
         nc.sync.dma_start(v_raw[1][:], vT[:, T // 2 :])
 
         lists = [offsets[:, b * N // 16 : (b + 1) * N // 16] for b in range(B)]
 
         pg = [work.tile([P, N], F32, name=f"pg{b}") for b in range(B)]
-        upright = banks.tile([P, B, CHUNKS, P], F32, name="upright", offset=BANK * 2)
+        upright = [banks.tile([P, CHUNKS, P], F32, name=f"upright{b}", offset=BANK * (2 + b)) for b in range(B)]
         nc.vector.tensor_copy(pg[0][:, : N // 2], pos_pool[:].indirect(offsets[:, : N // 32]))
         nc.scalar.activation(pg[0][:, N // 2 :], pos_pool[:].indirect(offsets[:, N // 32 : N // 16]), ACT.Copy)
         nc.scalar.activation(pg[1][:], pos_pool[:].indirect(lists[1]), ACT.Copy)
         for b in range(B):
             for c in range(CHUNKS):
-                nc.tensor.transpose(upright[:, b, c, :], pg[b][:, c * P : (c + 1) * P], ident[:])
+                nc.tensor.transpose(upright[b][:, c, :], pg[b][:, c * P : (c + 1) * P], ident[:])
 
         ks = work.tile([P, B * N], U8, name="ks", align_bytes=64)
         kw = [work.tile([P, N], U32, name=f"kw{b}", align_bytes=64) for b in range(B)]
@@ -112,7 +108,7 @@ def tile_attend_soft_draft_sink_pgb2q256n512t2048_kernel(
         for h in range(2):
             nc.gpsimd.tensor_copy(v_pool[:, h * T // 2 : (h + 1) * T // 2], v_raw[h][:])
 
-        columns = [work.tile([P, CHUNKS], F32, name="columns0"), shared.tile([P, CHUNKS], F32, name="columns1", offset=AT_QPOS)]
+        columns = [work.tile([P, CHUNKS], F32, name=f"columns{b}") for b in range(B)]
         place_rows = [work.tile([P, N], F32, name="place_rows0"), shared.tile([P, N], F32, name="place_rows1", offset=AT_PLACES)]
         scale_cols = [work.tile([P, PLACES], F32, name=f"scale_cols{b}") for b in range(B)]
 
@@ -122,19 +118,27 @@ def tile_attend_soft_draft_sink_pgb2q256n512t2048_kernel(
                 nc.tensor.transpose(place_spread[:, c * P : (c + 1) * P], columns[b][:, c : c + 1].to_broadcast([P, P]), ident[:])
             nc.scalar.copy(place_rows[b][:].rearrange("q (t c) -> q t c", t=PLACES), place_spread[:].rearrange("q (c t) -> q t c", t=PLACES))
 
-        def scales_of(b, first, sg):
-            count = sg.shape[1]
-            at = b * N + first
-            nc.scalar.activation(sg[:], vs_pool[:].indirect(offsets[:, at // 16 : (at + count) // 16]), ACT.Copy)
-            nc.sync.dma_start(scale_cols[b][first // PLACES : (first + count) // PLACES, :], sg[P - 1 :, :])
+        def half_scales(b, half, into):
+            at = b * N + half * N // 2
+            nc.scalar.activation(into, vs_pool[:].indirect(offsets[:, at // 16 : (at + N // 2) // 16]), ACT.Copy)
 
-        nc.scalar.activation(columns[0][:], upright[:, 0, :, P - 1], ACT.Copy, scale=-BIG)
-        scales_of(0, 0, work.tile([P, N], F32, name="sg0"))
+        def second_scales(half, sg):
+            half_scales(1, half, sg[:])
+            nc.sync.dma_start(scale_cols[1][half * P // 2 : (half + 1) * P // 2, :], sg[P - 1 :, :])
+
+        sg0 = work.tile([P, N], F32, name="sg0")
+        for b in range(B):
+            nc.scalar.activation(columns[b][:], upright[b][:, :, P - 1], ACT.Copy, bias=MARGIN, scale=-BIG)
+            half_scales(0, b, sg0[:, b * N // 2 : (b + 1) * N // 2])
+        nc.sync.dma_start(scale_cols[0][:], sg0[P - 1 :, :])
         spread(0)
+        turned_places = banks.tile([P, P], F32, name="turned_places", offset=BANK * 6)
+        nc.tensor.transpose(turned_places[:], rows[:, 0, :], ident[:])
+        qpos_cols = turned_places[:, P - TILES :]
 
         step = shared.tile([P, TILES], F32, name="step", offset=AT_STEP)
         limit = work.tile([P, TILES], F32, name="limit")
-        nc.scalar.activation(step[:], qpos_cols[:], ACT.Abs, scale=BIG * HALF_STEP, bias=margin[:])
+        nc.scalar.activation(step[:], qpos_cols, ACT.Abs, scale=BIG * HALF_STEP)
         for j in range(TILES):
             nc.scalar.activation(limit[:, j : j + 1], qpos_cols[:, j : j + 1], ACT.Identity, scale=BIG, bias=step[:, j : j + 1])
 
@@ -155,10 +159,11 @@ def tile_attend_soft_draft_sink_pgb2q256n512t2048_kernel(
 
         score(0)
         score(1)
-        nc.scalar.activation(columns[1][:], upright[:, 1, :, P - 1], ACT.Copy, scale=-BIG)
-        scales_of(1, 0, shared.tile([P, N // 2], F32, name="sg1_first", offset=AT_STEP))
-        nc.scalar.copy(xs[:, :, N], sink_cols[:, :TILES])
-        scales_of(1, N // 2, shared.tile([P, N // 2], F32, name="sg1_second", offset=AT_SG1))
+        second_scales(0, shared.tile([P, N // 2], F32, name="sg1_first", offset=AT_STEP))
+        turned_sinks = banks.tile([P, 2 * N], F32, name="turned_sinks", offset=BANK * 2)
+        nc.tensor.transpose(turned_sinks[:, :P], rows[:, 1, :], ident[:])
+        nc.scalar.copy(xs[:, :, N], turned_sinks[:, P - TILES : P])
+        second_scales(1, shared.tile([P, N // 2], F32, name="sg1_second", offset=AT_SG1))
         spread(1)
         score(2)
         score(3)

@@ -10,6 +10,7 @@ CHUNKS = N // P
 PLACES = 4
 WORDS = N // 2
 XW = N + PLACES
+HALF = N // 2
 FLOPS = 2 * B * NQ * N * (D + DV)
 
 F32 = mybir.dt.float32
@@ -72,7 +73,7 @@ def tile_attend_soft_draft_sink_pgb2q256n512t2048_kernel(
 
         nc.sync.dma_start(offsets[:], offs)
         nc.sync.dma_start(pos_pool[P - 1 :, :], pos[P - 1 :, :])
-        nc.sync.dma_start(vs_pool[P - 1 :, :], vs[P - 1 :, :])
+        nc.scalar.dma_start(vs_pool[P - 1 :, :], vs[P - 1 :, :])
         for r in range(4):
             nc.sync.dma_start(ks_pool[r:P:32, :].bitcast(I32), k_scales[0, r:16:4, :].bitcast(I32))
         nc.sync.dma_start(kw_pool[:], k_words[0].rearrange("p t r -> p (t r)").bitcast(I32))
@@ -101,8 +102,12 @@ def tile_attend_soft_draft_sink_pgb2q256n512t2048_kernel(
         ks = work.tile([P, B * N], U8, name="ks", align_bytes=64)
         kw = [work.tile([P, N], U32, name=f"kw{b}", align_bytes=64) for b in range(B)]
         nc.vector.tensor_copy(ks[:], ks_pool[:].indirect(offsets[:]))
-        for b in range(B):
-            nc.vector.tensor_copy(kw[b][:], kw_pool[:].bitcast(U32).indirect(lists[b]))
+        for half in range(2):
+            nc.vector.tensor_copy(
+                kw[0][:, half * HALF : (half + 1) * HALF],
+                kw_pool[:].bitcast(U32).indirect(offsets[:, half * HALF // 16 : (half + 1) * HALF // 16]),
+            )
+        nc.vector.tensor_copy(kw[1][:], kw_pool[:].bitcast(U32).indirect(lists[1]))
 
         v_pool = shared.tile([P, T], BF16, name="v_pool", offset=AT_KEYS + 4 * KB)
         for h in range(2):
@@ -142,31 +147,32 @@ def tile_attend_soft_draft_sink_pgb2q256n512t2048_kernel(
         for j in range(TILES):
             nc.scalar.activation(limit[:, j : j + 1], qpos_cols[:, j : j + 1], ACT.Identity, scale=BIG, bias=step[:, j : j + 1])
 
-        scores = []
+        scores = [banks.tile([P, N], F32, name=f"scores{j}", offset=BANK * j) for j in range(QT)]
 
-        def score(j):
+        def score(j, first, count):
             b, h = divmod(j, QT)
-            scores.append(banks.tile([P, N], F32, name=f"scores{j}", offset=BANK * j))
             nc.tensor.matmul_mx(
-                out=scores[j][:],
+                out=scores[j][:, first : first + count],
                 lhsT=qw[:, b, h * P : (h + 1) * P].bitcast(FP8X4),
                 lhsT_scale=qs[:, j * P : (j + 1) * P],
-                rhs=kw[b][:].bitcast(FP8X4),
-                rhs_scale=ks[:, b * N : (b + 1) * N],
+                rhs=kw[b][:, first : first + count].bitcast(FP8X4),
+                rhs_scale=ks[:, b * N + first : b * N + first + count],
                 start=True,
                 stop=True,
             )
 
-        score(0)
-        score(1)
+        for half in range(2):
+            for j in range(QT):
+                score(j, half * HALF, HALF)
         second_scales(0, shared.tile([P, N // 2], F32, name="sg1_first", offset=AT_STEP))
         turned_sinks = banks.tile([P, 2 * N], F32, name="turned_sinks", offset=BANK * 2)
         nc.tensor.transpose(turned_sinks[:, :P], rows[:, 1, :], ident[:])
         nc.scalar.copy(xs[:, :, N], turned_sinks[:, P - TILES : P])
         second_scales(1, shared.tile([P, N // 2], F32, name="sg1_second", offset=AT_SG1))
         spread(1)
-        score(2)
-        score(3)
+        for j in range(QT, TILES):
+            scores.append(banks.tile([P, N], F32, name=f"scores{j}", offset=BANK * j))
+            score(j, 0, N)
 
         minus_m = held.tile([P, TILES], F32, name="minus_m")
         total = held.tile([P, TILES], F32, name="total")
@@ -194,7 +200,9 @@ def tile_attend_soft_draft_sink_pgb2q256n512t2048_kernel(
 
         v_turned = [values_of(0, work.tile([P, N], BF16, name="vg0"))]
 
-        w_woven = [work.tile([P, QT * N], BF16, name=f"w_woven{b}", align_bytes=64) for b in range(B)]
+        w_woven = [work.tile([P, N], BF16, name=f"w_woven{j}", align_bytes=64) for j in range(TILES)]
+        wq = [work.tile([P, P], U32, name=f"wq{j}", align_bytes=64) for j in range(TILES)]
+        wsc = [work.tile([P, P], U8, name=f"wsc{j}", align_bytes=64) for j in range(TILES)]
         for j in range(TILES):
             b, h = divmod(j, QT)
             p = shared.tile([P, N + 8], F32, name=f"p{j}", offset=AT_P + j * P_BYTES)
@@ -203,11 +211,14 @@ def tile_attend_soft_draft_sink_pgb2q256n512t2048_kernel(
             for t in range(PLACES):
                 nc.tensor.transpose(p_turned[:, t, :], p[:, t * P : (t + 1) * P], ident[:])
             nc.vector.tensor_tensor(
-                w_woven[b][:, h * N : (h + 1) * N].rearrange("p (q t) -> p q t", t=PLACES),
+                w_woven[j][:].rearrange("p (q t) -> p q t", t=PLACES),
                 p_turned[:].rearrange("p t q -> p q t"),
                 scale_cols[b][:].unsqueeze(1).to_broadcast([P, P, PLACES]),
                 ALU.mult,
             )
+            if j == QT - 1:
+                for i in range(QT):
+                    quantise(nc, w_woven[i][:], wq[i][:], wsc[i][:])
 
         v_turned.append(values_of(1, shared.tile([P, N], BF16, name="vg1", offset=AT_P + QT * P_BYTES)))
         v_woven = work.tile([P, B * WORDS], F32, name="v_woven", align_bytes=64)
@@ -215,14 +226,12 @@ def tile_attend_soft_draft_sink_pgb2q256n512t2048_kernel(
             nc.scalar.copy(
                 v_woven[:, b * WORDS : (b + 1) * WORDS].rearrange("p (c u) -> p c u", u=2), v_turned[b][:].rearrange("p u c -> p c u")
             )
-        wq = [work.tile([P, NQ], U32, name=f"wq{b}", align_bytes=64) for b in range(B)]
-        wsc = [work.tile([P, NQ], U8, name=f"wsc{b}", align_bytes=64) for b in range(B)]
         vq = work.tile([P, B * DV], U32, name="vq", align_bytes=64)
         vsc = work.tile([P, B * DV], U8, name="vsc", align_bytes=64)
-        quantise(nc, w_woven[0][:], wq[0][:], wsc[0][:])
-        nc.vector.reciprocal(inv[:], total[:])
         quantise(nc, v_woven[:, :WORDS].bitcast(BF16), vq[:, :DV], vsc[:, :DV])
-        quantise(nc, w_woven[1][:], wq[1][:], wsc[1][:])
+        quantise(nc, w_woven[2][:], wq[2][:], wsc[2][:])
+        nc.vector.reciprocal(inv[:], total[:])
+        quantise(nc, w_woven[3][:], wq[3][:], wsc[3][:])
         quantise(nc, v_woven[:, WORDS:].bitcast(BF16), vq[:, DV:], vsc[:, DV:])
 
         for j in range(TILES):
@@ -230,8 +239,8 @@ def tile_attend_soft_draft_sink_pgb2q256n512t2048_kernel(
             y = banks.tile([P, DV], F32, name=f"y{j}", offset=BANK * (4 + (j + QT) % TILES))
             nc.tensor.matmul_mx(
                 out=y[:],
-                lhsT=wq[b][:, h * P : (h + 1) * P].bitcast(FP8X4),
-                lhsT_scale=wsc[b][:, h * P : (h + 1) * P],
+                lhsT=wq[j][:].bitcast(FP8X4),
+                lhsT_scale=wsc[j][:],
                 rhs=vq[:, b * DV : (b + 1) * DV].bitcast(FP8X4),
                 rhs_scale=vsc[:, b * DV : (b + 1) * DV],
                 start=True,

@@ -45,7 +45,7 @@ def tile_attend_soft_draft_sink_pgb2q256n512t2048_kernel(
 
         KB = 1024
         BANK = 2 * KB
-        AT_KEYS, AT_PLACES, AT_SG1, AT_STEP, AT_P = 0, 8 * KB, 10 * KB, 11 * KB, 13 * KB
+        AT_KEYS, AT_PLACES, AT_SG1, AT_P = 0, 8 * KB, 10 * KB, 11 * KB
         P_BYTES = 4 * (N + 8)
 
         offsets = held.tile([P, B * N // 16], U16, name="offsets")
@@ -65,15 +65,15 @@ def tile_attend_soft_draft_sink_pgb2q256n512t2048_kernel(
         kw_pool = shared.tile([P, T], I32, name="kw_pool", offset=AT_KEYS)
         qw = work.tile([P, B, NQ], I32, name="qw", align_bytes=64)
         qs = work.tile([P, B * NQ], U8, name="qs", align_bytes=64)
-        rows = shared.tile([P, 2, P], F32, name="rows", offset=AT_SG1 - KB // 2)
-        v_raw = [work.tile([P, T // 2], F32, name="v_raw0"), shared.tile([P, T // 2], F32, name="v_raw1", offset=AT_P + QT * P_BYTES)]
+        rows = work.tile([P, 2, P], F32, name="rows")
+        v_raw = [work.tile([P, T // 2], F32, name="v_raw0"), shared.tile([P, T // 2], F32, name="v_raw1", offset=AT_P)]
         nc.gpsimd.memset(qs[:].bitcast(I32), 0)
         nc.scalar.copy(rows[: P - TILES], zeros[: P - TILES, :].unsqueeze(1).to_broadcast([P - TILES, 2, P]))
         nc.gpsimd.memset(vs_pool[: P - 1, :], 0.0)
 
         nc.sync.dma_start(offsets[:], offs)
         nc.sync.dma_start(pos_pool[P - 1 :, :], pos[P - 1 :, :])
-        nc.scalar.dma_start(vs_pool[P - 1 :, :], vs[P - 1 :, :])
+        nc.sync.dma_start(vs_pool[P - 1 :, :], vs[P - 1 :, :])
         for r in range(4):
             nc.sync.dma_start(ks_pool[r:P:32, :].bitcast(I32), k_scales[0, r:16:4, :].bitcast(I32))
         nc.sync.dma_start(kw_pool[:], k_words[0].rearrange("p t r -> p (t r)").bitcast(I32))
@@ -92,8 +92,7 @@ def tile_attend_soft_draft_sink_pgb2q256n512t2048_kernel(
 
         pg = [work.tile([P, N], F32, name=f"pg{b}") for b in range(B)]
         upright = [banks.tile([P, CHUNKS, P], F32, name=f"upright{b}", offset=BANK * (2 + b)) for b in range(B)]
-        nc.vector.tensor_copy(pg[0][:, : N // 2], pos_pool[:].indirect(offsets[:, : N // 32]))
-        nc.scalar.activation(pg[0][:, N // 2 :], pos_pool[:].indirect(offsets[:, N // 32 : N // 16]), ACT.Copy)
+        nc.vector.tensor_copy(pg[0][:], pos_pool[:].indirect(lists[0]))
         nc.scalar.activation(pg[1][:], pos_pool[:].indirect(lists[1]), ACT.Copy)
         for b in range(B):
             for c in range(CHUNKS):
@@ -110,8 +109,8 @@ def tile_attend_soft_draft_sink_pgb2q256n512t2048_kernel(
         nc.vector.tensor_copy(kw[1][:], kw_pool[:].bitcast(U32).indirect(lists[1]))
 
         v_pool = shared.tile([P, T], BF16, name="v_pool", offset=AT_KEYS + 4 * KB)
-        for h in range(2):
-            nc.gpsimd.tensor_copy(v_pool[:, h * T // 2 : (h + 1) * T // 2], v_raw[h][:])
+        nc.gpsimd.tensor_copy(v_pool[:, : T // 2], v_raw[0][:])
+        nc.gpsimd.tensor_copy(v_pool[:, T // 2 : 3 * T // 4], v_raw[1][:, : T // 4])
 
         columns = [work.tile([P, CHUNKS], F32, name=f"columns{b}") for b in range(B)]
         place_rows = [work.tile([P, N], F32, name="place_rows0"), shared.tile([P, N], F32, name="place_rows1", offset=AT_PLACES)]
@@ -137,13 +136,14 @@ def tile_attend_soft_draft_sink_pgb2q256n512t2048_kernel(
             half_scales(0, b, sg0[:, b * N // 2 : (b + 1) * N // 2])
         nc.sync.dma_start(scale_cols[0][:], sg0[P - 1 :, :])
         spread(0)
+        second_scales(0, work.tile([P, N // 2], F32, name="sg1_first"))
         turned_places = banks.tile([P, P], F32, name="turned_places", offset=BANK * 6)
         nc.tensor.transpose(turned_places[:], rows[:, 0, :], ident[:])
         qpos_cols = turned_places[:, P - TILES :]
 
-        step = shared.tile([P, TILES], F32, name="step", offset=AT_STEP)
+        step = shared.tile([P, 16], F32, name="step", offset=AT_SG1 - 32)
         limit = work.tile([P, TILES], F32, name="limit")
-        nc.scalar.activation(step[:], qpos_cols, ACT.Abs, scale=BIG * HALF_STEP)
+        nc.scalar.activation(step[:, :TILES], qpos_cols, ACT.Abs, scale=BIG * HALF_STEP)
         for j in range(TILES):
             nc.scalar.activation(limit[:, j : j + 1], qpos_cols[:, j : j + 1], ACT.Identity, scale=BIG, bias=step[:, j : j + 1])
 
@@ -164,12 +164,12 @@ def tile_attend_soft_draft_sink_pgb2q256n512t2048_kernel(
         for half in range(2):
             for j in range(QT):
                 score(j, half * HALF, HALF)
-        second_scales(0, shared.tile([P, N // 2], F32, name="sg1_first", offset=AT_STEP))
+        second_scales(1, shared.tile([P, N // 2], F32, name="sg1_second", offset=AT_SG1))
+        spread(1)
         turned_sinks = banks.tile([P, 2 * N], F32, name="turned_sinks", offset=BANK * 2)
         nc.tensor.transpose(turned_sinks[:, :P], rows[:, 1, :], ident[:])
         nc.scalar.copy(xs[:, :, N], turned_sinks[:, P - TILES : P])
-        second_scales(1, shared.tile([P, N // 2], F32, name="sg1_second", offset=AT_SG1))
-        spread(1)
+        nc.scalar.copy(v_pool[:, 3 * T // 4 :], v_raw[1][:, T // 4 :])
         for j in range(QT, TILES):
             scores.append(banks.tile([P, N], F32, name=f"scores{j}", offset=BANK * j))
             score(j, 0, N)
@@ -190,21 +190,33 @@ def tile_attend_soft_draft_sink_pgb2q256n512t2048_kernel(
             for j in range(QT * b, QT * (b + 1)):
                 nc.vector.tensor_reduce(minus_m[:, j : j + 1], xs[:, j, : N + 1], AXIS.X, ALU.max, negate=True)
 
-        def values_of(b, vg):
-            nc.scalar.activation(vg[:], v_pool[:].indirect(lists[b]), ACT.Copy)
+        vg = [work.tile([P, N], BF16, name=f"vg{b}") for b in range(B)]
+
+        def half_values(b, half):
+            at = b * N + half * HALF
+            nc.scalar.activation(
+                vg[b][:, half * HALF : (half + 1) * HALF], v_pool[:].indirect(offsets[:, at // 16 : (at + HALF) // 16]), ACT.Copy
+            )
+
+        def turn_values(b):
             turned = banks.tile([P, 2, P], F32, name=f"v_turned{b}", offset=BANK * b)
-            words = vg[:].bitcast(F32)
+            words = vg[b][:].bitcast(F32)
             for u in range(2):
                 nc.tensor.transpose(turned[:, u, :], words[:, u:WORDS:2], ident[:])
             return turned
 
-        v_turned = [values_of(0, work.tile([P, N], BF16, name="vg0"))]
+        half_values(0, 0)
+        v_turned = []
 
         w_woven = [work.tile([P, N], BF16, name=f"w_woven{j}", align_bytes=64) for j in range(TILES)]
         wq = [work.tile([P, P], U32, name=f"wq{j}", align_bytes=64) for j in range(TILES)]
         wsc = [work.tile([P, P], U8, name=f"wsc{j}", align_bytes=64) for j in range(TILES)]
         for j in range(TILES):
             b, h = divmod(j, QT)
+            if j == QT:
+                half_values(0, 1)
+                v_turned.append(turn_values(0))
+                half_values(1, 0)
             p = shared.tile([P, N + 8], F32, name=f"p{j}", offset=AT_P + j * P_BYTES)
             nc.scalar.activation(p[:, : N + 1], xs[:, j, : N + 1], ACT.Exp, bias=minus_m[:, j : j + 1], accum_out=total[:, j : j + 1])
             p_turned = banks.tile([P, PLACES, P], F32, name=f"p_turned{j}", offset=BANK * (4 + j))
@@ -220,7 +232,8 @@ def tile_attend_soft_draft_sink_pgb2q256n512t2048_kernel(
                 for i in range(QT):
                     quantise(nc, w_woven[i][:], wq[i][:], wsc[i][:])
 
-        v_turned.append(values_of(1, shared.tile([P, N], BF16, name="vg1", offset=AT_P + QT * P_BYTES)))
+        half_values(1, 1)
+        v_turned.append(turn_values(1))
         v_woven = work.tile([P, B * WORDS], F32, name="v_woven", align_bytes=64)
         for b in range(B):
             nc.scalar.copy(

from contextlib import ExitStack

import concourse.mybir as mybir

B, N, T, D, DV, NQ = 2, 512, 2048, 512, 128, 256
P = 128
QT = NQ // P
TILES = B * QT
CHUNKS = N // P
PLACES = 4
WORDS = N // 2
XW = N + PLACES
HALF = N // 2
FLOPS = 2 * B * NQ * N * (D + DV)

F32 = mybir.dt.float32
BF16 = mybir.dt.bfloat16
I32 = mybir.dt.int32
U32 = mybir.dt.uint32
U16 = mybir.dt.uint16
U8 = mybir.dt.uint8
FP8X4 = mybir.dt.float8_e4m3fn_x4
ALU = mybir.AluOpType
ACT = mybir.ActivationFunctionType
AXIS = mybir.AxisListType

BIG = 2.0 ** 80
HALF_STEP = 2.0 ** -24 + 2.0 ** -34
MARGIN = 2.0 ** 50


def quantise(nc, woven, codes, scales):
    nc.vector.quantize_mx(out=codes.bitcast(FP8X4), scales=scales, in_=woven)


def tile_attend_soft_draft_sink_pgb2q256n512t2048_kernel(
    tc, q_words, q_scales, k_words, k_scales, vT, vs, pos, qpos, sink, offs, out
):
    nc = tc.nc
    with ExitStack() as ctx:
        held = ctx.enter_context(tc.tile_pool(name="held", bufs=1))
        work = ctx.enter_context(tc.tile_pool(name="work", bufs=1))
        shared = ctx.enter_context(tc.tile_pool(name="shared", bufs=1))
        banks = ctx.enter_context(tc.psum_pool(name="banks", bufs=1))

        KB = 1024
        BANK = 2 * KB
        AT_KEYS, AT_PLACES, AT_SG1, AT_P = 0, 8 * KB, 10 * KB, 11 * KB
        P_BYTES = 4 * (N + 8)

        offsets = held.tile([P, B * N // 16], U16, name="offsets")
        ks_pool = held.tile([P, T], U8, name="ks_pool", align_bytes=64)
        pos_pool = held.tile([P, T], F32, name="pos_pool")
        ident = held.tile([P, P], F32, name="ident")
        xs = held.tile([P, TILES, XW], F32, name="xs")

        vs_pool = held.tile([P, T], F32, name="vs_pool")
        zeros = work.tile([P, P], F32, name="zeros")
        nc.vector.memset(zeros[:], 0.0)
        nc.vector.memset(pos_pool[: P - 1, :], 0.0)
        nc.gpsimd.memset(ks_pool[:].bitcast(I32), 0)
        nc.gpsimd.affine_select(
            out=ident[:], in_=zeros[:], compare_op=ALU.not_equal, fill=1.0, base=0, pattern=[[-1, P]], channel_multiplier=1
        )
        kw_pool = shared.tile([P, T], I32, name="kw_pool", offset=AT_KEYS)
        qw = work.tile([P, B, NQ], I32, name="qw", align_bytes=64)
        qs = work.tile([P, B * NQ], U8, name="qs", align_bytes=64)
        rows = work.tile([P, 2, P], F32, name="rows")
        v_raw = [work.tile([P, T // 2], F32, name="v_raw0"), shared.tile([P, T // 2], F32, name="v_raw1", offset=AT_P)]
        nc.gpsimd.memset(qs[:].bitcast(I32), 0)
        nc.scalar.copy(rows[: P - TILES], zeros[: P - TILES, :].unsqueeze(1).to_broadcast([P - TILES, 2, P]))
        nc.gpsimd.memset(vs_pool[: P - 1, :], 0.0)

        nc.sync.dma_start(offsets[:], offs)
        nc.sync.dma_start(pos_pool[P - 1 :, :], pos[P - 1 :, :])
        nc.sync.dma_start(vs_pool[P - 1 :, :], vs[P - 1 :, :])
        for r in range(4):
            nc.sync.dma_start(ks_pool[r:P:32, :].bitcast(I32), k_scales[0, r:16:4, :].bitcast(I32))
        nc.sync.dma_start(kw_pool[:], k_words[0].rearrange("p t r -> p (t r)").bitcast(I32))
        nc.sync.dma_start(rows[P - TILES :, 0, :], qpos.rearrange("b (h p) o -> (b h) (p o)", p=P))
        nc.sync.dma_start(qw[:], q_words.rearrange("b o p q r -> p (b o) (q r)").bitcast(I32))
        for r in range(4):
            nc.sync.dma_start(
                qs[r:P:32, :].bitcast(I32).rearrange("f (b q) -> f b q", b=B),
                q_scales[:, 0, r:16:4, :].rearrange("b f q -> f b q").bitcast(I32),
            )
        nc.sync.dma_start(v_raw[0][:], vT[:, : T // 2])
        nc.sync.dma_start(rows[P - TILES :, 1, :], sink.rearrange("b (h p) o -> (b h) (p o)", p=P))
        nc.sync.dma_start(v_raw[1][:], vT[:, T // 2 :])

        lists = [offsets[:, b * N // 16 : (b + 1) * N // 16] for b in range(B)]

        pg = [work.tile([P, N], F32, name=f"pg{b}") for b in range(B)]
        upright = [banks.tile([P, CHUNKS, P], F32, name=f"upright{b}", offset=BANK * (2 + b)) for b in range(B)]
        nc.vector.tensor_copy(pg[0][:], pos_pool[:].indirect(lists[0]))
        nc.scalar.activation(pg[1][:], pos_pool[:].indirect(lists[1]), ACT.Copy)
        for b in range(B):
            for c in range(CHUNKS):
                nc.tensor.transpose(upright[b][:, c, :], pg[b][:, c * P : (c + 1) * P], ident[:])

        ks = work.tile([P, B * N], U8, name="ks", align_bytes=64)
        kw = [work.tile([P, N], U32, name=f"kw{b}", align_bytes=64) for b in range(B)]
        nc.vector.tensor_copy(ks[:], ks_pool[:].indirect(offsets[:]))
        for half in range(2):
            nc.vector.tensor_copy(
                kw[0][:, half * HALF : (half + 1) * HALF],
                kw_pool[:].bitcast(U32).indirect(offsets[:, half * HALF // 16 : (half + 1) * HALF // 16]),
            )
        nc.vector.tensor_copy(kw[1][:], kw_pool[:].bitcast(U32).indirect(lists[1]))

        v_pool = shared.tile([P, T], BF16, name="v_pool", offset=AT_KEYS + 4 * KB)
        nc.gpsimd.tensor_copy(v_pool[:, : T // 2], v_raw[0][:])
        nc.gpsimd.tensor_copy(v_pool[:, T // 2 : 3 * T // 4], v_raw[1][:, : T // 4])

        columns = [work.tile([P, CHUNKS], F32, name=f"columns{b}") for b in range(B)]
        place_rows = [work.tile([P, N], F32, name="place_rows0"), shared.tile([P, N], F32, name="place_rows1", offset=AT_PLACES)]
        scale_cols = [work.tile([P, PLACES], F32, name=f"scale_cols{b}") for b in range(B)]

        def spread(b):
            place_spread = banks.tile([P, N], F32, name=f"place_spread{b}", offset=BANK * (4 + b))
            for c in range(CHUNKS):
                nc.tensor.transpose(place_spread[:, c * P : (c + 1) * P], columns[b][:, c : c + 1].to_broadcast([P, P]), ident[:])
            nc.scalar.copy(place_rows[b][:].rearrange("q (t c) -> q t c", t=PLACES), place_spread[:].rearrange("q (c t) -> q t c", t=PLACES))

        def half_scales(b, half, into):
            at = b * N + half * N // 2
            nc.scalar.activation(into, vs_pool[:].indirect(offsets[:, at // 16 : (at + N // 2) // 16]), ACT.Copy)

        def second_scales(half, sg):
            half_scales(1, half, sg[:])
            nc.sync.dma_start(scale_cols[1][half * P // 2 : (half + 1) * P // 2, :], sg[P - 1 :, :])

        sg0 = work.tile([P, N], F32, name="sg0")
        for b in range(B):
            nc.scalar.activation(columns[b][:], upright[b][:, :, P - 1], ACT.Copy, bias=MARGIN, scale=-BIG)
            half_scales(0, b, sg0[:, b * N // 2 : (b + 1) * N // 2])
        nc.sync.dma_start(scale_cols[0][:], sg0[P - 1 :, :])
        spread(0)
        second_scales(0, work.tile([P, N // 2], F32, name="sg1_first"))
        turned_places = banks.tile([P, P], F32, name="turned_places", offset=BANK * 6)
        nc.tensor.transpose(turned_places[:], rows[:, 0, :], ident[:])
        qpos_cols = turned_places[:, P - TILES :]

        step = shared.tile([P, 16], F32, name="step", offset=AT_SG1 - 32)
        limit = work.tile([P, TILES], F32, name="limit")
        nc.scalar.activation(step[:, :TILES], qpos_cols, ACT.Abs, scale=BIG * HALF_STEP)
        for j in range(TILES):
            nc.scalar.activation(limit[:, j : j + 1], qpos_cols[:, j : j + 1], ACT.Identity, scale=BIG, bias=step[:, j : j + 1])

        scores = [banks.tile([P, N], F32, name=f"scores{j}", offset=BANK * j) for j in range(QT)]

        def score(j, first, count):
            b, h = divmod(j, QT)
            nc.tensor.matmul_mx(
                out=scores[j][:, first : first + count],
                lhsT=qw[:, b, h * P : (h + 1) * P].bitcast(FP8X4),
                lhsT_scale=qs[:, j * P : (j + 1) * P],
                rhs=kw[b][:, first : first + count].bitcast(FP8X4),
                rhs_scale=ks[:, b * N + first : b * N + first + count],
                start=True,
                stop=True,
            )

        for half in range(2):
            for j in range(QT):
                score(j, half * HALF, HALF)
        second_scales(1, shared.tile([P, N // 2], F32, name="sg1_second", offset=AT_SG1))
        spread(1)
        turned_sinks = banks.tile([P, 2 * N], F32, name="turned_sinks", offset=BANK * 2)
        nc.tensor.transpose(turned_sinks[:, :P], rows[:, 1, :], ident[:])
        nc.scalar.copy(xs[:, :, N], turned_sinks[:, P - TILES : P])
        nc.scalar.copy(v_pool[:, 3 * T // 4 :], v_raw[1][:, T // 4 :])
        for j in range(QT, TILES):
            scores.append(banks.tile([P, N], F32, name=f"scores{j}", offset=BANK * j))
            score(j, 0, N)

        minus_m = held.tile([P, TILES], F32, name="minus_m")
        total = held.tile([P, TILES], F32, name="total")
        inv = held.tile([P, TILES], F32, name="inv")
        for b in range(B):
            for j in range(QT * b, QT * (b + 1)):
                nc.vector.scalar_tensor_tensor(
                    xs[:, j, :N].rearrange("q (t c) -> q t c", t=PLACES),
                    place_rows[b][:].rearrange("q (t c) -> q t c", t=PLACES),
                    limit[:, j : j + 1],
                    scores[j][:].rearrange("q (c t) -> q t c", t=PLACES),
                    ALU.add,
                    ALU.min,
                )
            for j in range(QT * b, QT * (b + 1)):
                nc.vector.tensor_reduce(minus_m[:, j : j + 1], xs[:, j, : N + 1], AXIS.X, ALU.max, negate=True)

        vg = [work.tile([P, N], BF16, name=f"vg{b}") for b in range(B)]

        def half_values(b, half):
            at = b * N + half * HALF
            nc.scalar.activation(
                vg[b][:, half * HALF : (half + 1) * HALF], v_pool[:].indirect(offsets[:, at // 16 : (at + HALF) // 16]), ACT.Copy
            )

        def turn_values(b):
            turned = banks.tile([P, 2, P], F32, name=f"v_turned{b}", offset=BANK * b)
            words = vg[b][:].bitcast(F32)
            for u in range(2):
                nc.tensor.transpose(turned[:, u, :], words[:, u:WORDS:2], ident[:])
            return turned

        half_values(0, 0)
        v_turned = []

        w_woven = [work.tile([P, N], BF16, name=f"w_woven{j}", align_bytes=64) for j in range(TILES)]
        wq = [work.tile([P, P], U32, name=f"wq{j}", align_bytes=64) for j in range(TILES)]
        wsc = [work.tile([P, P], U8, name=f"wsc{j}", align_bytes=64) for j in range(TILES)]
        for j in range(TILES):
            b, h = divmod(j, QT)
            if j == QT:
                half_values(0, 1)
                v_turned.append(turn_values(0))
                half_values(1, 0)
            p = shared.tile([P, N + 8], F32, name=f"p{j}", offset=AT_P + j * P_BYTES)
            nc.scalar.activation(p[:, : N + 1], xs[:, j, : N + 1], ACT.Exp, bias=minus_m[:, j : j + 1], accum_out=total[:, j : j + 1])
            p_turned = banks.tile([P, PLACES, P], F32, name=f"p_turned{j}", offset=BANK * (4 + j))
            for t in range(PLACES):
                nc.tensor.transpose(p_turned[:, t, :], p[:, t * P : (t + 1) * P], ident[:])
            nc.vector.tensor_tensor(
                w_woven[j][:].rearrange("p (q t) -> p q t", t=PLACES),
                p_turned[:].rearrange("p t q -> p q t"),
                scale_cols[b][:].unsqueeze(1).to_broadcast([P, P, PLACES]),
                ALU.mult,
            )
            if j == QT - 1:
                for i in range(QT):
                    quantise(nc, w_woven[i][:], wq[i][:], wsc[i][:])

        half_values(1, 1)
        v_turned.append(turn_values(1))
        v_woven = work.tile([P, B * WORDS], F32, name="v_woven", align_bytes=64)
        for b in range(B):
            nc.scalar.copy(
                v_woven[:, b * WORDS : (b + 1) * WORDS].rearrange("p (c u) -> p c u", u=2), v_turned[b][:].rearrange("p u c -> p c u")
            )
        vq = work.tile([P, B * DV], U32, name="vq", align_bytes=64)
        vsc = work.tile([P, B * DV], U8, name="vsc", align_bytes=64)
        quantise(nc, v_woven[:, :WORDS].bitcast(BF16), vq[:, :DV], vsc[:, :DV])
        quantise(nc, w_woven[2][:], wq[2][:], wsc[2][:])
        nc.vector.reciprocal(inv[:], total[:])
        quantise(nc, w_woven[3][:], wq[3][:], wsc[3][:])
        quantise(nc, v_woven[:, WORDS:].bitcast(BF16), vq[:, DV:], vsc[:, DV:])

        for j in range(TILES):
            b, h = divmod(j, QT)
            y = banks.tile([P, DV], F32, name=f"y{j}", offset=BANK * (4 + (j + QT) % TILES))
            nc.tensor.matmul_mx(
                out=y[:],
                lhsT=wq[j][:].bitcast(FP8X4),
                lhsT_scale=wsc[j][:],
                rhs=vq[:, b * DV : (b + 1) * DV].bitcast(FP8X4),
                rhs_scale=vsc[:, b * DV : (b + 1) * DV],
                start=True,
                stop=True,
            )
            res = work.tile([P, DV], F32, name=f"res{j}")
            if j == TILES - 1:
                nc.vector.tensor_scalar(res[:], y[:], inv[:, j : j + 1], None, ALU.mult)
            else:
                nc.scalar.activation(res[:], y[:], ACT.Copy, scale=inv[:, j : j + 1])
            nc.sync.dma_start(out[b, h * P : (h + 1) * P, :], res[:])
